import numpy as np
import ml_dtypes


def mxq(x, axis, fmt="e4m3"):
    dtype, down = {"e4m3": (ml_dtypes.float8_e4m3fn, 7), "e5m2": (ml_dtypes.float8_e5m2, 14)}[fmt]
    v = np.moveaxis(np.asarray(x, np.float32).astype(ml_dtypes.bfloat16).astype(np.float64), axis, -1)
    blocks = v.reshape(v.shape[:-1] + (-1, 32))
    amax = np.abs(blocks).max(-1, keepdims=True)
    byte = np.maximum(np.where(amax > 0, np.frexp(amax)[1] - 1 + 127, 0) - down, 1)
    scale = np.exp2(byte - 127.0)
    codes = (blocks / scale).astype(np.float32).astype(dtype).astype(np.float64)
    return np.moveaxis((codes * scale).reshape(v.shape), -1, axis)


WIDE = False


def mx_kscale(k):
    if not WIDE:
        return np.ones(k)
    levels = np.array([24, -24, 12, -12, 0])
    if k % 512:
        return np.exp2(np.random.permutation(np.resize(levels, k // 32))).repeat(32)
    a = np.empty((k // 512, 16))
    for p in range(k // 512):
        a[p, :8] = np.random.permutation(np.resize(levels, 8))
        for g in range(8):
            far = levels[np.abs(levels - a[p, g]) >= 10]
            a[p, g + 8] = far[np.random.randint(len(far))]
    return np.exp2(a.ravel()).repeat(32)


def f64(x):
    return np.asarray(x).astype(np.float64)


def striped(idx):
    return np.tile(idx.reshape(-1, 16).T, (8, 1)).astype(np.uint16)


def unstriped(offs):
    return offs[:16].T.reshape(-1).astype(np.int64)


E2M1 = np.array([0.0, 0.5, 1.0, 1.5, 2.0, 3.0, 4.0, 6.0, -0.0, -0.5, -1.0, -1.5, -2.0, -3.0, -4.0, -6.0])


def pack_weight(w, fmt):
    k, n = w.shape
    w = f64(np.asarray(w, np.float32).astype(ml_dtypes.bfloat16)).reshape(k // 32, 32, n)
    amax = np.abs(w).max(1)
    if fmt == "e4m3":
        byte = np.frexp(amax)[1] - 1 + 127 - 7
    else:
        mant, ex = np.frexp(amax / 6.0)
        byte = np.where(mant > 0.5, ex, ex - 1) + 127
    byte = np.clip(np.where(amax > 0, byte, 1), 1, 254)
    scaled = (w * np.exp2(127.0 - byte)[:, None, :]).reshape(k, n).astype(np.float32)
    by_word = np.ascontiguousarray(scaled.reshape(k // 512, 128, 4, n).transpose(0, 1, 3, 2))
    if fmt == "e4m3":
        words = by_word.astype(ml_dtypes.float8_e4m3fn).view(np.uint8)
    else:
        c = by_word.astype(ml_dtypes.float4_e2m1fn).view(np.uint8) & 0xF
        words = (c[..., 0::2] | (c[..., 1::2] << 4)).reshape(k // 512, 128, 2 * n)
    return np.ascontiguousarray(words), np.ascontiguousarray(byte.astype(np.uint8).reshape(k // 512, 16, n))


def unpack_weight(words, scales, fmt):
    g, _, n = scales.shape
    words = np.ascontiguousarray(words).reshape(g, 128, n, -1)
    if fmt == "e4m3":
        vals = words.view(ml_dtypes.float8_e4m3fn).astype(np.float64)
    else:
        nib = np.empty((g, 128, n, 4), np.uint8)
        nib[..., 0::2] = words & 0xF
        nib[..., 1::2] = words >> 4
        vals = E2M1[nib]
    vals = vals * np.repeat(np.exp2(scales.astype(np.float64) - 127.0), 8, axis=1)[..., None]
    return vals.transpose(0, 1, 3, 2).reshape(g * 512, n)


def pack_table4(v):
    words, scales = pack_weight(v, "e2m1")
    g, t = words.shape[0] // 2, v.shape[1]
    return np.ascontiguousarray(words.reshape(g, 2, 128, t, 2).transpose(0, 2, 3, 1, 4).reshape(g, 128, t, 4)), scales


def unpack_table4(words, scales):
    g, _, t, _ = words.shape
    return unpack_weight(words.reshape(g, 128, t, 2, 2).transpose(0, 3, 1, 2, 4).reshape(2 * g, 128, 2 * t), scales, "e2m1")


K, R, N, T, J = 1024, 1024, 512, 2048, 1024


def setup_inputs():
    n = np.random.standard_normal
    s = mx_kscale(K)[:, None]
    u = mx_kscale(R)[:, None]
    wd = n((R, N)) / np.sqrt(R) / u
    p_tab = pack_table4(n((K, T)) * s)
    p_wu = pack_weight(n((K, R)) / np.sqrt(K) / s, "e4m3")
    p_wd8 = pack_weight(wd[:512], "e4m3")
    p_wd4 = pack_weight(wd[512:], "e2m1")
    return {
        "tab_words": p_tab[0],
        "tab_scales": p_tab[1],
        "wu_words": p_wu[0],
        "wu_scales": p_wu[1],
        "sm": (np.random.uniform(0.5, 2.0, R) * u[:, 0]).astype(np.float32),
        "wd8_words": p_wd8[0],
        "wd8_scales": p_wd8[1],
        "wd4_words": p_wd4[0],
        "wd4_scales": p_wd4[1],
        "rT": (n((N, T))).astype(np.float32),
        "b": (0.3 * n(N)).astype(np.float32),
        "wgo": np.tile(np.random.uniform(0.5, 2.0, J), (128, 1)).astype(np.float32),
        "offs": striped(np.random.permutation(T)[:J]),
    }


def reference(tab_words, tab_scales, wu_words, wu_scales, sm, wd8_words, wd8_scales, wd4_words, wd4_scales, rT, b, wgo, offs):
    idx = unstriped(offs)
    tab_ = unpack_table4(tab_words, tab_scales)[:, idx]
    wu_ = unpack_weight(wu_words, wu_scales, "e4m3")
    a = wu_.T @ tab_
    h = f64(sm)[:, None] * (np.maximum(a, 0.0)) ** 2
    h_ = mxq(h, 0, "e4m3")
    wd8_ = unpack_weight(wd8_words, wd8_scales, "e4m3")
    wd4_ = unpack_weight(wd4_words, wd4_scales, "e2m1")
    y = wd8_.T @ h_[:512] + wd4_.T @ h_[512:]
    out = np.zeros((N, T))
    out[:, idx] = f64(wgo)[0] * (y + f64(rT)[:, idx] + f64(b)[:, None])
    return out

@@ -1,0 +1,258 @@
+from contextlib import ExitStack
+
+import concourse.mybir as mybir
+
+K, R, N, T, J = 1024, 1024, 512, 2048, 1024
+FLOPS = 2 * K * R * J + 2 * R * N * J
+
+F32 = mybir.dt.float32
+BF16 = mybir.dt.bfloat16
+I32 = mybir.dt.int32
+U32 = mybir.dt.uint32
+U16 = mybir.dt.uint16
+U8 = mybir.dt.uint8
+FP8X4 = mybir.dt.float8_e4m3fn_x4
+FP4X4 = mybir.dt.float4_e2m1fn_x4
+ALU = mybir.AluOpType
+ACT = mybir.ActivationFunctionType
+
+P = 128
+PACK = 4
+PASS = P * PACK
+CH = 512
+NCH = J // CH
+NT = N // P
+RB = R // PASS
+SHIFT = 4
+MOVED = 112
+EARLY_BYTES = 2 * PASS * 4 + T * 4
+LATE_BYTES = (NT - 1) * T * 4 + N * 4 + N * 2 + N * 2 + J * 4 + 64
+
+
+def tile_list_modp_relu2_mix_resb_kernel(
+    tc, tab_words, tab_scales, wu_words, wu_scales, sm, wd8_words, wd8_scales,
+    wd4_words, wd4_scales, rT, b, wgo, offs, out,
+):
+    nc = tc.nc
+    with ExitStack() as ctx:
+        keep = ctx.enter_context(tc.tile_pool(name="keep", bufs=1))
+        ring = ctx.enter_context(tc.tile_pool(name="ring", bufs=2))
+        late = ctx.enter_context(tc.tile_pool(name="late", bufs=1))
+        mid = ctx.enter_context(tc.tile_pool(name="mid", bufs=1))
+        early = ctx.enter_context(tc.tile_pool(name="early", bufs=1))
+        psum = ctx.enter_context(tc.psum_pool(name="psum", bufs=4))
+
+        offsets = keep.tile([P, J // 16], U16, name="offsets")
+        nc.sync.dma_start(offsets[:], offs)
+
+        def chunk_offsets(c):
+            return offsets[:, c * (CH // 16) : (c + 1) * (CH // 16)]
+
+        sm_sb = keep.tile([P, RB, PACK], F32, name="sm_sb")
+        nc.sync.dma_start(sm_sb[:], sm.rearrange("(b p i) -> p b i", b=RB, i=PACK))
+        tab_sc_wide = early.tile([P, EARLY_BYTES // 4], I32, name="tab_sc", align_bytes=64, offset=0)
+        tab_sc = tab_sc_wide[:, 0 : T // 4]
+        wu_sc = mid.tile([P, 2, R // 4], I32, name="wu_sc", align_bytes=64, offset=0)
+        nc.gpsimd.memset(tab_sc, 0)
+        nc.vector.memset(wu_sc[:], 0)
+        got_sc1 = keep.tile([P, J // 4], I32, name="got_sc1", align_bytes=64)
+        half = keep.tile([P, RB * PACK], F32, name="half")
+        nc.gpsimd.memset(half[:], 0.5)
+        nc.gpsimd.memset(got_sc1[:], 0)
+
+        for q in range(4):
+            nc.sync.dma_start(tab_sc[32 * q : 32 * q + 8, :], tab_scales.bitcast(I32)[:, 4 * q : 4 * q + 4, :])
+        tab_w = keep.tile([P, T], I32, name="tab_w", tag="big_a", align_bytes=64)
+        nc.sync.dma_start(tab_w[:], tab_words[0].rearrange("p t f -> p (t f)").bitcast(I32))
+        wu_view = wu_words.rearrange("a p r i -> p a (r i)").bitcast(I32)
+        wu_raw0 = keep.tile([P, 2, PASS], I32, name="wu_raw0", align_bytes=64)
+        nc.sync.dma_start(wu_raw0[:], wu_view[:, :, 0:PASS])
+        wu_sc_view = wu_scales.bitcast(I32).rearrange("a q r -> q a r")
+        for q in range(4):
+            nc.sync.dma_start(wu_sc[32 * q : 32 * q + 4, :, :], wu_sc_view[4 * q : 4 * q + 4, :, :])
+
+        sm_flat = sm_sb[:].rearrange("p b i -> p (b i)")
+        sign_bf = keep.tile([P, RB * PACK], BF16, name="sign_bf")
+        mag = keep.tile([P, RB * PACK], F32, name="mag")[:]
+        root = keep.tile([P, RB * PACK], F32, name="root")
+        nc.scalar.activation(mag, sm_flat, ACT.Abs)
+        nc.scalar.activation(sign_bf[:], sm_flat, ACT.Sign)
+        nc.gpsimd.tensor_tensor(root[:], mag, half[:], ALU.pow)
+
+        got_sc = keep.tile([P, J], U8, name="got_sc", align_bytes=64)
+        nc.vector.tensor_copy(got_sc[:], tab_sc.bitcast(U8).indirect(offsets[:]))
+        nc.sync.dma_start(got_sc1[0:MOVED, :], got_sc[:].bitcast(I32)[SHIFT : SHIFT + MOVED, :])
+        tab_planes = (got_sc[:], got_sc1[:].bitcast(U8))
+
+        wu_raw1 = early.tile([P, 2, PASS], I32, name="wu_raw1", align_bytes=64, offset=0)
+        nc.sync.dma_start(wu_raw1[:], wu_view[:, :, PASS : 2 * PASS])
+        wu_raw = (wu_raw0[:], wu_raw1[:])
+
+        wu_planes = []
+        parted = []
+        wu_p = []
+
+        def gather_words(c):
+            if c == 0:
+                wide = late.tile([P, LATE_BYTES // 4], U32, name="got_first", align_bytes=64, offset=0)
+                got = wide[:, 0:CH]
+            else:
+                got = mid.tile([P, CH], U32, name="got_second", align_bytes=64, offset=CH)[:]
+            nc.vector.tensor_copy(got, tab_w[:].bitcast(U32).indirect(chunk_offsets(c)))
+            return got
+
+        def part_words(got, c):
+            pt = keep.tile([P, 2, CH], U16, name=f"parted{c}", align_bytes=64)
+            nc.vector.tensor_copy(pt[:], got.bitcast(U16).rearrange("p (j d) -> p d j", d=2))
+            parted.append(pt)
+
+        def permute_wu(rb):
+            w = keep.tile([P, 2, PASS], I32, name=f"wu_p{rb}", align_bytes=64)
+            nc.vector.tensor_copy(
+                w[:].rearrange("p a (i m) -> p a m i", i=PACK),
+                wu_raw[rb].rearrange("p a (m i) -> p a m i", i=PACK),
+            )
+            wu_p.append(w)
+
+        def permute_wu_scales(rb):
+            s = keep.tile([P, 2, PASS], U8, name=f"wup_sc{rb}", align_bytes=64)
+            raw = wu_sc[:].rearrange("p a r -> p (a r)").bitcast(U8).rearrange("p (a b m i) -> p b a m i", a=2, b=RB, i=PACK)
+            nc.vector.tensor_copy(s[:].rearrange("p a (i m) -> p a m i", i=PACK), raw[:, rb])
+            wu_planes.append(s)
+
+        got0 = gather_words(0)
+        permute_wu(0)
+        part_words(got0, 0)
+        permute_wu_scales(0)
+
+        r_sb = [early.tile([P, T], F32, name="r_sb0", align_bytes=64, offset=2 * PASS * 4)]
+        for t in range(1, NT):
+            r_sb.append(late.tile([P, T], F32, name=f"r_sb{t}", align_bytes=64, offset=(t - 1) * T * 4))
+        at = (NT - 1) * T * 4
+        wd8_w = late.tile([P, N], I32, name="wd8_w", align_bytes=64, offset=at)
+        wd4_w = late.tile([P, N // 2], I32, name="wd4_w", align_bytes=64, offset=at + N * 4)
+        wd_sc = late.tile([P, 2, N // 4], I32, name="wd_sc", align_bytes=64, offset=at + N * 6)
+        wgo_sb = late.tile([P, J], F32, name="wgo_sb", align_bytes=64, offset=at + N * 8)
+        b_sb = late.tile([P, NT], F32, name="b_sb", align_bytes=64, offset=at + N * 8 + J * 4)
+        nc.gpsimd.memset(wd_sc[:], 0)
+        for t in range(2):
+            nc.sync.dma_start(r_sb[t][:], rT[t * P : (t + 1) * P, :])
+        nc.sync.dma_start(wd8_w[:], wd8_words[0].rearrange("p n i -> p (n i)").bitcast(I32))
+        nc.sync.dma_start(wd4_w[:], wd4_words[0].bitcast(I32))
+        for rb, sc in enumerate((wd8_scales, wd4_scales)):
+            for q in range(4):
+                nc.sync.dma_start(wd_sc[32 * q : 32 * q + 4, rb, :], sc[0].bitcast(I32)[4 * q : 4 * q + 4, :])
+        nc.sync.dma_start(r_sb[2][:], rT[2 * P : 3 * P, :])
+        with nc.allow_non_contiguous_dma(reason="one bias value to a partition"):
+            nc.sync.dma_start(b_sb[:], b.rearrange("(t p) -> p t", p=P))
+        nc.sync.dma_start(wgo_sb[:], wgo)
+        nc.sync.dma_start(r_sb[3][:], rT[3 * P : 4 * P, :])
+
+        permute_wu_scales(1)
+        permute_wu(1)
+        got1 = gather_words(1)
+        part_words(got1, 1)
+
+        windows = []
+        for t in range(NT):
+            if t < 2:
+                w = keep.tile([P, T], F32, name=f"window{t}", align_bytes=64)
+                nc.vector.memset(w[:], 0.0)
+            else:
+                if t == 2:
+                    w = keep.tile([P, T], F32, name="window2", tag="big_a", align_bytes=64)
+                else:
+                    w = mid.tile([P, T], F32, name="window3", align_bytes=64, offset=CH)
+                nc.gpsimd.memset(w[:], 0.0)
+            windows.append(w)
+
+        h_codes, h_scales = {}, {}
+
+        def hidden(c, rb):
+            u = ring.tile([P, PACK, CH], F32, name="u")
+            for i in range(PACK):
+                acc = psum.tile([P, CH], F32, name="acc_a")
+                for a in range(2):
+                    nc.tensor.matmul_mx(
+                        out=acc[:],
+                        lhsT=wu_p[rb][:, a, i * P : (i + 1) * P].bitcast(FP8X4),
+                        lhsT_scale=wu_planes[rb][:, a, i * P : (i + 1) * P],
+                        rhs=parted[c][:, a, :].bitcast(FP4X4),
+                        rhs_scale=tab_planes[a][:, c * CH : (c + 1) * CH],
+                        start=(a == 0),
+                        stop=(a == 1),
+                    )
+                col = rb * PACK + i
+                nc.scalar.activation(u[:, i, :], acc[:], ACT.Relu, scale=root[:, col : col + 1])
+            hb = ring.tile([P, CH * PACK], BF16, name="hb", align_bytes=64)
+            nc.scalar.activation(
+                hb[:].rearrange("p (g k i) -> p g i k", k=4, i=PACK),
+                u[:].rearrange("p i (g k) -> p g i k", k=4),
+                ACT.Square,
+            )
+            hs = ring.tile([P, CH * PACK], BF16, name="hs", tag="hs", align_bytes=64)
+            nc.vector.tensor_tensor(
+                hs[:].rearrange("p (j i) -> p j i", i=PACK),
+                hb[:].rearrange("p (j i) -> p j i", i=PACK),
+                sign_bf[:, rb * PACK : (rb + 1) * PACK].unsqueeze(1).to_broadcast([P, CH, PACK]),
+                ALU.mult,
+            )
+            codes = keep.tile([P, CH], U32, name=f"h_codes{c}{rb}", align_bytes=64)
+            scales = keep.tile([P, CH], U8, name=f"h_scales{c}{rb}", align_bytes=64)
+            nc.vector.quantize_mx(out=codes[:].bitcast(FP8X4), scales=scales[:], in_=hs[:])
+            h_codes[c, rb], h_scales[c, rb] = codes, scales
+
+        for c in range(NCH):
+            for rb in range(RB):
+                hidden(c, rb)
+
+        picked = {}
+        for c in range(NCH):
+            for t in range(NT):
+                g = keep.tile([P, CH], F32, name=f"picked{c}{t}")
+                nc.vector.tensor_copy(g[:], r_sb[t][:].indirect(chunk_offsets(c)))
+                picked[c, t] = g
+
+        wd_sc8 = wd_sc[:].rearrange("p a n -> p (a n)").bitcast(U8)
+
+        def add_up(c, t):
+            acc = psum.tile([P, CH], F32, name="acc_y")
+            nc.tensor.matmul_mx(
+                out=acc[:],
+                lhsT=wd8_w[:, t * P : (t + 1) * P].bitcast(FP8X4),
+                lhsT_scale=wd_sc8[:, t * P : (t + 1) * P],
+                rhs=h_codes[c, 0][:].bitcast(FP8X4),
+                rhs_scale=h_scales[c, 0][:],
+                start=True,
+                stop=False,
+            )
+            nc.tensor.matmul_mx(
+                out=acc[:],
+                lhsT=wd4_w[:, t * P // 2 : (t + 1) * P // 2].bitcast(FP4X4),
+                lhsT_scale=wd_sc8[:, N + t * P : N + (t + 1) * P],
+                rhs=h_codes[c, 1][:].bitcast(FP8X4),
+                rhs_scale=h_scales[c, 1][:],
+                start=False,
+                stop=True,
+            )
+            g = picked[c, t]
+            if c == 0 and t >= 2:
+                picked[c, t] = ring.tile([P, CH], F32, name="summed", tag="hs", align_bytes=64)
+            nc.vector.scalar_tensor_tensor(picked[c, t][:], acc[:], b_sb[:, t : t + 1], g[:], ALU.add, ALU.add)
+
+        def put(c, t):
+            nc.vector.tensor_tensor(
+                windows[t][:].indirect(chunk_offsets(c)),
+                picked[c, t][:],
+                wgo_sb[:, c * CH : (c + 1) * CH],
+                ALU.mult,
+            )
+            if c == NCH - 1:
+                nc.sync.dma_start(out[t * P : (t + 1) * P, :], windows[t][:])
+
+        steps = [(c, t) for c in range(NCH) for t in range(NT)]
+        add_up(*steps[0])
+        for s in range(len(steps)):
+            if s + 1 < len(steps):
+                add_up(*steps[s + 1])
+            put(*steps[s])

@@ -40,6 +40,7 @@ def tile_list_modp_relu2_mix_resb_kernel(
         late = ctx.enter_context(tc.tile_pool(name="late", bufs=1))
         mid = ctx.enter_context(tc.tile_pool(name="mid", bufs=1))
         early = ctx.enter_context(tc.tile_pool(name="early", bufs=1))
+        last = ctx.enter_context(tc.tile_pool(name="last", bufs=1))
         psum = ctx.enter_context(tc.psum_pool(name="psum", bufs=4))
 
         offsets = keep.tile([P, J // 16], U16, name="offsets")
@@ -62,7 +63,7 @@ def tile_list_modp_relu2_mix_resb_kernel(
 
         for q in range(4):
             nc.sync.dma_start(tab_sc[32 * q : 32 * q + 8, :], tab_scales.bitcast(I32)[:, 4 * q : 4 * q + 4, :])
-        tab_w = keep.tile([P, T], I32, name="tab_w", tag="big_a", align_bytes=64)
+        tab_w = keep.tile([P, T], I32, name="tab_w", align_bytes=64)
         nc.sync.dma_start(tab_w[:], tab_words[0].rearrange("p t f -> p (t f)").bitcast(I32))
         wu_view = wu_words.rearrange("a p r i -> p a (r i)").bitcast(I32)
         wu_raw0 = keep.tile([P, 2, PASS], I32, name="wu_raw0", align_bytes=64)
@@ -72,11 +73,16 @@ def tile_list_modp_relu2_mix_resb_kernel(
             nc.sync.dma_start(wu_sc[32 * q : 32 * q + 4, :, :], wu_sc_view[4 * q : 4 * q + 4, :, :])
 
         sm_flat = sm_sb[:].rearrange("p b i -> p (b i)")
-        sign_bf = keep.tile([P, RB * PACK], BF16, name="sign_bf")
+        sign_bf = keep.tile([P, RB, CH * PACK], BF16, name="sign_bf", align_bytes=64)
         mag = keep.tile([P, RB * PACK], F32, name="mag")[:]
         root = keep.tile([P, RB * PACK], F32, name="root")
         nc.scalar.activation(mag, sm_flat, ACT.Abs)
-        nc.scalar.activation(sign_bf[:], sm_flat, ACT.Sign)
+        for rb in range(RB):
+            nc.scalar.activation(
+                sign_bf[:, rb, :].rearrange("p (j i) -> p j i", i=PACK),
+                sm_sb[:, rb, :].unsqueeze(1).to_broadcast([P, CH, PACK]),
+                ACT.Sign,
+            )
         nc.gpsimd.tensor_tensor(root[:], mag, half[:], ALU.pow)
 
         got_sc = keep.tile([P, J], U8, name="got_sc", align_bytes=64)
@@ -116,8 +122,8 @@ def tile_list_modp_relu2_mix_resb_kernel(
 
         def permute_wu_scales(rb):
             s = keep.tile([P, 2, PASS], U8, name=f"wup_sc{rb}", align_bytes=64)
-            raw = wu_sc[:].rearrange("p a r -> p (a r)").bitcast(U8).rearrange("p (a b m i) -> p b a m i", a=2, b=RB, i=PACK)
-            nc.vector.tensor_copy(s[:].rearrange("p a (i m) -> p a m i", i=PACK), raw[:, rb])
+            raw = wu_sc[:].rearrange("p a r -> p (a r)").bitcast(U8).rearrange("p (a b m i) -> p b a i m", a=2, b=RB, i=PACK)
+            nc.vector.tensor_copy(s[:].rearrange("p a (i m) -> p a i m", i=PACK), raw[:, rb])
             wu_planes.append(s)
 
         got0 = gather_words(0)
@@ -154,16 +160,9 @@ def tile_list_modp_relu2_mix_resb_kernel(
         part_words(got1, 1)
 
         windows = []
-        for t in range(NT):
-            if t < 2:
-                w = keep.tile([P, T], F32, name=f"window{t}", align_bytes=64)
-                nc.vector.memset(w[:], 0.0)
-            else:
-                if t == 2:
-                    w = keep.tile([P, T], F32, name="window2", tag="big_a", align_bytes=64)
-                else:
-                    w = mid.tile([P, T], F32, name="window3", align_bytes=64, offset=CH)
-                nc.gpsimd.memset(w[:], 0.0)
+        for t in range(2):
+            w = keep.tile([P, T], F32, name=f"window{t}", align_bytes=64)
+            nc.vector.memset(w[:], 0.0)
             windows.append(w)
 
         h_codes, h_scales = {}, {}
@@ -183,20 +182,28 @@ def tile_list_modp_relu2_mix_resb_kernel(
                         stop=(a == 1),
                     )
                 col = rb * PACK + i
-                nc.scalar.activation(u[:, i, :], acc[:], ACT.Relu, scale=root[:, col : col + 1])
+                if c == 0:
+                    nc.scalar.activation(u[:, i, :], acc[:], ACT.Relu, scale=root[:, col : col + 1])
+                else:
+                    nc.scalar.activation(u[:, i, :], acc[:], ACT.Relu)
             hb = ring.tile([P, CH * PACK], BF16, name="hb", align_bytes=64)
-            nc.scalar.activation(
-                hb[:].rearrange("p (g k i) -> p g i k", k=4, i=PACK),
-                u[:].rearrange("p i (g k) -> p g i k", k=4),
-                ACT.Square,
-            )
             hs = ring.tile([P, CH * PACK], BF16, name="hs", tag="hs", align_bytes=64)
-            nc.vector.tensor_tensor(
-                hs[:].rearrange("p (j i) -> p j i", i=PACK),
-                hb[:].rearrange("p (j i) -> p j i", i=PACK),
-                sign_bf[:, rb * PACK : (rb + 1) * PACK].unsqueeze(1).to_broadcast([P, CH, PACK]),
-                ALU.mult,
-            )
+            if c == 0:
+                nc.scalar.activation(
+                    hb[:].rearrange("p (g k i) -> p g i k", k=4, i=PACK),
+                    u[:].rearrange("p i (g k) -> p g i k", k=4),
+                    ACT.Square,
+                )
+                nc.vector.tensor_tensor(hs[:], hb[:], sign_bf[:, rb, :], ALU.mult)
+            else:
+                sq = ring.tile([P, PACK, CH], F32, name="sq")
+                nc.scalar.activation(sq[:], u[:], ACT.Square)
+                for i in range(PACK):
+                    nc.scalar.activation(hb[:, i * CH : (i + 1) * CH], sq[:, i, :], ACT.Copy, scale=sm_sb[:, rb, i : i + 1])
+                nc.scalar.copy(
+                    hs[:].rearrange("p (g k i) -> p g i k", k=4, i=PACK),
+                    hb[:].rearrange("p (i g k) -> p g i k", k=4, i=PACK),
+                )
             codes = keep.tile([P, CH], U32, name=f"h_codes{c}{rb}", align_bytes=64)
             scales = keep.tile([P, CH], U8, name=f"h_scales{c}{rb}", align_bytes=64)
             nc.vector.quantize_mx(out=codes[:].bitcast(FP8X4), scales=scales[:], in_=hs[:])
@@ -207,11 +214,17 @@ def tile_list_modp_relu2_mix_resb_kernel(
                 hidden(c, rb)
 
         picked = {}
-        for c in range(NCH):
-            for t in range(NT):
-                g = keep.tile([P, CH], F32, name=f"picked{c}{t}")
-                nc.vector.tensor_copy(g[:], r_sb[t][:].indirect(chunk_offsets(c)))
-                picked[c, t] = g
+        first = last.tile([P, 2 * T], F32, name="picked_first", align_bytes=64, offset=0)
+        nc.vector.tensor_copy(first[:, 0:CH], r_sb[0][:].indirect(chunk_offsets(0)))
+        picked[0, 0] = first[:, 0:CH]
+        second = keep.tile([P, CH], F32, name="picked_second")
+        nc.vector.tensor_copy(second[:], r_sb[0][:].indirect(chunk_offsets(1)))
+        picked[1, 0] = second[:]
+        for t in range(1, NT):
+            g = keep.tile([P, J], F32, name=f"picked{t}")
+            nc.vector.tensor_copy(g[:], r_sb[t][:].indirect(offsets[:]))
+            for c in range(NCH):
+                picked[c, t] = g[:, c * CH : (c + 1) * CH]
 
         wd_sc8 = wd_sc[:].rearrange("p a n -> p (a n)").bitcast(U8)
 
@@ -237,13 +250,19 @@ def tile_list_modp_relu2_mix_resb_kernel(
             )
             g = picked[c, t]
             if c == 0 and t >= 2:
-                picked[c, t] = ring.tile([P, CH], F32, name="summed", tag="hs", align_bytes=64)
-            nc.vector.scalar_tensor_tensor(picked[c, t][:], acc[:], b_sb[:, t : t + 1], g[:], ALU.add, ALU.add)
+                picked[c, t] = ring.tile([P, CH], F32, name="summed", tag="hs", align_bytes=64)[:]
+            if (c, t) == (0, 0):
+                picked[c, t] = keep.tile([P, CH], F32, name="summed_first")[:]
+            nc.vector.scalar_tensor_tensor(picked[c, t], acc[:], b_sb[:, t : t + 1], g, ALU.add, ALU.add)
+            if (c, t) == (0, 0):
+                for w in range(2, NT):
+                    windows.append(last.tile([P, T], F32, name=f"window{w}", align_bytes=64, offset=(w - 2) * T * 4))
+                    nc.gpsimd.memset(windows[w][:], 0.0)
 
         def put(c, t):
             nc.vector.tensor_tensor(
                 windows[t][:].indirect(chunk_offsets(c)),
-                picked[c, t][:],
+                picked[c, t],
                 wgo_sb[:, c * CH : (c + 1) * CH],
                 ALU.mult,
             )

@@ -25,6 +25,8 @@ NT = N // P
 RB = R // PASS
 SHIFT = 4
 MOVED = 112
+HS_THIRD_AT = 2 * T * 4
+HS_LAST_AT = HS_THIRD_AT + CH * PACK * 2
 EARLY_BYTES = 2 * PASS * 4 + T * 4
 LATE_BYTES = (NT - 1) * T * 4 + N * 4 + N * 2 + N * 2 + J * 4 + 64
 
@@ -90,6 +92,8 @@ def tile_list_modp_relu2_mix_resb_kernel(
         nc.sync.dma_start(got_sc1[0:MOVED, :], got_sc[:].bitcast(I32)[SHIFT : SHIFT + MOVED, :])
         tab_planes = (got_sc[:], got_sc1[:].bitcast(U8))
 
+        r_sb = [early.tile([P, T], F32, name="r_sb0", align_bytes=64, offset=2 * PASS * 4)]
+        nc.sync.dma_start(r_sb[0][:], rT[0:P, :])
         wu_raw1 = early.tile([P, 2, PASS], I32, name="wu_raw1", align_bytes=64, offset=0)
         nc.sync.dma_start(wu_raw1[:], wu_view[:, :, PASS : 2 * PASS])
         wu_raw = (wu_raw0[:], wu_raw1[:])
@@ -114,16 +118,22 @@ def tile_list_modp_relu2_mix_resb_kernel(
 
         def permute_wu(rb):
             w = keep.tile([P, 2, PASS], I32, name=f"wu_p{rb}", align_bytes=64)
-            nc.vector.tensor_copy(
-                w[:].rearrange("p a (i m) -> p a m i", i=PACK),
-                wu_raw[rb].rearrange("p a (m i) -> p a m i", i=PACK),
-            )
+            if rb == 0:
+                nc.vector.tensor_copy(
+                    w[:].rearrange("p a (i m) -> p a m i", i=PACK),
+                    wu_raw[rb].rearrange("p a (m i) -> p a m i", i=PACK),
+                )
+            else:
+                nc.gpsimd.tensor_copy(
+                    w[:].rearrange("p a (i m) -> p a i m", i=PACK),
+                    wu_raw[rb].rearrange("p a (m i) -> p a i m", i=PACK),
+                )
             wu_p.append(w)
 
         def permute_wu_scales(rb):
             s = keep.tile([P, 2, PASS], U8, name=f"wup_sc{rb}", align_bytes=64)
             raw = wu_sc[:].rearrange("p a r -> p (a r)").bitcast(U8).rearrange("p (a b m i) -> p b a i m", a=2, b=RB, i=PACK)
-            nc.vector.tensor_copy(s[:].rearrange("p a (i m) -> p a i m", i=PACK), raw[:, rb])
+            nc.gpsimd.tensor_copy(s[:].rearrange("p a (i m) -> p a i m", i=PACK), raw[:, rb])
             wu_planes.append(s)
 
         got0 = gather_words(0)
@@ -131,7 +141,6 @@ def tile_list_modp_relu2_mix_resb_kernel(
         part_words(got0, 0)
         permute_wu_scales(0)
 
-        r_sb = [early.tile([P, T], F32, name="r_sb0", align_bytes=64, offset=2 * PASS * 4)]
         for t in range(1, NT):
             r_sb.append(late.tile([P, T], F32, name=f"r_sb{t}", align_bytes=64, offset=(t - 1) * T * 4))
         at = (NT - 1) * T * 4
@@ -140,19 +149,22 @@ def tile_list_modp_relu2_mix_resb_kernel(
         wd_sc = late.tile([P, 2, N // 4], I32, name="wd_sc", align_bytes=64, offset=at + N * 6)
         wgo_sb = late.tile([P, J], F32, name="wgo_sb", align_bytes=64, offset=at + N * 8)
         b_sb = late.tile([P, NT], F32, name="b_sb", align_bytes=64, offset=at + N * 8 + J * 4)
-        nc.gpsimd.memset(wd_sc[:], 0)
-        for t in range(2):
-            nc.sync.dma_start(r_sb[t][:], rT[t * P : (t + 1) * P, :])
-        nc.sync.dma_start(wd8_w[:], wd8_words[0].rearrange("p n i -> p (n i)").bitcast(I32))
-        nc.sync.dma_start(wd4_w[:], wd4_words[0].bitcast(I32))
-        for rb, sc in enumerate((wd8_scales, wd4_scales)):
+        nc.vector.memset(wd_sc[:], 0)
+
+        def load_wd_scales(rb, sc):
             for q in range(4):
                 nc.sync.dma_start(wd_sc[32 * q : 32 * q + 4, rb, :], sc[0].bitcast(I32)[4 * q : 4 * q + 4, :])
+
+        nc.sync.dma_start(r_sb[1][:], rT[P : 2 * P, :])
+        load_wd_scales(0, wd8_scales)
         nc.sync.dma_start(r_sb[2][:], rT[2 * P : 3 * P, :])
+        nc.sync.dma_start(wd8_w[:], wd8_words[0].rearrange("p n i -> p (n i)").bitcast(I32))
+        nc.sync.dma_start(wd4_w[:], wd4_words[0].bitcast(I32))
+        nc.sync.dma_start(r_sb[3][:], rT[3 * P : 4 * P, :])
+        load_wd_scales(1, wd4_scales)
+        nc.sync.dma_start(wgo_sb[:], wgo)
         with nc.allow_non_contiguous_dma(reason="one bias value to a partition"):
             nc.sync.dma_start(b_sb[:], b.rearrange("(t p) -> p t", p=P))
-        nc.sync.dma_start(wgo_sb[:], wgo)
-        nc.sync.dma_start(r_sb[3][:], rT[3 * P : 4 * P, :])
 
         permute_wu_scales(1)
         permute_wu(1)
@@ -166,6 +178,8 @@ def tile_list_modp_relu2_mix_resb_kernel(
             windows.append(w)
 
         h_codes, h_scales = {}, {}
+
+        squared = {}
 
         def hidden(c, rb):
             u = ring.tile([P, PACK, CH], F32, name="u")
@@ -182,20 +196,21 @@ def tile_list_modp_relu2_mix_resb_kernel(
                         stop=(a == 1),
                     )
                 col = rb * PACK + i
-                if c == 0:
+                if (c, rb) != (1, 1):
                     nc.scalar.activation(u[:, i, :], acc[:], ACT.Relu, scale=root[:, col : col + 1])
                 else:
                     nc.scalar.activation(u[:, i, :], acc[:], ACT.Relu)
             hb = ring.tile([P, CH * PACK], BF16, name="hb", align_bytes=64)
-            hs = ring.tile([P, CH * PACK], BF16, name="hs", tag="hs", align_bytes=64)
-            if c == 0:
+            if (c, rb) != (1, 1):
                 nc.scalar.activation(
                     hb[:].rearrange("p (g k i) -> p g i k", k=4, i=PACK),
                     u[:].rearrange("p i (g k) -> p g i k", k=4),
                     ACT.Square,
                 )
-                nc.vector.tensor_tensor(hs[:], hb[:], sign_bf[:, rb, :], ALU.mult)
+                squared[c, rb] = hb
             else:
+                hs = last.tile([P, CH * PACK], BF16, name="hs_last", align_bytes=64, offset=HS_LAST_AT)
+                squared[c, rb] = hs
                 sq = ring.tile([P, PACK, CH], F32, name="sq")
                 nc.scalar.activation(sq[:], u[:], ACT.Square)
                 for i in range(PACK):
@@ -204,27 +219,41 @@ def tile_list_modp_relu2_mix_resb_kernel(
                     hs[:].rearrange("p (g k i) -> p g i k", k=4, i=PACK),
                     hb[:].rearrange("p (i g k) -> p g i k", k=4, i=PACK),
                 )
+
+        def quantise(c, rb):
+            hs = squared[c, rb]
+            if (c, rb) != (1, 1):
+                if c == 0:
+                    hs = late.tile([P, CH * PACK], BF16, name=f"hs{rb}", align_bytes=64, offset=rb * T * 4)
+                else:
+                    hs = last.tile([P, CH * PACK], BF16, name="hs_third", align_bytes=64, offset=HS_THIRD_AT)
+                nc.vector.tensor_tensor(hs[:], squared[c, rb][:], sign_bf[:, rb, :], ALU.mult)
             codes = keep.tile([P, CH], U32, name=f"h_codes{c}{rb}", align_bytes=64)
             scales = keep.tile([P, CH], U8, name=f"h_scales{c}{rb}", align_bytes=64)
             nc.vector.quantize_mx(out=codes[:].bitcast(FP8X4), scales=scales[:], in_=hs[:])
             h_codes[c, rb], h_scales[c, rb] = codes, scales
 
-        for c in range(NCH):
-            for rb in range(RB):
-                hidden(c, rb)
-
         picked = {}
+
+        def gather_residual(t):
+            g = keep.tile([P, J], F32, name=f"picked{t}")
+            nc.vector.tensor_copy(g[:], r_sb[t][:].indirect(offsets[:]))
+            for c in range(NCH):
+                picked[c, t] = g[:, c * CH : (c + 1) * CH]
+
         first = last.tile([P, 2 * T], F32, name="picked_first", align_bytes=64, offset=0)
         nc.vector.tensor_copy(first[:, 0:CH], r_sb[0][:].indirect(chunk_offsets(0)))
         picked[0, 0] = first[:, 0:CH]
         second = keep.tile([P, CH], F32, name="picked_second")
         nc.vector.tensor_copy(second[:], r_sb[0][:].indirect(chunk_offsets(1)))
         picked[1, 0] = second[:]
-        for t in range(1, NT):
-            g = keep.tile([P, J], F32, name=f"picked{t}")
-            nc.vector.tensor_copy(g[:], r_sb[t][:].indirect(offsets[:]))
-            for c in range(NCH):
-                picked[c, t] = g[:, c * CH : (c + 1) * CH]
+        for rb in range(RB):
+            hidden(0, rb)
+            gather_residual(rb + 1)
+            quantise(0, rb)
+        gather_residual(3)
+        for rb in range(RB):
+            hidden(1, rb)
 
         wd_sc8 = wd_sc[:].rearrange("p a n -> p (a n)").bitcast(U8)
 
@@ -249,29 +278,39 @@ def tile_list_modp_relu2_mix_resb_kernel(
                 stop=True,
             )
             g = picked[c, t]
-            if c == 0 and t >= 2:
-                picked[c, t] = ring.tile([P, CH], F32, name="summed", tag="hs", align_bytes=64)[:]
+            if (c, t) == (0, 3):
+                picked[c, t] = last.tile([P, CH], F32, name="summed", align_bytes=64, offset=HS_LAST_AT)[:]
             if (c, t) == (0, 0):
-                picked[c, t] = keep.tile([P, CH], F32, name="summed_first")[:]
-            nc.vector.scalar_tensor_tensor(picked[c, t], acc[:], b_sb[:, t : t + 1], g, ALU.add, ALU.add)
+                picked[c, t] = last.tile([P, CH], F32, name="summed_first", align_bytes=64, offset=HS_THIRD_AT)[:]
+            weight = wgo_sb[:, c * CH : (c + 1) * CH]
+            if c == 0:
+                nc.vector.scalar_tensor_tensor(picked[c, t], acc[:], b_sb[:, t : t + 1], g, ALU.add, ALU.add)
+            else:
+                biased = ring.tile([P, CH], F32, name="biased")
+                nc.scalar.activation(biased[:], acc[:], ACT.Identity, bias=b_sb[:, t : t + 1])
+                nc.gpsimd.tensor_tensor(g, g, biased[:], ALU.add)
+                nc.gpsimd.tensor_tensor(g, g, weight, ALU.mult)
+            if (c, t) == (0, 3):
+                nc.vector.tensor_tensor(picked[c, t], picked[c, t], weight, ALU.mult)
             if (c, t) == (0, 0):
                 for w in range(2, NT):
                     windows.append(last.tile([P, T], F32, name=f"window{w}", align_bytes=64, offset=(w - 2) * T * 4))
                     nc.gpsimd.memset(windows[w][:], 0.0)
 
         def put(c, t):
-            nc.vector.tensor_tensor(
-                windows[t][:].indirect(chunk_offsets(c)),
-                picked[c, t],
-                wgo_sb[:, c * CH : (c + 1) * CH],
-                ALU.mult,
-            )
+            places = windows[t][:].indirect(chunk_offsets(c))
+            if c == 0 and t < 3:
+                nc.vector.tensor_tensor(places, picked[c, t], wgo_sb[:, c * CH : (c + 1) * CH], ALU.mult)
+            else:
+                nc.vector.tensor_copy(places, picked[c, t])
             if c == NCH - 1:
                 nc.sync.dma_start(out[t * P : (t + 1) * P, :], windows[t][:])
 
         steps = [(c, t) for c in range(NCH) for t in range(NT)]
         add_up(*steps[0])
         for s in range(len(steps)):
+            if s in (1, 2):
+                quantise(1, s - 1)
             if s + 1 < len(steps):
                 add_up(*steps[s + 1])
             put(*steps[s])

@@ -25,10 +25,10 @@ NT = N // P
 RB = R // PASS
 SHIFT = 4
 MOVED = 112
-HS_THIRD_AT = 2 * T * 4
-HS_LAST_AT = HS_THIRD_AT + CH * PACK * 2
-EARLY_BYTES = 2 * PASS * 4 + T * 4
-LATE_BYTES = (NT - 1) * T * 4 + N * 4 + N * 2 + N * 2 + J * 4 + 64
+HS_AT = 2 * T * 4
+HS_LAST_AT = HS_AT + CH * PACK * 2
+CODES_AT = HS_LAST_AT + CH * PACK * 2
+LATE_BYTES = NT * T * 4 + N * 4 + N * 2 + N * 2 + J * 4 + 2 * PASS * 4 + 64
 
 
 def tile_list_modp_relu2_mix_resb_kernel(
@@ -41,7 +41,6 @@ def tile_list_modp_relu2_mix_resb_kernel(
         ring = ctx.enter_context(tc.tile_pool(name="ring", bufs=2))
         late = ctx.enter_context(tc.tile_pool(name="late", bufs=1))
         mid = ctx.enter_context(tc.tile_pool(name="mid", bufs=1))
-        early = ctx.enter_context(tc.tile_pool(name="early", bufs=1))
         last = ctx.enter_context(tc.tile_pool(name="last", bufs=1))
         psum = ctx.enter_context(tc.psum_pool(name="psum", bufs=4))
 
@@ -53,8 +52,7 @@ def tile_list_modp_relu2_mix_resb_kernel(
 
         sm_sb = keep.tile([P, RB, PACK], F32, name="sm_sb")
         nc.sync.dma_start(sm_sb[:], sm.rearrange("(b p i) -> p b i", b=RB, i=PACK))
-        tab_sc_wide = early.tile([P, EARLY_BYTES // 4], I32, name="tab_sc", align_bytes=64, offset=0)
-        tab_sc = tab_sc_wide[:, 0 : T // 4]
+        tab_sc = keep.tile([P, T // 4], I32, name="tab_sc", align_bytes=64)[:]
         wu_sc = mid.tile([P, 2, R // 4], I32, name="wu_sc", align_bytes=64, offset=0)
         nc.gpsimd.memset(tab_sc, 0)
         nc.vector.memset(wu_sc[:], 0)
@@ -87,16 +85,18 @@ def tile_list_modp_relu2_mix_resb_kernel(
             )
         nc.gpsimd.tensor_tensor(root[:], mag, half[:], ALU.pow)
 
-        got_sc = keep.tile([P, J], U8, name="got_sc", align_bytes=64)
-        nc.vector.tensor_copy(got_sc[:], tab_sc.bitcast(U8).indirect(offsets[:]))
-        nc.sync.dma_start(got_sc1[0:MOVED, :], got_sc[:].bitcast(I32)[SHIFT : SHIFT + MOVED, :])
-        tab_planes = (got_sc[:], got_sc1[:].bitcast(U8))
+        tab_planes = []
+        wu_raw = [wu_raw0[:]]
 
-        r_sb = [early.tile([P, T], F32, name="r_sb0", align_bytes=64, offset=2 * PASS * 4)]
-        nc.sync.dma_start(r_sb[0][:], rT[0:P, :])
-        wu_raw1 = early.tile([P, 2, PASS], I32, name="wu_raw1", align_bytes=64, offset=0)
-        nc.sync.dma_start(wu_raw1[:], wu_view[:, :, PASS : 2 * PASS])
-        wu_raw = (wu_raw0[:], wu_raw1[:])
+        def gather_scales(c):
+            if c == 0:
+                got_sc = keep.tile([P, CH], U8, name="got_sc_first", align_bytes=64)
+            else:
+                got_sc = mid.tile([P, CH], U8, name="got_sc_second", align_bytes=64, offset=0)
+            moved = got_sc1[:, c * CH // 4 : (c + 1) * CH // 4]
+            nc.vector.tensor_copy(got_sc[:], tab_sc.bitcast(U8).indirect(chunk_offsets(c)))
+            nc.sync.dma_start(moved[0:MOVED, :], got_sc[:].bitcast(I32)[SHIFT : SHIFT + MOVED, :])
+            tab_planes.append((got_sc[:], moved.bitcast(U8)))
 
         wu_planes = []
         parted = []
@@ -118,43 +118,44 @@ def tile_list_modp_relu2_mix_resb_kernel(
 
         def permute_wu(rb):
             w = keep.tile([P, 2, PASS], I32, name=f"wu_p{rb}", align_bytes=64)
-            if rb == 0:
-                nc.vector.tensor_copy(
-                    w[:].rearrange("p a (i m) -> p a m i", i=PACK),
-                    wu_raw[rb].rearrange("p a (m i) -> p a m i", i=PACK),
-                )
-            else:
-                nc.gpsimd.tensor_copy(
-                    w[:].rearrange("p a (i m) -> p a i m", i=PACK),
-                    wu_raw[rb].rearrange("p a (m i) -> p a i m", i=PACK),
-                )
+            nc.vector.tensor_copy(
+                w[:].rearrange("p a (i m) -> p a m i", i=PACK),
+                wu_raw[rb].rearrange("p a (m i) -> p a m i", i=PACK),
+            )
             wu_p.append(w)
 
         def permute_wu_scales(rb):
             s = keep.tile([P, 2, PASS], U8, name=f"wup_sc{rb}", align_bytes=64)
             raw = wu_sc[:].rearrange("p a r -> p (a r)").bitcast(U8).rearrange("p (a b m i) -> p b a i m", a=2, b=RB, i=PACK)
-            nc.gpsimd.tensor_copy(s[:].rearrange("p a (i m) -> p a i m", i=PACK), raw[:, rb])
+            nc.vector.tensor_copy(s[:].rearrange("p a (i m) -> p a i m", i=PACK), raw[:, rb])
             wu_planes.append(s)
 
+        gather_scales(0)
         got0 = gather_words(0)
         permute_wu(0)
         part_words(got0, 0)
         permute_wu_scales(0)
+        permute_wu_scales(1)
+        gather_scales(1)
+        got1 = gather_words(1)
 
-        for t in range(1, NT):
-            r_sb.append(late.tile([P, T], F32, name=f"r_sb{t}", align_bytes=64, offset=(t - 1) * T * 4))
-        at = (NT - 1) * T * 4
+        r_sb = [late.tile([P, T], F32, name=f"r_sb{t}", align_bytes=64, offset=t * T * 4) for t in range(NT)]
+        at = NT * T * 4
         wd8_w = late.tile([P, N], I32, name="wd8_w", align_bytes=64, offset=at)
         wd4_w = late.tile([P, N // 2], I32, name="wd4_w", align_bytes=64, offset=at + N * 4)
         wd_sc = late.tile([P, 2, N // 4], I32, name="wd_sc", align_bytes=64, offset=at + N * 6)
         wgo_sb = late.tile([P, J], F32, name="wgo_sb", align_bytes=64, offset=at + N * 8)
-        b_sb = late.tile([P, NT], F32, name="b_sb", align_bytes=64, offset=at + N * 8 + J * 4)
+        wu_raw1 = late.tile([P, 2, PASS], I32, name="wu_raw1", align_bytes=64, offset=at + N * 8 + J * 4)
+        wu_raw.append(wu_raw1[:])
+        b_sb = late.tile([P, NT], F32, name="b_sb", align_bytes=64, offset=at + N * 8 + J * 4 + 2 * PASS * 4)
         nc.vector.memset(wd_sc[:], 0)
 
         def load_wd_scales(rb, sc):
             for q in range(4):
                 nc.sync.dma_start(wd_sc[32 * q : 32 * q + 4, rb, :], sc[0].bitcast(I32)[4 * q : 4 * q + 4, :])
 
+        nc.sync.dma_start(wu_raw1[:], wu_view[:, :, PASS : 2 * PASS])
+        nc.sync.dma_start(r_sb[0][:], rT[0:P, :])
         nc.sync.dma_start(r_sb[1][:], rT[P : 2 * P, :])
         load_wd_scales(0, wd8_scales)
         nc.sync.dma_start(r_sb[2][:], rT[2 * P : 3 * P, :])
@@ -166,9 +167,7 @@ def tile_list_modp_relu2_mix_resb_kernel(
         with nc.allow_non_contiguous_dma(reason="one bias value to a partition"):
             nc.sync.dma_start(b_sb[:], b.rearrange("(t p) -> p t", p=P))
 
-        permute_wu_scales(1)
         permute_wu(1)
-        got1 = gather_words(1)
         part_words(got1, 1)
 
         windows = []
@@ -191,17 +190,17 @@ def tile_list_modp_relu2_mix_resb_kernel(
                         lhsT=wu_p[rb][:, a, i * P : (i + 1) * P].bitcast(FP8X4),
                         lhsT_scale=wu_planes[rb][:, a, i * P : (i + 1) * P],
                         rhs=parted[c][:, a, :].bitcast(FP4X4),
-                        rhs_scale=tab_planes[a][:, c * CH : (c + 1) * CH],
+                        rhs_scale=tab_planes[c][a],
                         start=(a == 0),
                         stop=(a == 1),
                     )
                 col = rb * PACK + i
-                if (c, rb) != (1, 1):
+                if c == 0:
                     nc.scalar.activation(u[:, i, :], acc[:], ACT.Relu, scale=root[:, col : col + 1])
                 else:
                     nc.scalar.activation(u[:, i, :], acc[:], ACT.Relu)
             hb = ring.tile([P, CH * PACK], BF16, name="hb", align_bytes=64)
-            if (c, rb) != (1, 1):
+            if c == 0:
                 nc.scalar.activation(
                     hb[:].rearrange("p (g k i) -> p g i k", k=4, i=PACK),
                     u[:].rearrange("p i (g k) -> p g i k", k=4),
@@ -209,7 +208,7 @@ def tile_list_modp_relu2_mix_resb_kernel(
                 )
                 squared[c, rb] = hb
             else:
-                hs = last.tile([P, CH * PACK], BF16, name="hs_last", align_bytes=64, offset=HS_LAST_AT)
+                hs = last.tile([P, CH * PACK], BF16, name=f"hs_late{rb}", align_bytes=64, offset=HS_AT + rb * CH * PACK * 2)
                 squared[c, rb] = hs
                 sq = ring.tile([P, PACK, CH], F32, name="sq")
                 nc.scalar.activation(sq[:], u[:], ACT.Square)
@@ -222,13 +221,13 @@ def tile_list_modp_relu2_mix_resb_kernel(
 
         def quantise(c, rb):
             hs = squared[c, rb]
-            if (c, rb) != (1, 1):
-                if c == 0:
-                    hs = late.tile([P, CH * PACK], BF16, name=f"hs{rb}", align_bytes=64, offset=rb * T * 4)
-                else:
-                    hs = last.tile([P, CH * PACK], BF16, name="hs_third", align_bytes=64, offset=HS_THIRD_AT)
+            if c == 0:
+                hs = late.tile([P, CH * PACK], BF16, name=f"hs{rb}", align_bytes=64, offset=(rb + 1) * T * 4)
                 nc.vector.tensor_tensor(hs[:], squared[c, rb][:], sign_bf[:, rb, :], ALU.mult)
-            codes = keep.tile([P, CH], U32, name=f"h_codes{c}{rb}", align_bytes=64)
+            if (c, rb) == (1, 0):
+                codes = last.tile([P, CH], U32, name="h_codes_third", align_bytes=64, offset=CODES_AT)
+            else:
+                codes = keep.tile([P, CH], U32, name=f"h_codes{c}{rb}", align_bytes=64)
             scales = keep.tile([P, CH], U8, name=f"h_scales{c}{rb}", align_bytes=64)
             nc.vector.quantize_mx(out=codes[:].bitcast(FP8X4), scales=scales[:], in_=hs[:])
             h_codes[c, rb], h_scales[c, rb] = codes, scales
@@ -281,7 +280,7 @@ def tile_list_modp_relu2_mix_resb_kernel(
             if (c, t) == (0, 3):
                 picked[c, t] = last.tile([P, CH], F32, name="summed", align_bytes=64, offset=HS_LAST_AT)[:]
             if (c, t) == (0, 0):
-                picked[c, t] = last.tile([P, CH], F32, name="summed_first", align_bytes=64, offset=HS_THIRD_AT)[:]
+                picked[c, t] = last.tile([P, CH], F32, name="summed_first", align_bytes=64, offset=CODES_AT)[:]
             weight = wgo_sb[:, c * CH : (c + 1) * CH]
             if c == 0:
                 nc.vector.scalar_tensor_tensor(picked[c, t], acc[:], b_sb[:, t : t + 1], g, ALU.add, ALU.add)

@@ -19,16 +19,33 @@ ACT = mybir.ActivationFunctionType
 P = 128
 PACK = 4
 PASS = P * PACK
-CH = 512
-NCH = J // CH
-NT = N // P
-RB = R // PASS
-SHIFT = 4
-MOVED = 112
-HS_AT = 2 * T * 4
-HS_LAST_AT = HS_AT + CH * PACK * 2
-CODES_AT = HS_LAST_AT + CH * PACK * 2
-LATE_BYTES = NT * T * 4 + N * 4 + N * 2 + N * 2 + J * 4 + 2 * PASS * 4 + 64
+K_PASSES = K // PASS
+R_BLOCKS = R // PASS
+N_TILES = N // P
+CHUNK = 512
+CHUNKS = J // CHUNK
+QUADS = 4
+RUN = 4
+ALIGN = 64
+MOVED_ROWS = 112
+
+SIGN_ON_VECTOR = {(0, 0): CHUNK, (0, 1): CHUNK, (1, 0): CHUNK // 2, (1, 1): 0}
+
+ROW_BYTES = T * 4
+H_BYTES = CHUNK * PACK * 2
+CHUNK_BYTES = CHUNK * 4
+EARLY_WU, EARLY_R = 0, K_PASSES * PASS * 4
+EARLY_BYTES = EARLY_R + ROW_BYTES
+LATE_WD8 = (N_TILES - 1) * ROW_BYTES
+LATE_WD4 = LATE_WD8 + N * 4
+LATE_WD_SCALES = LATE_WD4 + N * 2
+LATE_WGO = LATE_WD_SCALES + R_BLOCKS * N
+LATE_B = LATE_WGO + J * 4
+LATE_BYTES = LATE_B + ALIGN
+LAST_H = 2 * ROW_BYTES
+LAST_CODES = LAST_H + H_BYTES
+LAST_SIGNED = LAST_CODES + CHUNK_BYTES
+LAST_FIRST_SUM = LAST_SIGNED - CHUNK_BYTES // 2
 
 
 def tile_list_modp_relu2_mix_resb_kernel(
@@ -39,8 +56,9 @@ def tile_list_modp_relu2_mix_resb_kernel(
     with ExitStack() as ctx:
         keep = ctx.enter_context(tc.tile_pool(name="keep", bufs=1))
         ring = ctx.enter_context(tc.tile_pool(name="ring", bufs=2))
-        late = ctx.enter_context(tc.tile_pool(name="late", bufs=1))
+        early = ctx.enter_context(tc.tile_pool(name="early", bufs=1))
         mid = ctx.enter_context(tc.tile_pool(name="mid", bufs=1))
+        late = ctx.enter_context(tc.tile_pool(name="late", bufs=1))
         last = ctx.enter_context(tc.tile_pool(name="last", bufs=1))
         psum = ctx.enter_context(tc.psum_pool(name="psum", bufs=4))
 
@@ -48,220 +66,224 @@ def tile_list_modp_relu2_mix_resb_kernel(
         nc.sync.dma_start(offsets[:], offs)
 
         def chunk_offsets(c):
-            return offsets[:, c * (CH // 16) : (c + 1) * (CH // 16)]
+            return offsets[:, c * (CHUNK // 16) : (c + 1) * (CHUNK // 16)]
 
-        sm_sb = keep.tile([P, RB, PACK], F32, name="sm_sb")
-        nc.sync.dma_start(sm_sb[:], sm.rearrange("(b p i) -> p b i", b=RB, i=PACK))
-        tab_sc = keep.tile([P, T // 4], I32, name="tab_sc", align_bytes=64)[:]
-        wu_sc = mid.tile([P, 2, R // 4], I32, name="wu_sc", align_bytes=64, offset=0)
+        def quad_rows(q, count):
+            return slice(32 * q, 32 * q + count)
+
+        sm_sb = keep.tile([P, R_BLOCKS, PACK], F32, name="sm_sb")
+        nc.sync.dma_start(sm_sb[:], sm.rearrange("(b p i) -> p b i", b=R_BLOCKS, i=PACK))
+
+        tab_sc = early.tile([P, EARLY_BYTES // 4], I32, name="tab_sc", align_bytes=ALIGN, offset=0)[:, 0 : T // 4]
+        wu_sc = mid.tile([P, K_PASSES, R // 4], I32, name="wu_sc", align_bytes=ALIGN, offset=0)
+        moved_sc = keep.tile([P, J // 4], I32, name="moved_sc", align_bytes=ALIGN)
+        half = keep.tile([P, R_BLOCKS * PACK], F32, name="half")
         nc.gpsimd.memset(tab_sc, 0)
         nc.vector.memset(wu_sc[:], 0)
-        got_sc1 = keep.tile([P, J // 4], I32, name="got_sc1", align_bytes=64)
-        half = keep.tile([P, RB * PACK], F32, name="half")
         nc.gpsimd.memset(half[:], 0.5)
-        nc.gpsimd.memset(got_sc1[:], 0)
+        nc.gpsimd.memset(moved_sc[:], 0)
 
-        for q in range(4):
-            nc.sync.dma_start(tab_sc[32 * q : 32 * q + 8, :], tab_scales.bitcast(I32)[:, 4 * q : 4 * q + 4, :])
-        tab_w = keep.tile([P, T], I32, name="tab_w", align_bytes=64)
+        for q in range(QUADS):
+            nc.sync.dma_start(
+                tab_sc[quad_rows(q, K_PASSES * PACK), :], tab_scales.bitcast(I32)[:, PACK * q : PACK * (q + 1), :]
+            )
+        tab_w = keep.tile([P, T], I32, name="tab_w", align_bytes=ALIGN)
         nc.sync.dma_start(tab_w[:], tab_words[0].rearrange("p t f -> p (t f)").bitcast(I32))
         wu_view = wu_words.rearrange("a p r i -> p a (r i)").bitcast(I32)
-        wu_raw0 = keep.tile([P, 2, PASS], I32, name="wu_raw0", align_bytes=64)
-        nc.sync.dma_start(wu_raw0[:], wu_view[:, :, 0:PASS])
+        wu_raw = [keep.tile([P, K_PASSES, PASS], I32, name="wu_raw0", align_bytes=ALIGN)]
+        nc.sync.dma_start(wu_raw[0][:], wu_view[:, :, 0:PASS])
         wu_sc_view = wu_scales.bitcast(I32).rearrange("a q r -> q a r")
-        for q in range(4):
-            nc.sync.dma_start(wu_sc[32 * q : 32 * q + 4, :, :], wu_sc_view[4 * q : 4 * q + 4, :, :])
+        for q in range(QUADS):
+            nc.sync.dma_start(wu_sc[quad_rows(q, PACK), :, :], wu_sc_view[PACK * q : PACK * (q + 1), :, :])
 
         sm_flat = sm_sb[:].rearrange("p b i -> p (b i)")
-        sign_bf = keep.tile([P, RB, CH * PACK], BF16, name="sign_bf", align_bytes=64)
-        mag = keep.tile([P, RB * PACK], F32, name="mag")[:]
-        root = keep.tile([P, RB * PACK], F32, name="root")
-        nc.scalar.activation(mag, sm_flat, ACT.Abs)
-        for rb in range(RB):
+        magnitude = keep.tile([P, R_BLOCKS * PACK], F32, name="magnitude")
+        root = keep.tile([P, R_BLOCKS * PACK], F32, name="root")
+        sign = keep.tile([P, R_BLOCKS * PACK], F32, name="sign")
+        sign_wide = keep.tile([P, R_BLOCKS, CHUNK * PACK], BF16, name="sign_wide", align_bytes=ALIGN)
+        nc.scalar.activation(magnitude[:], sm_flat, ACT.Abs)
+        nc.scalar.activation(sign[:], sm_flat, ACT.Sign)
+        for rb in range(R_BLOCKS):
             nc.scalar.activation(
-                sign_bf[:, rb, :].rearrange("p (j i) -> p j i", i=PACK),
-                sm_sb[:, rb, :].unsqueeze(1).to_broadcast([P, CH, PACK]),
+                sign_wide[:, rb, :].rearrange("p (j i) -> p j i", i=PACK),
+                sm_sb[:, rb, :].unsqueeze(1).to_broadcast([P, CHUNK, PACK]),
                 ACT.Sign,
             )
-        nc.gpsimd.tensor_tensor(root[:], mag, half[:], ALU.pow)
+        nc.gpsimd.tensor_tensor(root[:], magnitude[:], half[:], ALU.pow)
 
-        tab_planes = []
-        wu_raw = [wu_raw0[:]]
+        picked_sc = keep.tile([P, J], U8, name="picked_sc", align_bytes=ALIGN)
+        nc.vector.tensor_copy(picked_sc[:], tab_sc.bitcast(U8).indirect(offsets[:]))
+        nc.sync.dma_start(moved_sc[0:MOVED_ROWS, :], picked_sc[:].bitcast(I32)[PACK : PACK + MOVED_ROWS, :])
+        tab_planes = (picked_sc[:], moved_sc[:].bitcast(U8))
 
-        def gather_scales(c):
-            if c == 0:
-                got_sc = keep.tile([P, CH], U8, name="got_sc_first", align_bytes=64)
-            else:
-                got_sc = mid.tile([P, CH], U8, name="got_sc_second", align_bytes=64, offset=0)
-            moved = got_sc1[:, c * CH // 4 : (c + 1) * CH // 4]
-            nc.vector.tensor_copy(got_sc[:], tab_sc.bitcast(U8).indirect(chunk_offsets(c)))
-            nc.sync.dma_start(moved[0:MOVED, :], got_sc[:].bitcast(I32)[SHIFT : SHIFT + MOVED, :])
-            tab_planes.append((got_sc[:], moved.bitcast(U8)))
+        wu_raw.append(early.tile([P, K_PASSES, PASS], I32, name="wu_raw1", align_bytes=ALIGN, offset=EARLY_WU))
+        nc.sync.dma_start(wu_raw[1][:], wu_view[:, :, PASS : 2 * PASS])
+        r_sb = [early.tile([P, T], F32, name="r_sb0", align_bytes=ALIGN, offset=EARLY_R)]
+        nc.sync.dma_start(r_sb[0][:], rT[0:P, :])
 
-        wu_planes = []
-        parted = []
-        wu_p = []
+        parted, wu_codes, wu_planes = [], [], []
 
-        def gather_words(c):
-            if c == 0:
-                wide = late.tile([P, LATE_BYTES // 4], U32, name="got_first", align_bytes=64, offset=0)
-                got = wide[:, 0:CH]
-            else:
-                got = mid.tile([P, CH], U32, name="got_second", align_bytes=64, offset=CH)[:]
-            nc.vector.tensor_copy(got, tab_w[:].bitcast(U32).indirect(chunk_offsets(c)))
-            return got
+        def gather_words(c, picked_w):
+            nc.vector.tensor_copy(picked_w, tab_w[:].bitcast(U32).indirect(chunk_offsets(c)))
 
-        def part_words(got, c):
-            pt = keep.tile([P, 2, CH], U16, name=f"parted{c}", align_bytes=64)
-            nc.vector.tensor_copy(pt[:], got.bitcast(U16).rearrange("p (j d) -> p d j", d=2))
-            parted.append(pt)
+        def part_words(c, picked_w):
+            words = keep.tile([P, K_PASSES, CHUNK], U16, name=f"parted{c}", align_bytes=ALIGN)
+            nc.vector.tensor_copy(words[:], picked_w.bitcast(U16).rearrange("p (j a) -> p a j", a=K_PASSES))
+            parted.append(words)
 
-        def permute_wu(rb):
-            w = keep.tile([P, 2, PASS], I32, name=f"wu_p{rb}", align_bytes=64)
+        def reorder_wu_words(rb):
+            words = keep.tile([P, K_PASSES, PASS], I32, name=f"wu_codes{rb}", align_bytes=ALIGN)
             nc.vector.tensor_copy(
-                w[:].rearrange("p a (i m) -> p a m i", i=PACK),
-                wu_raw[rb].rearrange("p a (m i) -> p a m i", i=PACK),
+                words[:].rearrange("p a (i m) -> p a m i", i=PACK),
+                wu_raw[rb][:].rearrange("p a (m i) -> p a m i", i=PACK),
             )
-            wu_p.append(w)
+            wu_codes.append(words)
 
-        def permute_wu_scales(rb):
-            s = keep.tile([P, 2, PASS], U8, name=f"wup_sc{rb}", align_bytes=64)
-            raw = wu_sc[:].rearrange("p a r -> p (a r)").bitcast(U8).rearrange("p (a b m i) -> p b a i m", a=2, b=RB, i=PACK)
-            nc.vector.tensor_copy(s[:].rearrange("p a (i m) -> p a i m", i=PACK), raw[:, rb])
-            wu_planes.append(s)
+        def reorder_wu_scales(rb):
+            plane = keep.tile([P, K_PASSES, PASS], U8, name=f"wu_plane{rb}", align_bytes=ALIGN)
+            loaded = wu_sc[:].rearrange("p a r -> p (a r)").bitcast(U8)
+            loaded = loaded.rearrange("p (a b m i) -> p b a i m", a=K_PASSES, b=R_BLOCKS, i=PACK)
+            nc.vector.tensor_copy(plane[:].rearrange("p a (i m) -> p a i m", i=PACK), loaded[:, rb])
+            wu_planes.append(plane)
 
-        gather_scales(0)
-        got0 = gather_words(0)
-        permute_wu(0)
-        part_words(got0, 0)
-        permute_wu_scales(0)
-        permute_wu_scales(1)
-        gather_scales(1)
-        got1 = gather_words(1)
+        picked_w0 = late.tile([P, LATE_BYTES // 4], U32, name="picked_w0", align_bytes=ALIGN, offset=0)[:, 0:CHUNK]
+        gather_words(0, picked_w0)
+        reorder_wu_words(0)
+        part_words(0, picked_w0)
+        reorder_wu_scales(0)
 
-        r_sb = [late.tile([P, T], F32, name=f"r_sb{t}", align_bytes=64, offset=t * T * 4) for t in range(NT)]
-        at = NT * T * 4
-        wd8_w = late.tile([P, N], I32, name="wd8_w", align_bytes=64, offset=at)
-        wd4_w = late.tile([P, N // 2], I32, name="wd4_w", align_bytes=64, offset=at + N * 4)
-        wd_sc = late.tile([P, 2, N // 4], I32, name="wd_sc", align_bytes=64, offset=at + N * 6)
-        wgo_sb = late.tile([P, J], F32, name="wgo_sb", align_bytes=64, offset=at + N * 8)
-        wu_raw1 = late.tile([P, 2, PASS], I32, name="wu_raw1", align_bytes=64, offset=at + N * 8 + J * 4)
-        wu_raw.append(wu_raw1[:])
-        b_sb = late.tile([P, NT], F32, name="b_sb", align_bytes=64, offset=at + N * 8 + J * 4 + 2 * PASS * 4)
+        for t in range(1, N_TILES):
+            r_sb.append(late.tile([P, T], F32, name=f"r_sb{t}", align_bytes=ALIGN, offset=(t - 1) * ROW_BYTES))
+        wd8_w = late.tile([P, N], I32, name="wd8_w", align_bytes=ALIGN, offset=LATE_WD8)
+        wd4_w = late.tile([P, N // 2], I32, name="wd4_w", align_bytes=ALIGN, offset=LATE_WD4)
+        wd_sc = late.tile([P, R_BLOCKS, N // 4], I32, name="wd_sc", align_bytes=ALIGN, offset=LATE_WD_SCALES)
+        wgo_sb = late.tile([P, J], F32, name="wgo_sb", align_bytes=ALIGN, offset=LATE_WGO)
+        b_sb = late.tile([P, N_TILES], F32, name="b_sb", align_bytes=ALIGN, offset=LATE_B)
         nc.vector.memset(wd_sc[:], 0)
 
-        def load_wd_scales(rb, sc):
-            for q in range(4):
-                nc.sync.dma_start(wd_sc[32 * q : 32 * q + 4, rb, :], sc[0].bitcast(I32)[4 * q : 4 * q + 4, :])
+        def load_residual(t):
+            nc.sync.dma_start(r_sb[t][:], rT[t * P : (t + 1) * P, :])
 
-        nc.sync.dma_start(wu_raw1[:], wu_view[:, :, PASS : 2 * PASS])
-        nc.sync.dma_start(r_sb[0][:], rT[0:P, :])
-        nc.sync.dma_start(r_sb[1][:], rT[P : 2 * P, :])
+        def load_wd_scales(rb, scales):
+            for q in range(QUADS):
+                nc.sync.dma_start(
+                    wd_sc[quad_rows(q, PACK), rb, :], scales[0].bitcast(I32)[PACK * q : PACK * (q + 1), :]
+                )
+
+        load_residual(1)
         load_wd_scales(0, wd8_scales)
-        nc.sync.dma_start(r_sb[2][:], rT[2 * P : 3 * P, :])
+        load_residual(2)
         nc.sync.dma_start(wd8_w[:], wd8_words[0].rearrange("p n i -> p (n i)").bitcast(I32))
         nc.sync.dma_start(wd4_w[:], wd4_words[0].bitcast(I32))
-        nc.sync.dma_start(r_sb[3][:], rT[3 * P : 4 * P, :])
+        load_residual(3)
         load_wd_scales(1, wd4_scales)
         nc.sync.dma_start(wgo_sb[:], wgo)
         with nc.allow_non_contiguous_dma(reason="one bias value to a partition"):
             nc.sync.dma_start(b_sb[:], b.rearrange("(t p) -> p t", p=P))
 
-        permute_wu(1)
-        part_words(got1, 1)
+        reorder_wu_scales(1)
+        reorder_wu_words(1)
+        picked_w1 = mid.tile([P, CHUNK], U32, name="picked_w1", align_bytes=ALIGN, offset=0)[:]
+        gather_words(1, picked_w1)
+        part_words(1, picked_w1)
 
         windows = []
-        for t in range(2):
-            w = keep.tile([P, T], F32, name=f"window{t}", align_bytes=64)
-            nc.vector.memset(w[:], 0.0)
-            windows.append(w)
+        for t in range(N_TILES // 2):
+            windows.append(keep.tile([P, T], F32, name=f"window{t}", align_bytes=ALIGN))
+            nc.vector.memset(windows[t][:], 0.0)
 
-        h_codes, h_scales = {}, {}
+        unsigned, finished, h_codes, h_scales, picked_r = {}, {}, {}, {}, {}
 
-        squared = {}
+        def interleaved(values):
+            return values.rearrange("p (g k i) -> p g i k", k=RUN, i=PACK)
+
+        def by_output(values):
+            return values.rearrange("p i (g k) -> p g i k", k=RUN)
 
         def hidden(c, rb):
-            u = ring.tile([P, PACK, CH], F32, name="u")
+            rooted = ring.tile([P, PACK, CHUNK], F32, name="rooted")
             for i in range(PACK):
-                acc = psum.tile([P, CH], F32, name="acc_a")
-                for a in range(2):
+                acc = psum.tile([P, CHUNK], F32, name="acc_a")
+                for a in range(K_PASSES):
                     nc.tensor.matmul_mx(
                         out=acc[:],
-                        lhsT=wu_p[rb][:, a, i * P : (i + 1) * P].bitcast(FP8X4),
+                        lhsT=wu_codes[rb][:, a, i * P : (i + 1) * P].bitcast(FP8X4),
                         lhsT_scale=wu_planes[rb][:, a, i * P : (i + 1) * P],
                         rhs=parted[c][:, a, :].bitcast(FP4X4),
-                        rhs_scale=tab_planes[c][a],
+                        rhs_scale=tab_planes[a][:, c * CHUNK : (c + 1) * CHUNK],
                         start=(a == 0),
-                        stop=(a == 1),
+                        stop=(a == K_PASSES - 1),
                     )
                 col = rb * PACK + i
-                if c == 0:
-                    nc.scalar.activation(u[:, i, :], acc[:], ACT.Relu, scale=root[:, col : col + 1])
+                nc.scalar.activation(rooted[:, i, :], acc[:], ACT.Relu, scale=root[:, col : col + 1])
+            split = SIGN_ON_VECTOR[c, rb]
+            if split > 0:
+                unsigned[c, rb] = keep.tile([P, split * PACK], BF16, name=f"unsigned{c}{rb}", align_bytes=ALIGN)
+                nc.scalar.activation(interleaved(unsigned[c, rb][:]), by_output(rooted[:, :, 0:split]), ACT.Square)
+            if split < CHUNK:
+                rest = CHUNK - split
+                squares = keep.tile([P, PACK, rest], F32, name=f"squares{rb}")
+                rounded = keep.tile([P, PACK, rest], BF16, name=f"rounded{rb}")
+                if rb == R_BLOCKS - 1:
+                    finished[c, rb] = last.tile([P, rest * PACK], BF16, name="finished1", align_bytes=ALIGN, offset=LAST_H)
                 else:
-                    nc.scalar.activation(u[:, i, :], acc[:], ACT.Relu)
-            hb = ring.tile([P, CH * PACK], BF16, name="hb", align_bytes=64)
-            if c == 0:
-                nc.scalar.activation(
-                    hb[:].rearrange("p (g k i) -> p g i k", k=4, i=PACK),
-                    u[:].rearrange("p i (g k) -> p g i k", k=4),
-                    ACT.Square,
-                )
-                squared[c, rb] = hb
-            else:
-                hs = last.tile([P, CH * PACK], BF16, name=f"hs_late{rb}", align_bytes=64, offset=HS_AT + rb * CH * PACK * 2)
-                squared[c, rb] = hs
-                sq = ring.tile([P, PACK, CH], F32, name="sq")
-                nc.scalar.activation(sq[:], u[:], ACT.Square)
+                    finished[c, rb] = keep.tile([P, rest * PACK], BF16, name="finished0", align_bytes=ALIGN)
+                nc.scalar.activation(squares[:], rooted[:, :, split:CHUNK], ACT.Square)
                 for i in range(PACK):
-                    nc.scalar.activation(hb[:, i * CH : (i + 1) * CH], sq[:, i, :], ACT.Copy, scale=sm_sb[:, rb, i : i + 1])
-                nc.scalar.copy(
-                    hs[:].rearrange("p (g k i) -> p g i k", k=4, i=PACK),
-                    hb[:].rearrange("p (i g k) -> p g i k", k=4, i=PACK),
-                )
+                    col = rb * PACK + i
+                    nc.scalar.activation(rounded[:, i, :], squares[:, i, :], ACT.Copy, scale=sign[:, col : col + 1])
+                nc.scalar.copy(interleaved(finished[c, rb][:]), by_output(rounded[:]))
 
         def quantise(c, rb):
-            hs = squared[c, rb]
-            if c == 0:
-                hs = late.tile([P, CH * PACK], BF16, name=f"hs{rb}", align_bytes=64, offset=(rb + 1) * T * 4)
-                nc.vector.tensor_tensor(hs[:], squared[c, rb][:], sign_bf[:, rb, :], ALU.mult)
+            split = SIGN_ON_VECTOR[c, rb]
             if (c, rb) == (1, 0):
-                codes = last.tile([P, CH], U32, name="h_codes_third", align_bytes=64, offset=CODES_AT)
+                codes = last.tile([P, CHUNK], U32, name="h_codes10", align_bytes=ALIGN, offset=LAST_CODES)
             else:
-                codes = keep.tile([P, CH], U32, name=f"h_codes{c}{rb}", align_bytes=64)
-            scales = keep.tile([P, CH], U8, name=f"h_scales{c}{rb}", align_bytes=64)
-            nc.vector.quantize_mx(out=codes[:].bitcast(FP8X4), scales=scales[:], in_=hs[:])
+                codes = keep.tile([P, CHUNK], U32, name=f"h_codes{c}{rb}", align_bytes=ALIGN)
+            scales = keep.tile([P, CHUNK], U8, name=f"h_scales{c}{rb}", align_bytes=ALIGN)
             h_codes[c, rb], h_scales[c, rb] = codes, scales
-
-        picked = {}
+            if split > 0:
+                if c == 0:
+                    signed = late.tile([P, split * PACK], BF16, name=f"signed0{rb}", align_bytes=ALIGN, offset=rb * ROW_BYTES)
+                else:
+                    signed = last.tile([P, split * PACK], BF16, name="signed10", align_bytes=ALIGN, offset=LAST_SIGNED)
+                nc.vector.tensor_tensor(signed[:], unsigned[c, rb][:], sign_wide[:, rb, 0 : split * PACK], ALU.mult)
+            if split < CHUNK:
+                nc.vector.quantize_mx(
+                    out=codes[:, split:CHUNK].bitcast(FP8X4), scales=scales[:, split:CHUNK], in_=finished[c, rb][:]
+                )
+            if split > 0:
+                nc.vector.quantize_mx(out=codes[:, 0:split].bitcast(FP8X4), scales=scales[:, 0:split], in_=signed[:])
 
         def gather_residual(t):
-            g = keep.tile([P, J], F32, name=f"picked{t}")
-            nc.vector.tensor_copy(g[:], r_sb[t][:].indirect(offsets[:]))
-            for c in range(NCH):
-                picked[c, t] = g[:, c * CH : (c + 1) * CH]
+            both = keep.tile([P, J], F32, name=f"picked_r{t}")
+            nc.vector.tensor_copy(both[:], r_sb[t][:].indirect(offsets[:]))
+            for c in range(CHUNKS):
+                picked_r[c, t] = both[:, c * CHUNK : (c + 1) * CHUNK]
 
-        first = last.tile([P, 2 * T], F32, name="picked_first", align_bytes=64, offset=0)
-        nc.vector.tensor_copy(first[:, 0:CH], r_sb[0][:].indirect(chunk_offsets(0)))
-        picked[0, 0] = first[:, 0:CH]
-        second = keep.tile([P, CH], F32, name="picked_second")
-        nc.vector.tensor_copy(second[:], r_sb[0][:].indirect(chunk_offsets(1)))
-        picked[1, 0] = second[:]
-        for rb in range(RB):
+        picked_r[0, 0] = last.tile([P, LAST_H // 4], F32, name="picked_r00", align_bytes=ALIGN, offset=0)[:, 0:CHUNK]
+        picked_r[1, 0] = keep.tile([P, CHUNK], F32, name="picked_r10")[:]
+        for c in range(CHUNKS):
+            nc.vector.tensor_copy(picked_r[c, 0], r_sb[0][:].indirect(chunk_offsets(c)))
+        for rb in range(R_BLOCKS):
             hidden(0, rb)
             gather_residual(rb + 1)
             quantise(0, rb)
-        gather_residual(3)
-        for rb in range(RB):
+        gather_residual(N_TILES - 1)
+        for rb in range(R_BLOCKS):
             hidden(1, rb)
 
-        wd_sc8 = wd_sc[:].rearrange("p a n -> p (a n)").bitcast(U8)
+        wd_planes = wd_sc[:].rearrange("p b n -> p (b n)").bitcast(U8)
+        steps = [(c, t) for c in range(CHUNKS) for t in range(N_TILES)]
+        first_step, turn_step = (0, 0), (0, N_TILES - 1)
+        summed = {}
 
         def add_up(c, t):
-            acc = psum.tile([P, CH], F32, name="acc_y")
+            acc = psum.tile([P, CHUNK], F32, name="acc_y")
             nc.tensor.matmul_mx(
                 out=acc[:],
                 lhsT=wd8_w[:, t * P : (t + 1) * P].bitcast(FP8X4),
-                lhsT_scale=wd_sc8[:, t * P : (t + 1) * P],
+                lhsT_scale=wd_planes[:, t * P : (t + 1) * P],
                 rhs=h_codes[c, 0][:].bitcast(FP8X4),
                 rhs_scale=h_scales[c, 0][:],
                 start=True,
@@ -270,46 +292,49 @@ def tile_list_modp_relu2_mix_resb_kernel(
             nc.tensor.matmul_mx(
                 out=acc[:],
                 lhsT=wd4_w[:, t * P // 2 : (t + 1) * P // 2].bitcast(FP4X4),
-                lhsT_scale=wd_sc8[:, N + t * P : N + (t + 1) * P],
+                lhsT_scale=wd_planes[:, N + t * P : N + (t + 1) * P],
                 rhs=h_codes[c, 1][:].bitcast(FP8X4),
                 rhs_scale=h_scales[c, 1][:],
                 start=False,
                 stop=True,
             )
-            g = picked[c, t]
-            if (c, t) == (0, 3):
-                picked[c, t] = last.tile([P, CH], F32, name="summed", align_bytes=64, offset=HS_LAST_AT)[:]
-            if (c, t) == (0, 0):
-                picked[c, t] = last.tile([P, CH], F32, name="summed_first", align_bytes=64, offset=CODES_AT)[:]
-            weight = wgo_sb[:, c * CH : (c + 1) * CH]
-            if c == 0:
-                nc.vector.scalar_tensor_tensor(picked[c, t], acc[:], b_sb[:, t : t + 1], g, ALU.add, ALU.add)
+            residual = picked_r[c, t]
+            weight = wgo_sb[:, c * CHUNK : (c + 1) * CHUNK]
+            if (c, t) == first_step:
+                total = last.tile([P, CHUNK], F32, name="first_sum", align_bytes=ALIGN, offset=LAST_FIRST_SUM)[:]
+            elif (c, t) == turn_step:
+                total = last.tile([P, CHUNK], F32, name="turn_sum", align_bytes=ALIGN, offset=LAST_H)[:]
             else:
-                biased = ring.tile([P, CH], F32, name="biased")
+                total = residual
+            summed[c, t] = total
+            if c == 0:
+                nc.vector.scalar_tensor_tensor(total, acc[:], b_sb[:, t : t + 1], residual, ALU.add, ALU.add)
+            else:
+                biased = ring.tile([P, CHUNK], F32, name="biased")
                 nc.scalar.activation(biased[:], acc[:], ACT.Identity, bias=b_sb[:, t : t + 1])
-                nc.gpsimd.tensor_tensor(g, g, biased[:], ALU.add)
-                nc.gpsimd.tensor_tensor(g, g, weight, ALU.mult)
-            if (c, t) == (0, 3):
-                nc.vector.tensor_tensor(picked[c, t], picked[c, t], weight, ALU.mult)
-            if (c, t) == (0, 0):
-                for w in range(2, NT):
-                    windows.append(last.tile([P, T], F32, name=f"window{w}", align_bytes=64, offset=(w - 2) * T * 4))
+                nc.gpsimd.tensor_tensor(total, residual, biased[:], ALU.add)
+                nc.gpsimd.tensor_tensor(total, total, weight, ALU.mult)
+            if (c, t) == turn_step:
+                nc.vector.tensor_tensor(total, total, weight, ALU.mult)
+            if (c, t) == first_step:
+                for w in range(N_TILES // 2, N_TILES):
+                    at = (w - N_TILES // 2) * ROW_BYTES
+                    windows.append(last.tile([P, T], F32, name=f"window{w}", align_bytes=ALIGN, offset=at))
                     nc.gpsimd.memset(windows[w][:], 0.0)
 
-        def put(c, t):
+        def scatter(c, t):
             places = windows[t][:].indirect(chunk_offsets(c))
-            if c == 0 and t < 3:
-                nc.vector.tensor_tensor(places, picked[c, t], wgo_sb[:, c * CH : (c + 1) * CH], ALU.mult)
+            if (c, t) < turn_step:
+                nc.vector.tensor_tensor(places, summed[c, t], wgo_sb[:, c * CHUNK : (c + 1) * CHUNK], ALU.mult)
             else:
-                nc.vector.tensor_copy(places, picked[c, t])
-            if c == NCH - 1:
+                nc.vector.tensor_copy(places, summed[c, t])
+            if c == CHUNKS - 1:
                 nc.sync.dma_start(out[t * P : (t + 1) * P, :], windows[t][:])
 
-        steps = [(c, t) for c in range(NCH) for t in range(NT)]
         add_up(*steps[0])
         for s in range(len(steps)):
-            if s in (1, 2):
+            if 1 <= s <= R_BLOCKS:
                 quantise(1, s - 1)
             if s + 1 < len(steps):
                 add_up(*steps[s + 1])
-            put(*steps[s])
+            scatter(*steps[s])

@@ -27,25 +27,24 @@ CHUNKS = J // CHUNK
 QUADS = 4
 RUN = 4
 ALIGN = 64
-MOVED_ROWS = 112
 
-SIGN_ON_VECTOR = {(0, 0): CHUNK, (0, 1): CHUNK, (1, 0): CHUNK // 2, (1, 1): 0}
+
+SIGN_TOKENS = 128
+HALF = CHUNK // 2
+FILLER_ROWS = 32 - K_PASSES * PACK
+MOVED_ROWS = 32 * (QUADS - 1) + PACK
+
+SIGN_ON_VECTOR = {(0, 0): CHUNK, (0, 1): CHUNK, (1, 0): CHUNK, (1, 1): 0}
+HALVED_STEPS = 2
 
 ROW_BYTES = T * 4
-H_BYTES = CHUNK * PACK * 2
 CHUNK_BYTES = CHUNK * 4
-EARLY_WU, EARLY_R = 0, K_PASSES * PASS * 4
-EARLY_BYTES = EARLY_R + ROW_BYTES
-LATE_WD8 = (N_TILES - 1) * ROW_BYTES
-LATE_WD4 = LATE_WD8 + N * 4
-LATE_WD_SCALES = LATE_WD4 + N * 2
-LATE_WGO = LATE_WD_SCALES + R_BLOCKS * N
-LATE_B = LATE_WGO + J * 4
-LATE_BYTES = LATE_B + ALIGN
-LAST_H = 2 * ROW_BYTES
-LAST_CODES = LAST_H + H_BYTES
-LAST_SIGNED = LAST_CODES + CHUNK_BYTES
-LAST_FIRST_SUM = LAST_SIGNED - CHUNK_BYTES // 2
+EARLY_WD8 = N_TILES * ROW_BYTES
+EARLY_WD4 = EARLY_WD8 + N * 4
+EARLY_WD_SCALES = EARLY_WD4 + N * 2
+EARLY_WGO = EARLY_WD_SCALES + R_BLOCKS * N
+EARLY_B = EARLY_WGO + J * 4
+EARLY_BYTES = EARLY_B + ALIGN
 
 
 def tile_list_modp_relu2_mix_resb_kernel(
@@ -57,74 +56,107 @@ def tile_list_modp_relu2_mix_resb_kernel(
         keep = ctx.enter_context(tc.tile_pool(name="keep", bufs=1))
         ring = ctx.enter_context(tc.tile_pool(name="ring", bufs=2))
         early = ctx.enter_context(tc.tile_pool(name="early", bufs=1))
-        mid = ctx.enter_context(tc.tile_pool(name="mid", bufs=1))
-        late = ctx.enter_context(tc.tile_pool(name="late", bufs=1))
-        last = ctx.enter_context(tc.tile_pool(name="last", bufs=1))
-        psum = ctx.enter_context(tc.psum_pool(name="psum", bufs=4))
+        psum = ctx.enter_context(tc.psum_pool(name="psum", bufs=1))
+        places = {}
+
+        def shared(place, shape, dtype, name, offset=0):
+            if place not in places:
+                places[place] = ctx.enter_context(tc.tile_pool(name=place, bufs=1))
+            return places[place].tile(shape, dtype, name=name, align_bytes=ALIGN, offset=offset)
 
         offsets = keep.tile([P, J // 16], U16, name="offsets")
         nc.sync.dma_start(offsets[:], offs)
 
-        def chunk_offsets(c):
-            return offsets[:, c * (CHUNK // 16) : (c + 1) * (CHUNK // 16)]
+        def list_slice(lo, hi):
+            return offsets[:, lo // 16 : hi // 16]
 
         def quad_rows(q, count):
             return slice(32 * q, 32 * q + count)
 
+        tab_sc = early.tile([P, EARLY_BYTES // 4], I32, name="tab_sc", align_bytes=ALIGN, offset=0)[:, 0 : T // 4]
+        for q in range(QUADS):
+            rows = slice(32 * q + FILLER_ROWS, 32 * (q + 1))
+            nc.sync.dma_start(tab_sc[rows, :], tab_scales.bitcast(I32)[:, PACK * q : PACK * (q + 1), :])
         sm_sb = keep.tile([P, R_BLOCKS, PACK], F32, name="sm_sb")
         nc.sync.dma_start(sm_sb[:], sm.rearrange("(b p i) -> p b i", b=R_BLOCKS, i=PACK))
-
-        tab_sc = early.tile([P, EARLY_BYTES // 4], I32, name="tab_sc", align_bytes=ALIGN, offset=0)[:, 0 : T // 4]
-        wu_sc = mid.tile([P, K_PASSES, R // 4], I32, name="wu_sc", align_bytes=ALIGN, offset=0)
-        moved_sc = keep.tile([P, J // 4], I32, name="moved_sc", align_bytes=ALIGN)
-        half = keep.tile([P, R_BLOCKS * PACK], F32, name="half")
-        nc.gpsimd.memset(tab_sc, 0)
-        nc.vector.memset(wu_sc[:], 0)
-        nc.gpsimd.memset(half[:], 0.5)
-        nc.gpsimd.memset(moved_sc[:], 0)
-
-        for q in range(QUADS):
-            nc.sync.dma_start(
-                tab_sc[quad_rows(q, K_PASSES * PACK), :], tab_scales.bitcast(I32)[:, PACK * q : PACK * (q + 1), :]
-            )
-        tab_w = keep.tile([P, T], I32, name="tab_w", align_bytes=ALIGN)
-        nc.sync.dma_start(tab_w[:], tab_words[0].rearrange("p t f -> p (t f)").bitcast(I32))
         wu_view = wu_words.rearrange("a p r i -> p a (r i)").bitcast(I32)
         wu_raw = [keep.tile([P, K_PASSES, PASS], I32, name="wu_raw0", align_bytes=ALIGN)]
         nc.sync.dma_start(wu_raw[0][:], wu_view[:, :, 0:PASS])
+        tab_w = keep.tile([P, T], I32, name="tab_w", align_bytes=ALIGN)
+        nc.sync.dma_start(tab_w[:], tab_words[0].rearrange("p t f -> p (t f)").bitcast(I32))
+
+        wu_sc = shared("words", [P, K_PASSES, R // 4], I32, "wu_sc", offset=CHUNK_BYTES)
+        tab_planes = keep.tile([P, K_PASSES, J // 4], I32, name="tab_planes", align_bytes=ALIGN)
+        half = keep.tile([P, R_BLOCKS * PACK], F32, name="half")
+        windows = {3: keep.tile([P, T], F32, name="window3", align_bytes=ALIGN)}
+        nc.vector.memset(wu_sc[:], 0)
+        for q in range(QUADS):
+            nc.vector.memset(tab_sc[quad_rows(q, FILLER_ROWS), :], 0)
+        nc.vector.memset(tab_planes[96:128], 0)
+        nc.vector.memset(windows[3][:], 0.0)
+        nc.gpsimd.memset(half[:], 0.5)
         wu_sc_view = wu_scales.bitcast(I32).rearrange("a q r -> q a r")
         for q in range(QUADS):
             nc.sync.dma_start(wu_sc[quad_rows(q, PACK), :, :], wu_sc_view[PACK * q : PACK * (q + 1), :, :])
+        wu_raw.append(keep.tile([P, K_PASSES, PASS], I32, name="wu_raw1", align_bytes=ALIGN))
+        nc.sync.dma_start(wu_raw[1][:], wu_view[:, :, PASS : 2 * PASS])
 
         sm_flat = sm_sb[:].rearrange("p b i -> p (b i)")
         magnitude = keep.tile([P, R_BLOCKS * PACK], F32, name="magnitude")
         root = keep.tile([P, R_BLOCKS * PACK], F32, name="root")
         sign = keep.tile([P, R_BLOCKS * PACK], F32, name="sign")
-        sign_wide = keep.tile([P, R_BLOCKS, CHUNK * PACK], BF16, name="sign_wide", align_bytes=ALIGN)
+        sign_wide = keep.tile([P, R_BLOCKS, SIGN_TOKENS * PACK], BF16, name="sign_wide", align_bytes=ALIGN)
         nc.scalar.activation(magnitude[:], sm_flat, ACT.Abs)
         nc.scalar.activation(sign[:], sm_flat, ACT.Sign)
         for rb in range(R_BLOCKS):
             nc.scalar.activation(
                 sign_wide[:, rb, :].rearrange("p (j i) -> p j i", i=PACK),
-                sm_sb[:, rb, :].unsqueeze(1).to_broadcast([P, CHUNK, PACK]),
+                sm_sb[:, rb, :].unsqueeze(1).to_broadcast([P, SIGN_TOKENS, PACK]),
                 ACT.Sign,
             )
         nc.gpsimd.tensor_tensor(root[:], magnitude[:], half[:], ALU.pow)
 
         picked_sc = keep.tile([P, J], U8, name="picked_sc", align_bytes=ALIGN)
         nc.vector.tensor_copy(picked_sc[:], tab_sc.bitcast(U8).indirect(offsets[:]))
-        nc.sync.dma_start(moved_sc[0:MOVED_ROWS, :], picked_sc[:].bitcast(I32)[PACK : PACK + MOVED_ROWS, :])
-        tab_planes = (picked_sc[:], moved_sc[:].bitcast(U8))
+        for a, queue in enumerate((nc.sync, nc.scalar)):
+            row = FILLER_ROWS + PACK * a
+            queue.dma_start(tab_planes[0:MOVED_ROWS, a, :], picked_sc[:].bitcast(I32)[row : row + MOVED_ROWS, :])
+        tab_plane_bytes = tab_planes[:].rearrange("p a j -> p (a j)").bitcast(U8)
 
-        wu_raw.append(early.tile([P, K_PASSES, PASS], I32, name="wu_raw1", align_bytes=ALIGN, offset=EARLY_WU))
-        nc.sync.dma_start(wu_raw[1][:], wu_view[:, :, PASS : 2 * PASS])
-        r_sb = [early.tile([P, T], F32, name="r_sb0", align_bytes=ALIGN, offset=EARLY_R)]
-        nc.sync.dma_start(r_sb[0][:], rT[0:P, :])
+        r_sb = []
+        for t in range(N_TILES):
+            r_sb.append(early.tile([P, T], F32, name=f"r_sb{t}", align_bytes=ALIGN, offset=t * ROW_BYTES))
+        wd8_w = early.tile([P, N], I32, name="wd8_w", align_bytes=ALIGN, offset=EARLY_WD8)
+        wd4_w = early.tile([P, N // 2], I32, name="wd4_w", align_bytes=ALIGN, offset=EARLY_WD4)
+        wd_sc = early.tile([P, R_BLOCKS, N // 4], I32, name="wd_sc", align_bytes=ALIGN, offset=EARLY_WD_SCALES)
+        wgo_sb = early.tile([P, J], F32, name="wgo_sb", align_bytes=ALIGN, offset=EARLY_WGO)
+        b_sb = early.tile([P, N_TILES], F32, name="b_sb", align_bytes=ALIGN, offset=EARLY_B)
+        nc.gpsimd.memset(wd_sc[:], 0)
+
+        def load_residual(t):
+            nc.sync.dma_start(r_sb[t][:], rT[t * P : (t + 1) * P, :])
+
+        def load_wd_scales(rb, scales):
+            for q in range(QUADS):
+                nc.sync.dma_start(
+                    wd_sc[quad_rows(q, PACK), rb, :], scales[0].bitcast(I32)[PACK * q : PACK * (q + 1), :]
+                )
+
+        for t in range(N_TILES - 1):
+            load_residual(t)
+        load_wd_scales(0, wd8_scales)
+        nc.sync.dma_start(wd8_w[:], wd8_words[0].rearrange("p n i -> p (n i)").bitcast(I32))
+        nc.sync.dma_start(wd4_w[:], wd4_words[0].bitcast(I32))
+        load_residual(N_TILES - 1)
+        nc.sync.dma_start(wgo_sb[:], wgo)
+        load_wd_scales(1, wd4_scales)
+        with nc.allow_non_contiguous_dma(reason="one bias value to a partition"):
+            nc.sync.dma_start(b_sb[:], b.rearrange("(t p) -> p t", p=P))
 
         parted, wu_codes, wu_planes = [], [], []
 
         def gather_words(c, picked_w):
-            nc.vector.tensor_copy(picked_w, tab_w[:].bitcast(U32).indirect(chunk_offsets(c)))
+            nc.vector.tensor_copy(picked_w, tab_w[:].bitcast(U32).indirect(list_slice(c * CHUNK, (c + 1) * CHUNK)))
 
         def part_words(c, picked_w):
             words = keep.tile([P, K_PASSES, CHUNK], U16, name=f"parted{c}", align_bytes=ALIGN)
@@ -146,51 +178,19 @@ def tile_list_modp_relu2_mix_resb_kernel(
             nc.vector.tensor_copy(plane[:].rearrange("p a (i m) -> p a i m", i=PACK), loaded[:, rb])
             wu_planes.append(plane)
 
-        picked_w0 = late.tile([P, LATE_BYTES // 4], U32, name="picked_w0", align_bytes=ALIGN, offset=0)[:, 0:CHUNK]
-        gather_words(0, picked_w0)
+        picked_w0 = shared("words", [P, CHUNK], U32, "picked_w0")[:]
         reorder_wu_words(0)
-        part_words(0, picked_w0)
+        gather_words(0, picked_w0)
         reorder_wu_scales(0)
-
-        for t in range(1, N_TILES):
-            r_sb.append(late.tile([P, T], F32, name=f"r_sb{t}", align_bytes=ALIGN, offset=(t - 1) * ROW_BYTES))
-        wd8_w = late.tile([P, N], I32, name="wd8_w", align_bytes=ALIGN, offset=LATE_WD8)
-        wd4_w = late.tile([P, N // 2], I32, name="wd4_w", align_bytes=ALIGN, offset=LATE_WD4)
-        wd_sc = late.tile([P, R_BLOCKS, N // 4], I32, name="wd_sc", align_bytes=ALIGN, offset=LATE_WD_SCALES)
-        wgo_sb = late.tile([P, J], F32, name="wgo_sb", align_bytes=ALIGN, offset=LATE_WGO)
-        b_sb = late.tile([P, N_TILES], F32, name="b_sb", align_bytes=ALIGN, offset=LATE_B)
-        nc.vector.memset(wd_sc[:], 0)
-
-        def load_residual(t):
-            nc.sync.dma_start(r_sb[t][:], rT[t * P : (t + 1) * P, :])
-
-        def load_wd_scales(rb, scales):
-            for q in range(QUADS):
-                nc.sync.dma_start(
-                    wd_sc[quad_rows(q, PACK), rb, :], scales[0].bitcast(I32)[PACK * q : PACK * (q + 1), :]
-                )
-
-        load_residual(1)
-        load_wd_scales(0, wd8_scales)
-        load_residual(2)
-        nc.sync.dma_start(wd8_w[:], wd8_words[0].rearrange("p n i -> p (n i)").bitcast(I32))
-        nc.sync.dma_start(wd4_w[:], wd4_words[0].bitcast(I32))
-        load_residual(3)
-        load_wd_scales(1, wd4_scales)
-        nc.sync.dma_start(wgo_sb[:], wgo)
-        with nc.allow_non_contiguous_dma(reason="one bias value to a partition"):
-            nc.sync.dma_start(b_sb[:], b.rearrange("(t p) -> p t", p=P))
-
+        part_words(0, picked_w0)
         reorder_wu_scales(1)
         reorder_wu_words(1)
-        picked_w1 = mid.tile([P, CHUNK], U32, name="picked_w1", align_bytes=ALIGN, offset=0)[:]
+        picked_w1 = shared("words", [P, 2 * T], U32, "picked_w1")[:, 0:CHUNK]
         gather_words(1, picked_w1)
         part_words(1, picked_w1)
-
-        windows = []
-        for t in range(N_TILES // 2):
-            windows.append(keep.tile([P, T], F32, name=f"window{t}", align_bytes=ALIGN))
-            nc.vector.memset(windows[t][:], 0.0)
+        for t in range(2):
+            windows[t] = shared("words", [P, T], F32, f"window{t}", offset=t * ROW_BYTES)
+            nc.gpsimd.memset(windows[t][:], 0.0)
 
         unsigned, finished, h_codes, h_scales, picked_r = {}, {}, {}, {}, {}
 
@@ -203,14 +203,15 @@ def tile_list_modp_relu2_mix_resb_kernel(
         def hidden(c, rb):
             rooted = ring.tile([P, PACK, CHUNK], F32, name="rooted")
             for i in range(PACK):
-                acc = psum.tile([P, CHUNK], F32, name="acc_a")
+                first_bank = PACK if (c, rb) == (1, 1) else 0
+                acc = psum.tile([P, CHUNK], F32, name=f"acc_a{c}{rb}{i}", offset=(first_bank + i) * CHUNK_BYTES)
                 for a in range(K_PASSES):
                     nc.tensor.matmul_mx(
                         out=acc[:],
                         lhsT=wu_codes[rb][:, a, i * P : (i + 1) * P].bitcast(FP8X4),
                         lhsT_scale=wu_planes[rb][:, a, i * P : (i + 1) * P],
                         rhs=parted[c][:, a, :].bitcast(FP4X4),
-                        rhs_scale=tab_planes[a][:, c * CHUNK : (c + 1) * CHUNK],
+                        rhs_scale=tab_plane_bytes[:, a * J + c * CHUNK : a * J + (c + 1) * CHUNK],
                         start=(a == 0),
                         stop=(a == K_PASSES - 1),
                     )
@@ -218,16 +219,16 @@ def tile_list_modp_relu2_mix_resb_kernel(
                 nc.scalar.activation(rooted[:, i, :], acc[:], ACT.Relu, scale=root[:, col : col + 1])
             split = SIGN_ON_VECTOR[c, rb]
             if split > 0:
-                unsigned[c, rb] = keep.tile([P, split * PACK], BF16, name=f"unsigned{c}{rb}", align_bytes=ALIGN)
-                nc.scalar.activation(interleaved(unsigned[c, rb][:]), by_output(rooted[:, :, 0:split]), ACT.Square)
+                place = f"unsigned{rb}" if c == 0 else "codes"
+                unsigned[c, rb] = shared(place, [P, split * PACK], BF16, f"unsigned{c}{rb}")
+                for lo in range(0, split, HALF):
+                    values = unsigned[c, rb][:, lo * PACK : (lo + HALF) * PACK]
+                    nc.scalar.activation(interleaved(values), by_output(rooted[:, :, lo : lo + HALF]), ACT.Square)
             if split < CHUNK:
                 rest = CHUNK - split
                 squares = keep.tile([P, PACK, rest], F32, name=f"squares{rb}")
                 rounded = keep.tile([P, PACK, rest], BF16, name=f"rounded{rb}")
-                if rb == R_BLOCKS - 1:
-                    finished[c, rb] = last.tile([P, rest * PACK], BF16, name="finished1", align_bytes=ALIGN, offset=LAST_H)
-                else:
-                    finished[c, rb] = keep.tile([P, rest * PACK], BF16, name="finished0", align_bytes=ALIGN)
+                finished[c, rb] = shared("turn", [P, rest * PACK], BF16, f"finished{rb}", offset=2 * CHUNK_BYTES)
                 nc.scalar.activation(squares[:], rooted[:, :, split:CHUNK], ACT.Square)
                 for i in range(PACK):
                     col = rb * PACK + i
@@ -236,105 +237,119 @@ def tile_list_modp_relu2_mix_resb_kernel(
 
         def quantise(c, rb):
             split = SIGN_ON_VECTOR[c, rb]
-            if (c, rb) == (1, 0):
-                codes = last.tile([P, CHUNK], U32, name="h_codes10", align_bytes=ALIGN, offset=LAST_CODES)
+            if (c, rb) == (0, 1):
+                codes = shared("codes", [P, CHUNK], U32, "h_codes01")
             else:
                 codes = keep.tile([P, CHUNK], U32, name=f"h_codes{c}{rb}", align_bytes=ALIGN)
             scales = keep.tile([P, CHUNK], U8, name=f"h_scales{c}{rb}", align_bytes=ALIGN)
             h_codes[c, rb], h_scales[c, rb] = codes, scales
+            spans = [(lo, lo + HALF) for lo in range(0, split, HALF)]
             if split > 0:
-                if c == 0:
-                    signed = late.tile([P, split * PACK], BF16, name=f"signed0{rb}", align_bytes=ALIGN, offset=rb * ROW_BYTES)
-                else:
-                    signed = last.tile([P, split * PACK], BF16, name="signed10", align_bytes=ALIGN, offset=LAST_SIGNED)
-                nc.vector.tensor_tensor(signed[:], unsigned[c, rb][:], sign_wide[:, rb, 0 : split * PACK], ALU.mult)
+                place = f"signed{rb}" if c == 0 else "turn"
+                signed = shared(place, [P, split * PACK], BF16, f"signed{c}{rb}")
+                width = SIGN_TOKENS * PACK
+                for lo, hi in spans:
+                    cols = slice(lo * PACK, hi * PACK)
+                    nc.vector.tensor_tensor(
+                        signed[:, cols].rearrange("p (g x) -> p g x", x=width),
+                        unsigned[c, rb][:, cols].rearrange("p (g x) -> p g x", x=width),
+                        sign_wide[:, rb, :].unsqueeze(1).to_broadcast([P, (hi - lo) // SIGN_TOKENS, width]),
+                        ALU.mult,
+                    )
             if split < CHUNK:
                 nc.vector.quantize_mx(
                     out=codes[:, split:CHUNK].bitcast(FP8X4), scales=scales[:, split:CHUNK], in_=finished[c, rb][:]
                 )
-            if split > 0:
-                nc.vector.quantize_mx(out=codes[:, 0:split].bitcast(FP8X4), scales=scales[:, 0:split], in_=signed[:])
+            for lo, hi in spans:
+                nc.vector.quantize_mx(
+                    out=codes[:, lo:hi].bitcast(FP8X4), scales=scales[:, lo:hi], in_=signed[:, lo * PACK : hi * PACK]
+                )
 
-        def gather_residual(t):
-            both = keep.tile([P, J], F32, name=f"picked_r{t}")
-            nc.vector.tensor_copy(both[:], r_sb[t][:].indirect(offsets[:]))
-            for c in range(CHUNKS):
-                picked_r[c, t] = both[:, c * CHUNK : (c + 1) * CHUNK]
+        def gather_residual(t, into):
+            nc.vector.tensor_copy(into[:], r_sb[t][:].indirect(offsets[:]))
+            picked_r[t] = into
 
-        picked_r[0, 0] = last.tile([P, LAST_H // 4], F32, name="picked_r00", align_bytes=ALIGN, offset=0)[:, 0:CHUNK]
-        picked_r[1, 0] = keep.tile([P, CHUNK], F32, name="picked_r10")[:]
-        for c in range(CHUNKS):
-            nc.vector.tensor_copy(picked_r[c, 0], r_sb[0][:].indirect(chunk_offsets(c)))
+        for t in range(2):
+            gather_residual(t, keep.tile([P, J], F32, name=f"picked_r{t}"))
         for rb in range(R_BLOCKS):
             hidden(0, rb)
-            gather_residual(rb + 1)
             quantise(0, rb)
-        gather_residual(N_TILES - 1)
-        for rb in range(R_BLOCKS):
-            hidden(1, rb)
+            gather_residual(2 + rb, shared(f"unsigned{rb}", [P, J], F32, f"picked_r{2 + rb}"))
+            if rb == 0:
+                windows[2] = shared("signed0", [P, T], F32, "window2")
+                nc.gpsimd.memset(windows[2][:], 0.0)
 
         wd_planes = wd_sc[:].rearrange("p b n -> p (b n)").bitcast(U8)
-        steps = [(c, t) for c in range(CHUNKS) for t in range(N_TILES)]
         first_step, turn_step = (0, 0), (0, N_TILES - 1)
-        summed = {}
+        summed, weighed = {}, {}
+
+        def pieces(c, t):
+            return [(0, HALF), (HALF, CHUNK)] if t < HALVED_STEPS or (c, t) == turn_step else [(0, CHUNK)]
+
+        wd_codes = (
+            lambda t: wd8_w[:, t * P : (t + 1) * P].bitcast(FP8X4),
+            lambda t: wd4_w[:, t * P // 2 : (t + 1) * P // 2].bitcast(FP4X4),
+        )
+
+        def second_layer(c, t, acc, lo, hi):
+            blocks = (1, 0) if c > 0 and t > 0 else (0, 1)
+            for rb in blocks:
+                nc.tensor.matmul_mx(
+                    out=acc[:, lo:hi],
+                    lhsT=wd_codes[rb](t),
+                    lhsT_scale=wd_planes[:, rb * N + t * P : rb * N + (t + 1) * P],
+                    rhs=h_codes[c, rb][:, lo:hi].bitcast(FP8X4),
+                    rhs_scale=h_scales[c, rb][:, lo:hi],
+                    start=(rb == blocks[0]),
+                    stop=(rb == blocks[1]),
+                )
 
         def add_up(c, t):
-            acc = psum.tile([P, CHUNK], F32, name="acc_y")
-            nc.tensor.matmul_mx(
-                out=acc[:],
-                lhsT=wd8_w[:, t * P : (t + 1) * P].bitcast(FP8X4),
-                lhsT_scale=wd_planes[:, t * P : (t + 1) * P],
-                rhs=h_codes[c, 0][:].bitcast(FP8X4),
-                rhs_scale=h_scales[c, 0][:],
-                start=True,
-                stop=False,
-            )
-            nc.tensor.matmul_mx(
-                out=acc[:],
-                lhsT=wd4_w[:, t * P // 2 : (t + 1) * P // 2].bitcast(FP4X4),
-                lhsT_scale=wd_planes[:, N + t * P : N + (t + 1) * P],
-                rhs=h_codes[c, 1][:].bitcast(FP8X4),
-                rhs_scale=h_scales[c, 1][:],
-                start=False,
-                stop=True,
-            )
-            residual = picked_r[c, t]
-            weight = wgo_sb[:, c * CHUNK : (c + 1) * CHUNK]
-            if (c, t) == first_step:
-                total = last.tile([P, CHUNK], F32, name="first_sum", align_bytes=ALIGN, offset=LAST_FIRST_SUM)[:]
-            elif (c, t) == turn_step:
-                total = last.tile([P, CHUNK], F32, name="turn_sum", align_bytes=ALIGN, offset=LAST_H)[:]
+            acc = psum.tile([P, CHUNK], F32, name=f"acc_y{c}{t}", offset=((1 - c) * PACK + t) * CHUNK_BYTES)
+            if (c, t) != first_step:
+                second_layer(c, t, acc, 0, CHUNK)
+            if (c, t) == (0, N_TILES - 2):
+                total = shared("turn", [P, CHUNK], F32, "total02")
             else:
-                total = residual
-            summed[c, t] = total
-            if c == 0:
-                nc.vector.scalar_tensor_tensor(total, acc[:], b_sb[:, t : t + 1], residual, ALU.add, ALU.add)
-            else:
-                biased = ring.tile([P, CHUNK], F32, name="biased")
-                nc.scalar.activation(biased[:], acc[:], ACT.Identity, bias=b_sb[:, t : t + 1])
-                nc.gpsimd.tensor_tensor(total, residual, biased[:], ALU.add)
-                nc.gpsimd.tensor_tensor(total, total, weight, ALU.mult)
-            if (c, t) == turn_step:
-                nc.vector.tensor_tensor(total, total, weight, ALU.mult)
-            if (c, t) == first_step:
-                for w in range(N_TILES // 2, N_TILES):
-                    at = (w - N_TILES // 2) * ROW_BYTES
-                    windows.append(last.tile([P, T], F32, name=f"window{w}", align_bytes=ALIGN, offset=at))
-                    nc.gpsimd.memset(windows[w][:], 0.0)
+                total = keep.tile([P, CHUNK], F32, name=f"total{c}{t}")
+            for lo, hi in pieces(c, t):
+                if (c, t) == first_step:
+                    if lo > 0:
+                        acc = psum.tile([P, CHUNK], F32, name="acc_second_half", offset=(2 * PACK - 1) * CHUNK_BYTES)
+                    for group in range(lo, hi, P):
+                        second_layer(c, t, acc, group, group + P)
+                tokens = slice(c * CHUNK + lo, c * CHUNK + hi)
+                nc.scalar.activation(total[:, lo:hi], acc[:, lo:hi], ACT.Identity, bias=b_sb[:, t : t + 1])
+                nc.gpsimd.tensor_tensor(total[:, lo:hi], total[:, lo:hi], picked_r[t][:, tokens], ALU.add)
+                if (c, t) == turn_step:
+                    summed[lo] = total[:, lo:hi]
+                else:
+                    nc.gpsimd.tensor_tensor(total[:, lo:hi], total[:, lo:hi], wgo_sb[:, tokens], ALU.mult)
+                    weighed[c, t, lo] = total[:, lo:hi]
+
+        def weigh_turn():
+            c, t = turn_step
+            for lo, engine, at in ((0, nc.vector, 2 * CHUNK_BYTES - HALF * 2), (HALF, nc.gpsimd, 0)):
+                weighed[c, t, lo] = shared("turn", [P, HALF], F32, f"turn_sum{lo}", offset=at)[:]
+                engine.tensor_tensor(weighed[c, t, lo], summed[lo], wgo_sb[:, lo : lo + HALF], ALU.mult)
 
         def scatter(c, t):
-            places = windows[t][:].indirect(chunk_offsets(c))
-            if (c, t) < turn_step:
-                nc.vector.tensor_tensor(places, summed[c, t], wgo_sb[:, c * CHUNK : (c + 1) * CHUNK], ALU.mult)
-            else:
-                nc.vector.tensor_copy(places, summed[c, t])
+            for lo, hi in pieces(c, t):
+                nc.vector.tensor_copy(windows[t][:].indirect(list_slice(c * CHUNK + lo, c * CHUNK + hi)), weighed[c, t, lo])
             if c == CHUNKS - 1:
                 nc.sync.dma_start(out[t * P : (t + 1) * P, :], windows[t][:])
 
-        add_up(*steps[0])
-        for s in range(len(steps)):
-            if 1 <= s <= R_BLOCKS:
-                quantise(1, s - 1)
-            if s + 1 < len(steps):
-                add_up(*steps[s + 1])
-            scatter(*steps[s])
+        for t in range(N_TILES):
+            add_up(0, t)
+        for rb in range(R_BLOCKS):
+            hidden(1, rb)
+        for t in range(N_TILES - 1):
+            scatter(0, t)
+        for rb in range(R_BLOCKS):
+            quantise(1, rb)
+        weigh_turn()
+        scatter(*turn_step)
+        for t in range(N_TILES):
+            add_up(1, t)
+        for t in range(N_TILES):
+            scatter(1, t)

@@ -35,7 +35,7 @@ FILLER_ROWS = 32 - K_PASSES * PACK
 MOVED_ROWS = 32 * (QUADS - 1) + PACK
 
 SIGN_ON_VECTOR = {(0, 0): CHUNK, (0, 1): CHUNK, (1, 0): CHUNK, (1, 1): 0}
-HALVED_STEPS = 2
+HALVED_STEPS = 1
 
 ROW_BYTES = T * 4
 CHUNK_BYTES = CHUNK * 4
@@ -77,33 +77,30 @@ def tile_list_modp_relu2_mix_resb_kernel(
         for q in range(QUADS):
             rows = slice(32 * q + FILLER_ROWS, 32 * (q + 1))
             nc.sync.dma_start(tab_sc[rows, :], tab_scales.bitcast(I32)[:, PACK * q : PACK * (q + 1), :])
-        sm_sb = keep.tile([P, R_BLOCKS, PACK], F32, name="sm_sb")
+        sm_sb = shared("sm", [P, R_BLOCKS, PACK], F32, "sm_sb")
         nc.sync.dma_start(sm_sb[:], sm.rearrange("(b p i) -> p b i", b=R_BLOCKS, i=PACK))
         wu_view = wu_words.rearrange("a p r i -> p a (r i)").bitcast(I32)
-        wu_raw = [keep.tile([P, K_PASSES, PASS], I32, name="wu_raw0", align_bytes=ALIGN)]
+        wu_raw = [shared("wu0", [P, K_PASSES, PASS], I32, "wu_raw0")]
         nc.sync.dma_start(wu_raw[0][:], wu_view[:, :, 0:PASS])
         tab_w = keep.tile([P, T], I32, name="tab_w", align_bytes=ALIGN)
         nc.sync.dma_start(tab_w[:], tab_words[0].rearrange("p t f -> p (t f)").bitcast(I32))
 
         wu_sc = shared("words", [P, K_PASSES, R // 4], I32, "wu_sc", offset=CHUNK_BYTES)
         tab_planes = keep.tile([P, K_PASSES, J // 4], I32, name="tab_planes", align_bytes=ALIGN)
-        half = keep.tile([P, R_BLOCKS * PACK], F32, name="half")
-        windows = {3: keep.tile([P, T], F32, name="window3", align_bytes=ALIGN)}
-        nc.vector.memset(wu_sc[:], 0)
+        half = keep.tile([P, PACK], F32, name="half")
+        nc.gpsimd.memset(wu_sc[:], 0)
         for q in range(QUADS):
             nc.vector.memset(tab_sc[quad_rows(q, FILLER_ROWS), :], 0)
-        nc.vector.memset(tab_planes[96:128], 0)
-        nc.vector.memset(windows[3][:], 0.0)
+        nc.gpsimd.memset(tab_planes[96:128], 0)
         nc.gpsimd.memset(half[:], 0.5)
         wu_sc_view = wu_scales.bitcast(I32).rearrange("a q r -> q a r")
         for q in range(QUADS):
             nc.sync.dma_start(wu_sc[quad_rows(q, PACK), :, :], wu_sc_view[PACK * q : PACK * (q + 1), :, :])
-        wu_raw.append(keep.tile([P, K_PASSES, PASS], I32, name="wu_raw1", align_bytes=ALIGN))
+        wu_raw.append(shared("wu1", [P, K_PASSES, PASS], I32, "wu_raw1"))
         nc.sync.dma_start(wu_raw[1][:], wu_view[:, :, PASS : 2 * PASS])
 
         sm_flat = sm_sb[:].rearrange("p b i -> p (b i)")
         magnitude = keep.tile([P, R_BLOCKS * PACK], F32, name="magnitude")
-        root = keep.tile([P, R_BLOCKS * PACK], F32, name="root")
         sign = keep.tile([P, R_BLOCKS * PACK], F32, name="sign")
         sign_wide = keep.tile([P, R_BLOCKS, SIGN_TOKENS * PACK], BF16, name="sign_wide", align_bytes=ALIGN)
         nc.scalar.activation(magnitude[:], sm_flat, ACT.Abs)
@@ -111,10 +108,11 @@ def tile_list_modp_relu2_mix_resb_kernel(
         for rb in range(R_BLOCKS):
             nc.scalar.activation(
                 sign_wide[:, rb, :].rearrange("p (j i) -> p j i", i=PACK),
-                sm_sb[:, rb, :].unsqueeze(1).to_broadcast([P, SIGN_TOKENS, PACK]),
-                ACT.Sign,
+                sign[:, rb * PACK : (rb + 1) * PACK].unsqueeze(1).to_broadcast([P, SIGN_TOKENS, PACK]),
+                ACT.Copy,
             )
-        nc.gpsimd.tensor_tensor(root[:], magnitude[:], half[:], ALU.pow)
+        windows = {3: shared("sm", [P, T], F32, "window3")}
+        nc.gpsimd.memset(windows[3][:], 0.0)
 
         picked_sc = keep.tile([P, J], U8, name="picked_sc", align_bytes=ALIGN)
         nc.vector.tensor_copy(picked_sc[:], tab_sc.bitcast(U8).indirect(offsets[:]))
@@ -131,7 +129,7 @@ def tile_list_modp_relu2_mix_resb_kernel(
         wd_sc = early.tile([P, R_BLOCKS, N // 4], I32, name="wd_sc", align_bytes=ALIGN, offset=EARLY_WD_SCALES)
         wgo_sb = early.tile([P, J], F32, name="wgo_sb", align_bytes=ALIGN, offset=EARLY_WGO)
         b_sb = early.tile([P, N_TILES], F32, name="b_sb", align_bytes=ALIGN, offset=EARLY_B)
-        nc.gpsimd.memset(wd_sc[:], 0)
+        nc.vector.memset(wd_sc[:], 0)
 
         def load_residual(t):
             nc.sync.dma_start(r_sb[t][:], rT[t * P : (t + 1) * P, :])
@@ -153,7 +151,7 @@ def tile_list_modp_relu2_mix_resb_kernel(
         with nc.allow_non_contiguous_dma(reason="one bias value to a partition"):
             nc.sync.dma_start(b_sb[:], b.rearrange("(t p) -> p t", p=P))
 
-        parted, wu_codes, wu_planes = [], [], []
+        parted, wu_codes, wu_planes, roots = [], [], [], []
 
         def gather_words(c, picked_w):
             nc.vector.tensor_copy(picked_w, tab_w[:].bitcast(U32).indirect(list_slice(c * CHUNK, (c + 1) * CHUNK)))
@@ -170,6 +168,9 @@ def tile_list_modp_relu2_mix_resb_kernel(
                 wu_raw[rb][:].rearrange("p a (m i) -> p a m i", i=PACK),
             )
             wu_codes.append(words)
+            roots.append(shared(f"wu{rb}", [P, PACK], F32, f"root{rb}"))
+            cols = slice(rb * PACK, (rb + 1) * PACK)
+            nc.gpsimd.tensor_tensor(roots[rb][:], magnitude[:, cols], half[:], ALU.pow)
 
         def reorder_wu_scales(rb):
             plane = keep.tile([P, K_PASSES, PASS], U8, name=f"wu_plane{rb}", align_bytes=ALIGN)
@@ -215,11 +216,10 @@ def tile_list_modp_relu2_mix_resb_kernel(
                         start=(a == 0),
                         stop=(a == K_PASSES - 1),
                     )
-                col = rb * PACK + i
-                nc.scalar.activation(rooted[:, i, :], acc[:], ACT.Relu, scale=root[:, col : col + 1])
+                nc.scalar.activation(rooted[:, i, :], acc[:], ACT.Relu, scale=roots[rb][:, i : i + 1])
             split = SIGN_ON_VECTOR[c, rb]
             if split > 0:
-                place = f"unsigned{rb}" if c == 0 else "codes"
+                place = f"unsigned{rb}" if c == 0 else "codes1"
                 unsigned[c, rb] = shared(place, [P, split * PACK], BF16, f"unsigned{c}{rb}")
                 for lo in range(0, split, HALF):
                     values = unsigned[c, rb][:, lo * PACK : (lo + HALF) * PACK]
@@ -233,54 +233,63 @@ def tile_list_modp_relu2_mix_resb_kernel(
                 for i in range(PACK):
                     col = rb * PACK + i
                     nc.scalar.activation(rounded[:, i, :], squares[:, i, :], ACT.Copy, scale=sign[:, col : col + 1])
-                nc.scalar.copy(interleaved(finished[c, rb][:]), by_output(rounded[:]))
+                for lo in (0, HALF):
+                    values = finished[c, rb][:, lo * PACK : (lo + HALF) * PACK]
+                    nc.scalar.copy(interleaved(values), by_output(rounded[:, :, lo : lo + HALF]))
 
-        def quantise(c, rb):
-            split = SIGN_ON_VECTOR[c, rb]
+        signed = {}
+
+        def code_tiles(c, rb):
             if (c, rb) == (0, 1):
-                codes = shared("codes", [P, CHUNK], U32, "h_codes01")
+                codes = shared("codes1", [P, CHUNK], U32, "h_codes01")
             else:
                 codes = keep.tile([P, CHUNK], U32, name=f"h_codes{c}{rb}", align_bytes=ALIGN)
-            scales = keep.tile([P, CHUNK], U8, name=f"h_scales{c}{rb}", align_bytes=ALIGN)
-            h_codes[c, rb], h_scales[c, rb] = codes, scales
-            spans = [(lo, lo + HALF) for lo in range(0, split, HALF)]
-            if split > 0:
+            h_codes[c, rb] = codes
+            h_scales[c, rb] = keep.tile([P, CHUNK], U8, name=f"h_scales{c}{rb}", align_bytes=ALIGN)
+            if (c, rb) in unsigned:
                 place = f"signed{rb}" if c == 0 else "turn"
-                signed = shared(place, [P, split * PACK], BF16, f"signed{c}{rb}")
-                width = SIGN_TOKENS * PACK
-                for lo, hi in spans:
-                    cols = slice(lo * PACK, hi * PACK)
-                    nc.vector.tensor_tensor(
-                        signed[:, cols].rearrange("p (g x) -> p g x", x=width),
-                        unsigned[c, rb][:, cols].rearrange("p (g x) -> p g x", x=width),
-                        sign_wide[:, rb, :].unsqueeze(1).to_broadcast([P, (hi - lo) // SIGN_TOKENS, width]),
-                        ALU.mult,
-                    )
-            if split < CHUNK:
-                nc.vector.quantize_mx(
-                    out=codes[:, split:CHUNK].bitcast(FP8X4), scales=scales[:, split:CHUNK], in_=finished[c, rb][:]
-                )
-            for lo, hi in spans:
-                nc.vector.quantize_mx(
-                    out=codes[:, lo:hi].bitcast(FP8X4), scales=scales[:, lo:hi], in_=signed[:, lo * PACK : hi * PACK]
-                )
+                signed[c, rb] = shared(place, [P, CHUNK * PACK], BF16, f"signed{c}{rb}")
 
-        def gather_residual(t, into):
-            nc.vector.tensor_copy(into[:], r_sb[t][:].indirect(offsets[:]))
-            picked_r[t] = into
+        def apply_sign(c, rb, lo):
+            width = SIGN_TOKENS * PACK
+            cols = slice(lo * PACK, (lo + HALF) * PACK)
+            nc.vector.tensor_tensor(
+                signed[c, rb][:, cols].rearrange("p (g x) -> p g x", x=width),
+                unsigned[c, rb][:, cols].rearrange("p (g x) -> p g x", x=width),
+                sign_wide[:, rb, :].unsqueeze(1).to_broadcast([P, HALF // SIGN_TOKENS, width]),
+                ALU.mult,
+            )
+
+        def quantise(c, rb, lo):
+            values = signed[c, rb] if (c, rb) in signed else finished[c, rb]
+            nc.vector.quantize_mx(
+                out=h_codes[c, rb][:, lo : lo + HALF].bitcast(FP8X4),
+                scales=h_scales[c, rb][:, lo : lo + HALF],
+                in_=values[:, lo * PACK : (lo + HALF) * PACK],
+            )
+
+        def gather_residual(t, lo, hi, into):
+            nc.vector.tensor_copy(into[:], r_sb[t][:].indirect(list_slice(lo, hi)))
+            for c in range(lo // CHUNK, hi // CHUNK):
+                picked_r[c, t] = into[:, c * CHUNK - lo : (c + 1) * CHUNK - lo]
 
         for t in range(2):
-            gather_residual(t, keep.tile([P, J], F32, name=f"picked_r{t}"))
+            gather_residual(t, 0, J, keep.tile([P, J], F32, name=f"picked_r{t}"))
         for rb in range(R_BLOCKS):
             hidden(0, rb)
-            quantise(0, rb)
-            gather_residual(2 + rb, shared(f"unsigned{rb}", [P, J], F32, f"picked_r{2 + rb}"))
+            code_tiles(0, rb)
+            for lo in (0, HALF):
+                apply_sign(0, rb, lo)
+            for lo in (0, HALF):
+                quantise(0, rb, lo)
+            gather_residual(2, rb * CHUNK, (rb + 1) * CHUNK, shared(f"unsigned{rb}", [P, CHUNK], F32, f"picked_r2{rb}"))
             if rb == 0:
                 windows[2] = shared("signed0", [P, T], F32, "window2")
                 nc.gpsimd.memset(windows[2][:], 0.0)
+        gather_residual(3, 0, J, shared("signed1", [P, J], F32, "picked_r3"))
 
         wd_planes = wd_sc[:].rearrange("p b n -> p (b n)").bitcast(U8)
-        first_step, turn_step = (0, 0), (0, N_TILES - 1)
+        turn_step = (0, N_TILES - 1)
         summed, weighed = {}, {}
 
         def pieces(c, t):
@@ -306,21 +315,21 @@ def tile_list_modp_relu2_mix_resb_kernel(
 
         def add_up(c, t):
             acc = psum.tile([P, CHUNK], F32, name=f"acc_y{c}{t}", offset=((1 - c) * PACK + t) * CHUNK_BYTES)
-            if (c, t) != first_step:
+            if t > 0:
                 second_layer(c, t, acc, 0, CHUNK)
             if (c, t) == (0, N_TILES - 2):
                 total = shared("turn", [P, CHUNK], F32, "total02")
             else:
                 total = keep.tile([P, CHUNK], F32, name=f"total{c}{t}")
             for lo, hi in pieces(c, t):
-                if (c, t) == first_step:
+                if t == 0:
                     if lo > 0:
-                        acc = psum.tile([P, CHUNK], F32, name="acc_second_half", offset=(2 * PACK - 1) * CHUNK_BYTES)
+                        acc = psum.tile([P, CHUNK], F32, name=f"acc_second_half{c}", offset=((2 - c) * PACK - 1) * CHUNK_BYTES)
                     for group in range(lo, hi, P):
                         second_layer(c, t, acc, group, group + P)
                 tokens = slice(c * CHUNK + lo, c * CHUNK + hi)
                 nc.scalar.activation(total[:, lo:hi], acc[:, lo:hi], ACT.Identity, bias=b_sb[:, t : t + 1])
-                nc.gpsimd.tensor_tensor(total[:, lo:hi], total[:, lo:hi], picked_r[t][:, tokens], ALU.add)
+                nc.gpsimd.tensor_tensor(total[:, lo:hi], total[:, lo:hi], picked_r[c, t][:, lo:hi], ALU.add)
                 if (c, t) == turn_step:
                     summed[lo] = total[:, lo:hi]
                 else:
@@ -346,7 +355,12 @@ def tile_list_modp_relu2_mix_resb_kernel(
         for t in range(N_TILES - 1):
             scatter(0, t)
         for rb in range(R_BLOCKS):
-            quantise(1, rb)
+            code_tiles(1, rb)
+        for lo in (0, HALF):
+            apply_sign(1, 0, lo)
+        for rb in range(R_BLOCKS):
+            for lo in (0, HALF):
+                quantise(1, rb, lo)
         weigh_turn()
         scatter(*turn_step)
         for t in range(N_TILES):

@@ -116,9 +116,9 @@ def tile_list_modp_relu2_mix_resb_kernel(
 
         picked_sc = keep.tile([P, J], U8, name="picked_sc", align_bytes=ALIGN)
         nc.vector.tensor_copy(picked_sc[:], tab_sc.bitcast(U8).indirect(offsets[:]))
-        for a, queue in enumerate((nc.sync, nc.scalar)):
+        for a in range(K_PASSES):
             row = FILLER_ROWS + PACK * a
-            queue.dma_start(tab_planes[0:MOVED_ROWS, a, :], picked_sc[:].bitcast(I32)[row : row + MOVED_ROWS, :])
+            nc.sync.dma_start(tab_planes[0:MOVED_ROWS, a, :], picked_sc[:].bitcast(I32)[row : row + MOVED_ROWS, :])
         tab_plane_bytes = tab_planes[:].rearrange("p a j -> p (a j)").bitcast(U8)
 
         r_sb = []

@@ -39,10 +39,10 @@ HALVED_STEPS = 1
 
 ROW_BYTES = T * 4
 CHUNK_BYTES = CHUNK * 4
-EARLY_WD8 = N_TILES * ROW_BYTES
+EARLY_RESIDUAL = K_PASSES * J
+EARLY_WD8 = EARLY_RESIDUAL + N_TILES * ROW_BYTES
 EARLY_WD4 = EARLY_WD8 + N * 4
-EARLY_WD_SCALES = EARLY_WD4 + N * 2
-EARLY_WGO = EARLY_WD_SCALES + R_BLOCKS * N
+EARLY_WGO = EARLY_WD4 + N * 2
 EARLY_B = EARLY_WGO + J * 4
 EARLY_BYTES = EARLY_B + ALIGN
 
@@ -66,6 +66,8 @@ def tile_list_modp_relu2_mix_resb_kernel(
 
         offsets = keep.tile([P, J // 16], U16, name="offsets")
         nc.sync.dma_start(offsets[:], offs)
+        sm_sb = shared("sm", [P, R_BLOCKS, PACK], F32, "sm_sb")
+        nc.sync.dma_start(sm_sb[:], sm.rearrange("(b p i) -> p b i", b=R_BLOCKS, i=PACK))
 
         def list_slice(lo, hi):
             return offsets[:, lo // 16 : hi // 16]
@@ -77,22 +79,16 @@ def tile_list_modp_relu2_mix_resb_kernel(
         for q in range(QUADS):
             rows = slice(32 * q + FILLER_ROWS, 32 * (q + 1))
             nc.sync.dma_start(tab_sc[rows, :], tab_scales.bitcast(I32)[:, PACK * q : PACK * (q + 1), :])
-        sm_sb = shared("sm", [P, R_BLOCKS, PACK], F32, "sm_sb")
-        nc.sync.dma_start(sm_sb[:], sm.rearrange("(b p i) -> p b i", b=R_BLOCKS, i=PACK))
         wu_view = wu_words.rearrange("a p r i -> p a (r i)").bitcast(I32)
-        wu_raw = [shared("wu0", [P, K_PASSES, PASS], I32, "wu_raw0")]
-        nc.sync.dma_start(wu_raw[0][:], wu_view[:, :, 0:PASS])
         tab_w = keep.tile([P, T], I32, name="tab_w", align_bytes=ALIGN)
         nc.sync.dma_start(tab_w[:], tab_words[0].rearrange("p t f -> p (t f)").bitcast(I32))
+        wu_raw = [shared("wu0", [P, K_PASSES, PASS], I32, "wu_raw0")]
+        nc.sync.dma_start(wu_raw[0][:], wu_view[:, :, 0:PASS])
 
         wu_sc = shared("words", [P, K_PASSES, R // 4], I32, "wu_sc", offset=CHUNK_BYTES)
-        tab_planes = keep.tile([P, K_PASSES, J // 4], I32, name="tab_planes", align_bytes=ALIGN)
-        half = keep.tile([P, PACK], F32, name="half")
         nc.gpsimd.memset(wu_sc[:], 0)
         for q in range(QUADS):
             nc.vector.memset(tab_sc[quad_rows(q, FILLER_ROWS), :], 0)
-        nc.gpsimd.memset(tab_planes[96:128], 0)
-        nc.gpsimd.memset(half[:], 0.5)
         wu_sc_view = wu_scales.bitcast(I32).rearrange("a q r -> q a r")
         for q in range(QUADS):
             nc.sync.dma_start(wu_sc[quad_rows(q, PACK), :, :], wu_sc_view[PACK * q : PACK * (q + 1), :, :])
@@ -105,6 +101,8 @@ def tile_list_modp_relu2_mix_resb_kernel(
         sign_wide = keep.tile([P, R_BLOCKS, SIGN_TOKENS * PACK], BF16, name="sign_wide", align_bytes=ALIGN)
         nc.scalar.activation(magnitude[:], sm_flat, ACT.Abs)
         nc.scalar.activation(sign[:], sm_flat, ACT.Sign)
+        root = keep.tile([P, R_BLOCKS * PACK], F32, name="root")
+        nc.scalar.activation(root[:], magnitude[:], ACT.Sqrt)
         for rb in range(R_BLOCKS):
             nc.scalar.activation(
                 sign_wide[:, rb, :].rearrange("p (j i) -> p j i", i=PACK),
@@ -114,7 +112,8 @@ def tile_list_modp_relu2_mix_resb_kernel(
         windows = {3: shared("sm", [P, T], F32, "window3")}
         nc.gpsimd.memset(windows[3][:], 0.0)
 
-        picked_sc = keep.tile([P, J], U8, name="picked_sc", align_bytes=ALIGN)
+        picked_sc = shared("picked_sc", [P, J], U8, "picked_sc")
+        tab_planes = early.tile([P, K_PASSES, J // 4], I32, name="tab_planes", align_bytes=ALIGN, offset=0)
         nc.vector.tensor_copy(picked_sc[:], tab_sc.bitcast(U8).indirect(offsets[:]))
         for a in range(K_PASSES):
             row = FILLER_ROWS + PACK * a
@@ -123,13 +122,12 @@ def tile_list_modp_relu2_mix_resb_kernel(
 
         r_sb = []
         for t in range(N_TILES):
-            r_sb.append(early.tile([P, T], F32, name=f"r_sb{t}", align_bytes=ALIGN, offset=t * ROW_BYTES))
+            r_sb.append(early.tile([P, T], F32, name=f"r_sb{t}", align_bytes=ALIGN, offset=EARLY_RESIDUAL + t * ROW_BYTES))
         wd8_w = early.tile([P, N], I32, name="wd8_w", align_bytes=ALIGN, offset=EARLY_WD8)
         wd4_w = early.tile([P, N // 2], I32, name="wd4_w", align_bytes=ALIGN, offset=EARLY_WD4)
-        wd_sc = early.tile([P, R_BLOCKS, N // 4], I32, name="wd_sc", align_bytes=ALIGN, offset=EARLY_WD_SCALES)
+        wd_sc = shared("picked_sc", [P, R_BLOCKS, N // 4], I32, "wd_sc")
         wgo_sb = early.tile([P, J], F32, name="wgo_sb", align_bytes=ALIGN, offset=EARLY_WGO)
         b_sb = early.tile([P, N_TILES], F32, name="b_sb", align_bytes=ALIGN, offset=EARLY_B)
-        nc.vector.memset(wd_sc[:], 0)
 
         def load_residual(t):
             nc.sync.dma_start(r_sb[t][:], rT[t * P : (t + 1) * P, :])
@@ -151,7 +149,7 @@ def tile_list_modp_relu2_mix_resb_kernel(
         with nc.allow_non_contiguous_dma(reason="one bias value to a partition"):
             nc.sync.dma_start(b_sb[:], b.rearrange("(t p) -> p t", p=P))
 
-        parted, wu_codes, wu_planes, roots = [], [], [], []
+        parted, wu_codes, wu_planes = [], [], []
 
         def gather_words(c, picked_w):
             nc.vector.tensor_copy(picked_w, tab_w[:].bitcast(U32).indirect(list_slice(c * CHUNK, (c + 1) * CHUNK)))
@@ -168,9 +166,6 @@ def tile_list_modp_relu2_mix_resb_kernel(
                 wu_raw[rb][:].rearrange("p a (m i) -> p a m i", i=PACK),
             )
             wu_codes.append(words)
-            roots.append(shared(f"wu{rb}", [P, PACK], F32, f"root{rb}"))
-            cols = slice(rb * PACK, (rb + 1) * PACK)
-            nc.gpsimd.tensor_tensor(roots[rb][:], magnitude[:, cols], half[:], ALU.pow)
 
         def reorder_wu_scales(rb):
             plane = keep.tile([P, K_PASSES, PASS], U8, name=f"wu_plane{rb}", align_bytes=ALIGN)
@@ -180,10 +175,10 @@ def tile_list_modp_relu2_mix_resb_kernel(
             wu_planes.append(plane)
 
         picked_w0 = shared("words", [P, CHUNK], U32, "picked_w0")[:]
-        reorder_wu_words(0)
         gather_words(0, picked_w0)
-        reorder_wu_scales(0)
+        reorder_wu_words(0)
         part_words(0, picked_w0)
+        reorder_wu_scales(0)
         reorder_wu_scales(1)
         reorder_wu_words(1)
         picked_w1 = shared("words", [P, 2 * T], U32, "picked_w1")[:, 0:CHUNK]
@@ -203,25 +198,30 @@ def tile_list_modp_relu2_mix_resb_kernel(
 
         def hidden(c, rb):
             rooted = ring.tile([P, PACK, CHUNK], F32, name="rooted")
-            for i in range(PACK):
-                first_bank = PACK if (c, rb) == (1, 1) else 0
-                acc = psum.tile([P, CHUNK], F32, name=f"acc_a{c}{rb}{i}", offset=(first_bank + i) * CHUNK_BYTES)
-                for a in range(K_PASSES):
-                    nc.tensor.matmul_mx(
-                        out=acc[:],
-                        lhsT=wu_codes[rb][:, a, i * P : (i + 1) * P].bitcast(FP8X4),
-                        lhsT_scale=wu_planes[rb][:, a, i * P : (i + 1) * P],
-                        rhs=parted[c][:, a, :].bitcast(FP4X4),
-                        rhs_scale=tab_plane_bytes[:, a * J + c * CHUNK : a * J + (c + 1) * CHUNK],
-                        start=(a == 0),
-                        stop=(a == K_PASSES - 1),
-                    )
-                nc.scalar.activation(rooted[:, i, :], acc[:], ACT.Relu, scale=roots[rb][:, i : i + 1])
             split = SIGN_ON_VECTOR[c, rb]
             if split > 0:
                 place = f"unsigned{rb}" if c == 0 else "codes1"
                 unsigned[c, rb] = shared(place, [P, split * PACK], BF16, f"unsigned{c}{rb}")
-                for lo in range(0, split, HALF):
+            halved = (c, rb) == (0, 0)
+            for first, last in ((0, HALF), (HALF, CHUNK)) if halved else ((0, CHUNK),):
+                width = P if halved else CHUNK
+                first_bank = PACK if (c, rb) == (1, 1) or first > 0 else 0
+                for i in range(PACK):
+                    acc = psum.tile([P, CHUNK], F32, name=f"acc_a{c}{rb}{i}{first}", offset=(first_bank + i) * CHUNK_BYTES)
+                    for group in range(first, last, width):
+                        token = c * CHUNK + group
+                        for a in range(K_PASSES):
+                            nc.tensor.matmul_mx(
+                                out=acc[:, group : group + width],
+                                lhsT=wu_codes[rb][:, a, i * P : (i + 1) * P].bitcast(FP8X4),
+                                lhsT_scale=wu_planes[rb][:, a, i * P : (i + 1) * P],
+                                rhs=parted[c][:, a, group : group + width].bitcast(FP4X4),
+                                rhs_scale=tab_plane_bytes[:, a * J + token : a * J + token + width],
+                                start=(a == 0),
+                                stop=(a == K_PASSES - 1),
+                            )
+                    nc.scalar.activation(rooted[:, i, first:last], acc[:, first:last], ACT.Relu, scale=root[:, rb * PACK + i : rb * PACK + i + 1])
+                for lo in range(first, min(last, split), HALF):
                     values = unsigned[c, rb][:, lo * PACK : (lo + HALF) * PACK]
                     nc.scalar.activation(interleaved(values), by_output(rooted[:, :, lo : lo + HALF]), ACT.Square)
             if split < CHUNK:
@@ -247,8 +247,12 @@ def tile_list_modp_relu2_mix_resb_kernel(
             h_codes[c, rb] = codes
             h_scales[c, rb] = keep.tile([P, CHUNK], U8, name=f"h_scales{c}{rb}", align_bytes=ALIGN)
             if (c, rb) in unsigned:
-                place = f"signed{rb}" if c == 0 else "turn"
-                signed[c, rb] = shared(place, [P, CHUNK * PACK], BF16, f"signed{c}{rb}")
+                if (c, rb) == (0, 0):
+                    at = EARLY_RESIDUAL + ROW_BYTES
+                    signed[c, rb] = early.tile([P, CHUNK * PACK], BF16, name="signed00", align_bytes=ALIGN, offset=at)
+                else:
+                    place = f"signed{rb}" if c == 0 else "turn"
+                    signed[c, rb] = shared(place, [P, CHUNK * PACK], BF16, f"signed{c}{rb}")
 
         def apply_sign(c, rb, lo):
             width = SIGN_TOKENS * PACK
@@ -284,7 +288,7 @@ def tile_list_modp_relu2_mix_resb_kernel(
                 quantise(0, rb, lo)
             gather_residual(2, rb * CHUNK, (rb + 1) * CHUNK, shared(f"unsigned{rb}", [P, CHUNK], F32, f"picked_r2{rb}"))
             if rb == 0:
-                windows[2] = shared("signed0", [P, T], F32, "window2")
+                windows[2] = early.tile([P, T], F32, name="window2", align_bytes=ALIGN, offset=EARLY_RESIDUAL + ROW_BYTES)
                 nc.gpsimd.memset(windows[2][:], 0.0)
         gather_residual(3, 0, J, shared("signed1", [P, J], F32, "picked_r3"))
 
@@ -329,16 +333,18 @@ def tile_list_modp_relu2_mix_resb_kernel(
                         second_layer(c, t, acc, group, group + P)
                 tokens = slice(c * CHUNK + lo, c * CHUNK + hi)
                 nc.scalar.activation(total[:, lo:hi], acc[:, lo:hi], ACT.Identity, bias=b_sb[:, t : t + 1])
-                nc.gpsimd.tensor_tensor(total[:, lo:hi], total[:, lo:hi], picked_r[c, t][:, lo:hi], ALU.add)
+                at = lo * 4 if (c, t) == turn_step else 0
+                with_residual = shared("sum", [P, hi - lo], F32, f"sum{c}{t}{lo}", offset=at)
+                nc.gpsimd.tensor_tensor(with_residual[:], total[:, lo:hi], picked_r[c, t][:, lo:hi], ALU.add)
                 if (c, t) == turn_step:
-                    summed[lo] = total[:, lo:hi]
+                    summed[lo] = with_residual[:]
                 else:
-                    nc.gpsimd.tensor_tensor(total[:, lo:hi], total[:, lo:hi], wgo_sb[:, tokens], ALU.mult)
+                    nc.gpsimd.tensor_tensor(total[:, lo:hi], with_residual[:], wgo_sb[:, tokens], ALU.mult)
                     weighed[c, t, lo] = total[:, lo:hi]
 
         def weigh_turn():
             c, t = turn_step
-            for lo, engine, at in ((0, nc.vector, 2 * CHUNK_BYTES - HALF * 2), (HALF, nc.gpsimd, 0)):
+            for lo, engine, at in ((0, nc.vector, 2 * CHUNK_BYTES - HALF * 2), (HALF, nc.gpsimd, 2 * CHUNK_BYTES + HALF * 2)):
                 weighed[c, t, lo] = shared("turn", [P, HALF], F32, f"turn_sum{lo}", offset=at)[:]
                 engine.tensor_tensor(weighed[c, t, lo], summed[lo], wgo_sb[:, lo : lo + HALF], ALU.mult)
 

@@ -35,6 +35,7 @@ FILLER_ROWS = 32 - K_PASSES * PACK
 MOVED_ROWS = 32 * (QUADS - 1) + PACK
 
 SIGN_ON_VECTOR = {(0, 0): CHUNK, (0, 1): CHUNK, (1, 0): CHUNK, (1, 1): 0}
+HELD_TOKENS = 16
 HALVED_STEPS = 1
 
 ROW_BYTES = T * 4
@@ -227,7 +228,7 @@ def tile_list_modp_relu2_mix_resb_kernel(
             if split < CHUNK:
                 rest = CHUNK - split
                 squares = keep.tile([P, PACK, rest], F32, name=f"squares{rb}")
-                rounded = keep.tile([P, PACK, rest], BF16, name=f"rounded{rb}")
+                rounded = shared("rounded", [P, PACK, rest], BF16, f"rounded{rb}")
                 finished[c, rb] = shared("turn", [P, rest * PACK], BF16, f"finished{rb}", offset=2 * CHUNK_BYTES)
                 nc.scalar.activation(squares[:], rooted[:, :, split:CHUNK], ACT.Square)
                 for i in range(PACK):
@@ -294,10 +295,10 @@ def tile_list_modp_relu2_mix_resb_kernel(
 
         wd_planes = wd_sc[:].rearrange("p b n -> p (b n)").bitcast(U8)
         turn_step = (0, N_TILES - 1)
-        summed, weighed = {}, {}
+        totals, weighed = {}, {}
 
         def pieces(c, t):
-            return [(0, HALF), (HALF, CHUNK)] if t < HALVED_STEPS or (c, t) == turn_step else [(0, CHUNK)]
+            return [(0, HALF), (HALF, CHUNK)] if t < HALVED_STEPS else [(0, CHUNK)]
 
         wd_codes = (
             lambda t: wd8_w[:, t * P : (t + 1) * P].bitcast(FP8X4),
@@ -331,22 +332,16 @@ def tile_list_modp_relu2_mix_resb_kernel(
                         acc = psum.tile([P, CHUNK], F32, name=f"acc_second_half{c}", offset=((2 - c) * PACK - 1) * CHUNK_BYTES)
                     for group in range(lo, hi, P):
                         second_layer(c, t, acc, group, group + P)
-                tokens = slice(c * CHUNK + lo, c * CHUNK + hi)
                 nc.scalar.activation(total[:, lo:hi], acc[:, lo:hi], ACT.Identity, bias=b_sb[:, t : t + 1])
-                at = lo * 4 if (c, t) == turn_step else 0
-                with_residual = shared("sum", [P, hi - lo], F32, f"sum{c}{t}{lo}", offset=at)
-                nc.gpsimd.tensor_tensor(with_residual[:], total[:, lo:hi], picked_r[c, t][:, lo:hi], ALU.add)
-                if (c, t) == turn_step:
-                    summed[lo] = with_residual[:]
-                else:
-                    nc.gpsimd.tensor_tensor(total[:, lo:hi], with_residual[:], wgo_sb[:, tokens], ALU.mult)
-                    weighed[c, t, lo] = total[:, lo:hi]
+                weighed[c, t, lo] = total[:, lo:hi]
+                totals[c, t] = total
+                add_and_weigh(c, t, lo, hi - HELD_TOKENS if (c, t) == turn_step else hi, "sum")
 
-        def weigh_turn():
-            c, t = turn_step
-            for lo, engine, at in ((0, nc.vector, 2 * CHUNK_BYTES - HALF * 2), (HALF, nc.gpsimd, 2 * CHUNK_BYTES + HALF * 2)):
-                weighed[c, t, lo] = shared("turn", [P, HALF], F32, f"turn_sum{lo}", offset=at)[:]
-                engine.tensor_tensor(weighed[c, t, lo], summed[lo], wgo_sb[:, lo : lo + HALF], ALU.mult)
+        def add_and_weigh(c, t, lo, hi, place):
+            total = totals[c, t]
+            with_residual = shared(place, [P, hi - lo], F32, f"sum{c}{t}{lo}")
+            nc.gpsimd.tensor_tensor(with_residual[:], total[:, lo:hi], picked_r[c, t][:, lo:hi], ALU.add)
+            nc.gpsimd.tensor_tensor(total[:, lo:hi], with_residual[:], wgo_sb[:, c * CHUNK + lo : c * CHUNK + hi], ALU.mult)
 
         def scatter(c, t):
             for lo, hi in pieces(c, t):
@@ -367,7 +362,7 @@ def tile_list_modp_relu2_mix_resb_kernel(
         for rb in range(R_BLOCKS):
             for lo in (0, HALF):
                 quantise(1, rb, lo)
-        weigh_turn()
+        add_and_weigh(*turn_step, CHUNK - HELD_TOKENS, CHUNK, "rounded")
         scatter(*turn_step)
         for t in range(N_TILES):
             add_up(1, t)

@@ -208,7 +208,8 @@ def tile_list_modp_relu2_mix_resb_kernel(
                 width = P if halved else CHUNK
                 first_bank = PACK if (c, rb) == (1, 1) or first > 0 else 0
                 for i in range(PACK):
-                    acc = psum.tile([P, CHUNK], F32, name=f"acc_a{c}{rb}{i}{first}", offset=(first_bank + i) * CHUNK_BYTES)
+                    bank = first_bank + i
+                    acc = psum.tile([P, CHUNK], F32, name=f"acc_a{c}{rb}{i}{first}", offset=bank * CHUNK_BYTES)
                     for group in range(first, last, width):
                         token = c * CHUNK + group
                         for a in range(K_PASSES):
@@ -295,7 +296,8 @@ def tile_list_modp_relu2_mix_resb_kernel(
 
         wd_planes = wd_sc[:].rearrange("p b n -> p (b n)").bitcast(U8)
         turn_step = (0, N_TILES - 1)
-        totals, weighed = {}, {}
+        weighed = {}
+        held = keep.tile([P, HELD_TOKENS], F32, name="held")
 
         def pieces(c, t):
             return [(0, HALF), (HALF, CHUNK)] if t < HALVED_STEPS else [(0, CHUNK)]
@@ -324,6 +326,8 @@ def tile_list_modp_relu2_mix_resb_kernel(
                 second_layer(c, t, acc, 0, CHUNK)
             if (c, t) == (0, N_TILES - 2):
                 total = shared("turn", [P, CHUNK], F32, "total02")
+            elif (c, t) == (1, 0):
+                total = shared("rounded", [P, CHUNK], F32, "total10")
             else:
                 total = keep.tile([P, CHUNK], F32, name=f"total{c}{t}")
             for lo, hi in pieces(c, t):
@@ -334,14 +338,20 @@ def tile_list_modp_relu2_mix_resb_kernel(
                         second_layer(c, t, acc, group, group + P)
                 nc.scalar.activation(total[:, lo:hi], acc[:, lo:hi], ACT.Identity, bias=b_sb[:, t : t + 1])
                 weighed[c, t, lo] = total[:, lo:hi]
-                totals[c, t] = total
-                add_and_weigh(c, t, lo, hi - HELD_TOKENS if (c, t) == turn_step else hi, "sum")
+                with_residual = shared("sum", [P, hi - lo], F32, f"sum{c}{t}{lo}")
+                nc.gpsimd.tensor_tensor(with_residual[:], total[:, lo:hi], picked_r[c, t][:, lo:hi], ALU.add)
+                weights = wgo_sb[:, c * CHUNK + lo : c * CHUNK + hi]
+                if (c, t) == turn_step:
+                    free = CHUNK - HELD_TOKENS
+                    nc.gpsimd.tensor_tensor(total[:, 0:free], with_residual[:, 0:free], weights[:, 0:free], ALU.mult)
+                    nc.gpsimd.tensor_tensor(held[:], with_residual[:, free:CHUNK], weights[:, free:CHUNK], ALU.mult)
+                else:
+                    nc.gpsimd.tensor_tensor(total[:, lo:hi], with_residual[:], weights, ALU.mult)
 
-        def add_and_weigh(c, t, lo, hi, place):
-            total = totals[c, t]
-            with_residual = shared(place, [P, hi - lo], F32, f"sum{c}{t}{lo}")
-            nc.gpsimd.tensor_tensor(with_residual[:], total[:, lo:hi], picked_r[c, t][:, lo:hi], ALU.add)
-            nc.gpsimd.tensor_tensor(total[:, lo:hi], with_residual[:], wgo_sb[:, c * CHUNK + lo : c * CHUNK + hi], ALU.mult)
+        def release_turn():
+            relay = shared("rounded", [P, HELD_TOKENS], F32, "relay")
+            nc.scalar.copy(relay[:], held[:])
+            nc.scalar.copy(weighed[turn_step + (0,)][:, CHUNK - HELD_TOKENS : CHUNK], relay[:])
 
         def scatter(c, t):
             for lo, hi in pieces(c, t):
@@ -362,7 +372,7 @@ def tile_list_modp_relu2_mix_resb_kernel(
         for rb in range(R_BLOCKS):
             for lo in (0, HALF):
                 quantise(1, rb, lo)
-        add_and_weigh(*turn_step, CHUNK - HELD_TOKENS, CHUNK, "rounded")
+        release_turn()
         scatter(*turn_step)
         for t in range(N_TILES):
             add_up(1, t)

@@ -24,19 +24,19 @@ R_BLOCKS = R // PASS
 N_TILES = N // P
 CHUNK = 512
 CHUNKS = J // CHUNK
+HALF = CHUNK // 2
+HALVES = ((0, HALF), (HALF, CHUNK))
+WHOLE = ((0, CHUNK),)
 QUADS = 4
 RUN = 4
 ALIGN = 64
-
-
 SIGN_TOKENS = 128
-HALF = CHUNK // 2
 FILLER_ROWS = 32 - K_PASSES * PACK
 MOVED_ROWS = 32 * (QUADS - 1) + PACK
 
-SIGN_ON_VECTOR = {(0, 0): CHUNK, (0, 1): CHUNK, (1, 0): CHUNK, (1, 1): 0}
-HELD_TOKENS = 16
-HALVED_STEPS = 1
+FIRST_BLOCK = (0, 0)
+SCALAR_SIGNED = (1, 1)
+HELD_STEP = (0, N_TILES - 1)
 
 ROW_BYTES = T * 4
 CHUNK_BYTES = CHUNK * 4
@@ -65,10 +65,14 @@ def tile_list_modp_relu2_mix_resb_kernel(
                 places[place] = ctx.enter_context(tc.tile_pool(name=place, bufs=1))
             return places[place].tile(shape, dtype, name=name, align_bytes=ALIGN, offset=offset)
 
+        def early_tile(shape, dtype, name, offset):
+            return early.tile(shape, dtype, name=name, align_bytes=ALIGN, offset=offset)
+
+        def bank_tile(name, bank):
+            return psum.tile([P, CHUNK], F32, name=name, offset=bank * CHUNK_BYTES)
+
         offsets = keep.tile([P, J // 16], U16, name="offsets")
         nc.sync.dma_start(offsets[:], offs)
-        sm_sb = shared("sm", [P, R_BLOCKS, PACK], F32, "sm_sb")
-        nc.sync.dma_start(sm_sb[:], sm.rearrange("(b p i) -> p b i", b=R_BLOCKS, i=PACK))
 
         def list_slice(lo, hi):
             return offsets[:, lo // 16 : hi // 16]
@@ -76,14 +80,16 @@ def tile_list_modp_relu2_mix_resb_kernel(
         def quad_rows(q, count):
             return slice(32 * q, 32 * q + count)
 
-        tab_sc = early.tile([P, EARLY_BYTES // 4], I32, name="tab_sc", align_bytes=ALIGN, offset=0)[:, 0 : T // 4]
+        tab_sc = early_tile([P, EARLY_BYTES // 4], I32, "tab_sc", 0)[:, 0 : T // 4]
         for q in range(QUADS):
             rows = slice(32 * q + FILLER_ROWS, 32 * (q + 1))
             nc.sync.dma_start(tab_sc[rows, :], tab_scales.bitcast(I32)[:, PACK * q : PACK * (q + 1), :])
+        sm_sb = shared("sm", [P, R_BLOCKS, PACK], F32, "sm_sb")
+        nc.sync.dma_start(sm_sb[:], sm.rearrange("(b p i) -> p b i", b=R_BLOCKS, i=PACK))
         wu_view = wu_words.rearrange("a p r i -> p a (r i)").bitcast(I32)
         tab_w = keep.tile([P, T], I32, name="tab_w", align_bytes=ALIGN)
         nc.sync.dma_start(tab_w[:], tab_words[0].rearrange("p t f -> p (t f)").bitcast(I32))
-        wu_raw = [shared("wu0", [P, K_PASSES, PASS], I32, "wu_raw0")]
+        wu_raw = [keep.tile([P, K_PASSES, PASS], I32, name=f"wu_raw{rb}", align_bytes=ALIGN) for rb in range(R_BLOCKS)]
         nc.sync.dma_start(wu_raw[0][:], wu_view[:, :, 0:PASS])
 
         wu_sc = shared("words", [P, K_PASSES, R // 4], I32, "wu_sc", offset=CHUNK_BYTES)
@@ -93,16 +99,15 @@ def tile_list_modp_relu2_mix_resb_kernel(
         wu_sc_view = wu_scales.bitcast(I32).rearrange("a q r -> q a r")
         for q in range(QUADS):
             nc.sync.dma_start(wu_sc[quad_rows(q, PACK), :, :], wu_sc_view[PACK * q : PACK * (q + 1), :, :])
-        wu_raw.append(shared("wu1", [P, K_PASSES, PASS], I32, "wu_raw1"))
         nc.sync.dma_start(wu_raw[1][:], wu_view[:, :, PASS : 2 * PASS])
 
         sm_flat = sm_sb[:].rearrange("p b i -> p (b i)")
         magnitude = keep.tile([P, R_BLOCKS * PACK], F32, name="magnitude")
         sign = keep.tile([P, R_BLOCKS * PACK], F32, name="sign")
+        root = keep.tile([P, R_BLOCKS * PACK], F32, name="root")
         sign_wide = keep.tile([P, R_BLOCKS, SIGN_TOKENS * PACK], BF16, name="sign_wide", align_bytes=ALIGN)
         nc.scalar.activation(magnitude[:], sm_flat, ACT.Abs)
         nc.scalar.activation(sign[:], sm_flat, ACT.Sign)
-        root = keep.tile([P, R_BLOCKS * PACK], F32, name="root")
         nc.scalar.activation(root[:], magnitude[:], ACT.Sqrt)
         for rb in range(R_BLOCKS):
             nc.scalar.activation(
@@ -114,21 +119,19 @@ def tile_list_modp_relu2_mix_resb_kernel(
         nc.gpsimd.memset(windows[3][:], 0.0)
 
         picked_sc = shared("picked_sc", [P, J], U8, "picked_sc")
-        tab_planes = early.tile([P, K_PASSES, J // 4], I32, name="tab_planes", align_bytes=ALIGN, offset=0)
+        tab_planes = early_tile([P, K_PASSES, J // 4], I32, "tab_planes", 0)
         nc.vector.tensor_copy(picked_sc[:], tab_sc.bitcast(U8).indirect(offsets[:]))
         for a in range(K_PASSES):
             row = FILLER_ROWS + PACK * a
             nc.sync.dma_start(tab_planes[0:MOVED_ROWS, a, :], picked_sc[:].bitcast(I32)[row : row + MOVED_ROWS, :])
         tab_plane_bytes = tab_planes[:].rearrange("p a j -> p (a j)").bitcast(U8)
 
-        r_sb = []
-        for t in range(N_TILES):
-            r_sb.append(early.tile([P, T], F32, name=f"r_sb{t}", align_bytes=ALIGN, offset=EARLY_RESIDUAL + t * ROW_BYTES))
-        wd8_w = early.tile([P, N], I32, name="wd8_w", align_bytes=ALIGN, offset=EARLY_WD8)
-        wd4_w = early.tile([P, N // 2], I32, name="wd4_w", align_bytes=ALIGN, offset=EARLY_WD4)
+        r_sb = [early_tile([P, T], F32, f"r_sb{t}", EARLY_RESIDUAL + t * ROW_BYTES) for t in range(N_TILES)]
+        wd8_w = early_tile([P, N], I32, "wd8_w", EARLY_WD8)
+        wd4_w = early_tile([P, N // 2], I32, "wd4_w", EARLY_WD4)
         wd_sc = shared("picked_sc", [P, R_BLOCKS, N // 4], I32, "wd_sc")
-        wgo_sb = early.tile([P, J], F32, name="wgo_sb", align_bytes=ALIGN, offset=EARLY_WGO)
-        b_sb = early.tile([P, N_TILES], F32, name="b_sb", align_bytes=ALIGN, offset=EARLY_B)
+        wgo_sb = early_tile([P, J], F32, "wgo_sb", EARLY_WGO)
+        b_sb = early_tile([P, N_TILES], F32, "b_sb", EARLY_B)
 
         def load_residual(t):
             nc.sync.dma_start(r_sb[t][:], rT[t * P : (t + 1) * P, :])
@@ -189,7 +192,7 @@ def tile_list_modp_relu2_mix_resb_kernel(
             windows[t] = shared("words", [P, T], F32, f"window{t}", offset=t * ROW_BYTES)
             nc.gpsimd.memset(windows[t][:], 0.0)
 
-        unsigned, finished, h_codes, h_scales, picked_r = {}, {}, {}, {}, {}
+        unsigned, signed, h_codes, h_scales, picked_r, weighed = {}, {}, {}, {}, {}, {}
 
         def interleaved(values):
             return values.rearrange("p (g k i) -> p g i k", k=RUN, i=PACK)
@@ -197,81 +200,72 @@ def tile_list_modp_relu2_mix_resb_kernel(
         def by_output(values):
             return values.rearrange("p i (g k) -> p g i k", k=RUN)
 
-        def hidden(c, rb):
+        def token_columns(lo, hi):
+            return slice(lo * PACK, hi * PACK)
+
+        def rectify(c, rb, rooted, lo, hi, first_bank):
+            width = CHUNK if hi - lo == CHUNK else P
+            for i in range(PACK):
+                acc = bank_tile(f"acc_a{c}{rb}{i}{lo}", first_bank + i)
+                for group in range(lo, hi, width):
+                    token = c * CHUNK + group
+                    for a in range(K_PASSES):
+                        nc.tensor.matmul_mx(
+                            out=acc[:, group : group + width],
+                            lhsT=wu_codes[rb][:, a, i * P : (i + 1) * P].bitcast(FP8X4),
+                            lhsT_scale=wu_planes[rb][:, a, i * P : (i + 1) * P],
+                            rhs=parted[c][:, a, group : group + width].bitcast(FP4X4),
+                            rhs_scale=tab_plane_bytes[:, a * J + token : a * J + token + width],
+                            start=(a == 0),
+                            stop=(a == K_PASSES - 1),
+                        )
+                col = rb * PACK + i
+                nc.scalar.activation(rooted[:, i, lo:hi], acc[:, lo:hi], ACT.Relu, scale=root[:, col : col + 1])
+
+        def hidden_unsigned(c, rb, place):
             rooted = ring.tile([P, PACK, CHUNK], F32, name="rooted")
-            split = SIGN_ON_VECTOR[c, rb]
-            if split > 0:
-                place = f"unsigned{rb}" if c == 0 else "codes1"
-                unsigned[c, rb] = shared(place, [P, split * PACK], BF16, f"unsigned{c}{rb}")
-            halved = (c, rb) == (0, 0)
-            for first, last in ((0, HALF), (HALF, CHUNK)) if halved else ((0, CHUNK),):
-                width = P if halved else CHUNK
-                first_bank = PACK if (c, rb) == (1, 1) or first > 0 else 0
-                for i in range(PACK):
-                    bank = first_bank + i
-                    acc = psum.tile([P, CHUNK], F32, name=f"acc_a{c}{rb}{i}{first}", offset=bank * CHUNK_BYTES)
-                    for group in range(first, last, width):
-                        token = c * CHUNK + group
-                        for a in range(K_PASSES):
-                            nc.tensor.matmul_mx(
-                                out=acc[:, group : group + width],
-                                lhsT=wu_codes[rb][:, a, i * P : (i + 1) * P].bitcast(FP8X4),
-                                lhsT_scale=wu_planes[rb][:, a, i * P : (i + 1) * P],
-                                rhs=parted[c][:, a, group : group + width].bitcast(FP4X4),
-                                rhs_scale=tab_plane_bytes[:, a * J + token : a * J + token + width],
-                                start=(a == 0),
-                                stop=(a == K_PASSES - 1),
-                            )
-                    nc.scalar.activation(rooted[:, i, first:last], acc[:, first:last], ACT.Relu, scale=root[:, rb * PACK + i : rb * PACK + i + 1])
-                for lo in range(first, min(last, split), HALF):
-                    values = unsigned[c, rb][:, lo * PACK : (lo + HALF) * PACK]
+            unsigned[c, rb] = shared(place, [P, CHUNK * PACK], BF16, f"unsigned{c}{rb}")
+            for first, last in HALVES if (c, rb) == FIRST_BLOCK else WHOLE:
+                rectify(c, rb, rooted, first, last, PACK if first > 0 else 0)
+                for lo in range(first, last, HALF):
+                    values = unsigned[c, rb][:, token_columns(lo, lo + HALF)]
                     nc.scalar.activation(interleaved(values), by_output(rooted[:, :, lo : lo + HALF]), ACT.Square)
-            if split < CHUNK:
-                rest = CHUNK - split
-                squares = keep.tile([P, PACK, rest], F32, name=f"squares{rb}")
-                rounded = shared("rounded", [P, PACK, rest], BF16, f"rounded{rb}")
-                finished[c, rb] = shared("turn", [P, rest * PACK], BF16, f"finished{rb}", offset=2 * CHUNK_BYTES)
-                nc.scalar.activation(squares[:], rooted[:, :, split:CHUNK], ACT.Square)
-                for i in range(PACK):
-                    col = rb * PACK + i
-                    nc.scalar.activation(rounded[:, i, :], squares[:, i, :], ACT.Copy, scale=sign[:, col : col + 1])
-                for lo in (0, HALF):
-                    values = finished[c, rb][:, lo * PACK : (lo + HALF) * PACK]
-                    nc.scalar.copy(interleaved(values), by_output(rounded[:, :, lo : lo + HALF]))
 
-        signed = {}
+        def hidden_signed(c, rb):
+            rooted = ring.tile([P, PACK, CHUNK], F32, name="rooted")
+            rectify(c, rb, rooted, 0, CHUNK, PACK)
+            squares = keep.tile([P, PACK, CHUNK], F32, name="squares")
+            rounded = shared("rounded", [P, PACK, CHUNK], BF16, "rounded")
+            signed[c, rb] = keep.tile([P, CHUNK * PACK], BF16, name=f"signed{c}{rb}", align_bytes=ALIGN)
+            nc.scalar.activation(squares[:], rooted[:], ACT.Square)
+            for i in range(PACK):
+                col = rb * PACK + i
+                nc.scalar.activation(rounded[:, i, :], squares[:, i, :], ACT.Copy, scale=sign[:, col : col + 1])
+            for lo, hi in HALVES:
+                nc.scalar.copy(interleaved(signed[c, rb][:, token_columns(lo, hi)]), by_output(rounded[:, :, lo:hi]))
 
-        def code_tiles(c, rb):
-            if (c, rb) == (0, 1):
-                codes = shared("codes1", [P, CHUNK], U32, "h_codes01")
-            else:
-                codes = keep.tile([P, CHUNK], U32, name=f"h_codes{c}{rb}", align_bytes=ALIGN)
-            h_codes[c, rb] = codes
-            h_scales[c, rb] = keep.tile([P, CHUNK], U8, name=f"h_scales{c}{rb}", align_bytes=ALIGN)
-            if (c, rb) in unsigned:
-                if (c, rb) == (0, 0):
-                    at = EARLY_RESIDUAL + ROW_BYTES
-                    signed[c, rb] = early.tile([P, CHUNK * PACK], BF16, name="signed00", align_bytes=ALIGN, offset=at)
-                else:
-                    place = f"signed{rb}" if c == 0 else "turn"
-                    signed[c, rb] = shared(place, [P, CHUNK * PACK], BF16, f"signed{c}{rb}")
-
-        def apply_sign(c, rb, lo):
+        def apply_sign(c, rb, into):
+            signed[c, rb] = into
             width = SIGN_TOKENS * PACK
-            cols = slice(lo * PACK, (lo + HALF) * PACK)
-            nc.vector.tensor_tensor(
-                signed[c, rb][:, cols].rearrange("p (g x) -> p g x", x=width),
-                unsigned[c, rb][:, cols].rearrange("p (g x) -> p g x", x=width),
-                sign_wide[:, rb, :].unsqueeze(1).to_broadcast([P, HALF // SIGN_TOKENS, width]),
-                ALU.mult,
-            )
+            for lo, hi in HALVES:
+                nc.vector.tensor_tensor(
+                    into[:, token_columns(lo, hi)].rearrange("p (g x) -> p g x", x=width),
+                    unsigned[c, rb][:, token_columns(lo, hi)].rearrange("p (g x) -> p g x", x=width),
+                    sign_wide[:, rb, :].unsqueeze(1).to_broadcast([P, HALF // SIGN_TOKENS, width]),
+                    ALU.mult,
+                )
 
-        def quantise(c, rb, lo):
-            values = signed[c, rb] if (c, rb) in signed else finished[c, rb]
+        def code_tiles(c, rb, place):
+            h_codes[c, rb] = shared(place, [P, CHUNK], U32, f"h_codes{c}{rb}")
+            scales = keep.tile([P, CHUNK], U8, name=f"h_scales{c}{rb}", align_bytes=ALIGN)
+            for lo, hi in HALVES:
+                h_scales[c, rb, lo] = scales[:, lo:CHUNK]
+
+        def quantise(c, rb, lo, hi):
             nc.vector.quantize_mx(
-                out=h_codes[c, rb][:, lo : lo + HALF].bitcast(FP8X4),
-                scales=h_scales[c, rb][:, lo : lo + HALF],
-                in_=values[:, lo * PACK : (lo + HALF) * PACK],
+                out=h_codes[c, rb][:, lo:hi].bitcast(FP8X4),
+                scales=h_scales[c, rb, lo][:, 0 : hi - lo],
+                in_=signed[c, rb][:, token_columns(lo, hi)],
             )
 
         def gather_residual(t, lo, hi, into):
@@ -281,100 +275,94 @@ def tile_list_modp_relu2_mix_resb_kernel(
 
         for t in range(2):
             gather_residual(t, 0, J, keep.tile([P, J], F32, name=f"picked_r{t}"))
+        second_residual = EARLY_RESIDUAL + ROW_BYTES
         for rb in range(R_BLOCKS):
-            hidden(0, rb)
-            code_tiles(0, rb)
-            for lo in (0, HALF):
-                apply_sign(0, rb, lo)
-            for lo in (0, HALF):
-                quantise(0, rb, lo)
+            hidden_unsigned(0, rb, f"unsigned{rb}")
+            code_tiles(0, rb, f"codes0{rb}")
+            if rb == 0:
+                apply_sign(0, rb, early_tile([P, CHUNK * PACK], BF16, "signed00", second_residual))
+            else:
+                apply_sign(0, rb, shared("signed01", [P, CHUNK * PACK], BF16, "signed01"))
+            for lo, hi in HALVES:
+                quantise(0, rb, lo, hi)
             gather_residual(2, rb * CHUNK, (rb + 1) * CHUNK, shared(f"unsigned{rb}", [P, CHUNK], F32, f"picked_r2{rb}"))
             if rb == 0:
-                windows[2] = early.tile([P, T], F32, name="window2", align_bytes=ALIGN, offset=EARLY_RESIDUAL + ROW_BYTES)
+                windows[2] = early_tile([P, T], F32, "window2", second_residual)
                 nc.gpsimd.memset(windows[2][:], 0.0)
-        gather_residual(3, 0, J, shared("signed1", [P, J], F32, "picked_r3"))
+        gather_residual(3, 0, J, shared("signed01", [P, J], F32, "picked_r3"))
 
         wd_planes = wd_sc[:].rearrange("p b n -> p (b n)").bitcast(U8)
-        turn_step = (0, N_TILES - 1)
-        weighed = {}
-        held = keep.tile([P, HELD_TOKENS], F32, name="held")
-
-        def pieces(c, t):
-            return [(0, HALF), (HALF, CHUNK)] if t < HALVED_STEPS else [(0, CHUNK)]
-
         wd_codes = (
             lambda t: wd8_w[:, t * P : (t + 1) * P].bitcast(FP8X4),
             lambda t: wd4_w[:, t * P // 2 : (t + 1) * P // 2].bitcast(FP4X4),
         )
 
-        def second_layer(c, t, acc, lo, hi):
-            blocks = (1, 0) if c > 0 and t > 0 else (0, 1)
-            for rb in blocks:
-                nc.tensor.matmul_mx(
-                    out=acc[:, lo:hi],
-                    lhsT=wd_codes[rb](t),
-                    lhsT_scale=wd_planes[:, rb * N + t * P : rb * N + (t + 1) * P],
-                    rhs=h_codes[c, rb][:, lo:hi].bitcast(FP8X4),
-                    rhs_scale=h_scales[c, rb][:, lo:hi],
-                    start=(rb == blocks[0]),
-                    stop=(rb == blocks[1]),
-                )
+        def second_layer_pass(c, t, rb, acc, lo, hi, start, stop):
+            base = lo // HALF * HALF
+            nc.tensor.matmul_mx(
+                out=acc[:, lo:hi],
+                lhsT=wd_codes[rb](t),
+                lhsT_scale=wd_planes[:, rb * N + t * P : rb * N + (t + 1) * P],
+                rhs=h_codes[c, rb][:, lo:hi].bitcast(FP8X4),
+                rhs_scale=h_scales[c, rb, base][:, lo - base : hi - base],
+                start=start,
+                stop=stop,
+            )
 
-        def add_up(c, t):
-            acc = psum.tile([P, CHUNK], F32, name=f"acc_y{c}{t}", offset=((1 - c) * PACK + t) * CHUNK_BYTES)
-            if t > 0:
-                second_layer(c, t, acc, 0, CHUNK)
-            if (c, t) == (0, N_TILES - 2):
-                total = shared("turn", [P, CHUNK], F32, "total02")
-            elif (c, t) == (1, 0):
-                total = shared("rounded", [P, CHUNK], F32, "total10")
-            else:
-                total = keep.tile([P, CHUNK], F32, name=f"total{c}{t}")
-            for lo, hi in pieces(c, t):
-                if t == 0:
-                    if lo > 0:
-                        acc = psum.tile([P, CHUNK], F32, name=f"acc_second_half{c}", offset=((2 - c) * PACK - 1) * CHUNK_BYTES)
-                    for group in range(lo, hi, P):
-                        second_layer(c, t, acc, group, group + P)
+        def second_layer(c, t, acc, lo, hi):
+            if t > 0 and c > 0:
+                second_layer_pass(c, t, 1, acc, lo, hi, True, False)
+                for first, last in HALVES:
+                    second_layer_pass(c, t, 0, acc, first, last, False, last == hi)
+                return
+            width = CHUNK if hi - lo == CHUNK else P
+            for group in range(lo, hi, width):
+                for rb in range(R_BLOCKS):
+                    second_layer_pass(c, t, rb, acc, group, group + width, rb == 0, rb == R_BLOCKS - 1)
+
+        def pieces(t):
+            return HALVES if t == 0 else WHOLE
+
+        def finish(c, t, total):
+            first_bank = (1 - c) * PACK
+            for lo, hi in pieces(t):
+                acc = bank_tile(f"acc_y{c}{t}{lo}", first_bank + (t if lo == 0 else N_TILES - 1))
+                second_layer(c, t, acc, lo, hi)
                 nc.scalar.activation(total[:, lo:hi], acc[:, lo:hi], ACT.Identity, bias=b_sb[:, t : t + 1])
-                weighed[c, t, lo] = total[:, lo:hi]
                 with_residual = shared("sum", [P, hi - lo], F32, f"sum{c}{t}{lo}")
                 nc.gpsimd.tensor_tensor(with_residual[:], total[:, lo:hi], picked_r[c, t][:, lo:hi], ALU.add)
                 weights = wgo_sb[:, c * CHUNK + lo : c * CHUNK + hi]
-                if (c, t) == turn_step:
-                    free = CHUNK - HELD_TOKENS
-                    nc.gpsimd.tensor_tensor(total[:, 0:free], with_residual[:, 0:free], weights[:, 0:free], ALU.mult)
-                    nc.gpsimd.tensor_tensor(held[:], with_residual[:, free:CHUNK], weights[:, free:CHUNK], ALU.mult)
-                else:
-                    nc.gpsimd.tensor_tensor(total[:, lo:hi], with_residual[:], weights, ALU.mult)
-
-        def release_turn():
-            relay = shared("rounded", [P, HELD_TOKENS], F32, "relay")
-            nc.scalar.copy(relay[:], held[:])
-            nc.scalar.copy(weighed[turn_step + (0,)][:, CHUNK - HELD_TOKENS : CHUNK], relay[:])
+                nc.gpsimd.tensor_tensor(total[:, lo:hi], with_residual[:], weights, ALU.mult)
+            weighed[c, t] = total
 
         def scatter(c, t):
-            for lo, hi in pieces(c, t):
-                nc.vector.tensor_copy(windows[t][:].indirect(list_slice(c * CHUNK + lo, c * CHUNK + hi)), weighed[c, t, lo])
-            if c == CHUNKS - 1:
-                nc.sync.dma_start(out[t * P : (t + 1) * P, :], windows[t][:])
+            for lo, hi in pieces(t):
+                window = windows[t][:].indirect(list_slice(c * CHUNK + lo, c * CHUNK + hi))
+                nc.vector.tensor_copy(window, weighed[c, t][:, lo:hi])
 
+        last_free = HELD_STEP[1] - 1
         for t in range(N_TILES):
-            add_up(0, t)
-        for rb in range(R_BLOCKS):
-            hidden(1, rb)
-        for t in range(N_TILES - 1):
+            finish(0, t, shared(f"total0{t}", [P, CHUNK], F32, f"total0{t}"))
+        hidden_unsigned(1, 0, "codes01")
+        hidden_signed(*SCALAR_SIGNED)
+        for t in range(last_free + 1):
             scatter(0, t)
+
         for rb in range(R_BLOCKS):
-            code_tiles(1, rb)
-        for lo in (0, HALF):
-            apply_sign(1, 0, lo)
-        for rb in range(R_BLOCKS):
-            for lo in (0, HALF):
-                quantise(1, rb, lo)
-        release_turn()
-        scatter(*turn_step)
-        for t in range(N_TILES):
-            add_up(1, t)
+            code_tiles(1, rb, f"codes1{rb}")
+        h_scales[1, 0, HALF] = shared("rounded", [P, HALF], U8, "late_scales", offset=CHUNK_BYTES)[:]
+        apply_sign(1, 0, shared(f"total0{last_free}", [P, CHUNK * PACK], BF16, "signed10"))
+        for lo, hi in HALVES:
+            for rb in range(R_BLOCKS):
+                quantise(1, rb, lo, hi)
+        held = shared("rounded", [P, CHUNK], F32, "held")
+        nc.scalar.copy(held[:], weighed[HELD_STEP][:])
+        weighed[HELD_STEP] = held
+        scatter(*HELD_STEP)
+
+        finish(1, 0, shared("rounded", [P, CHUNK], F32, "total10", offset=CHUNK_BYTES + HALF))
+        for t in range(1, N_TILES):
+            finish(1, t, keep.tile([P, CHUNK], F32, name=f"total1{t}"))
         for t in range(N_TILES):
             scatter(1, t)
+            nc.sync.dma_start(out[t * P : (t + 1) * P, :], windows[t][:])

@@ -31,8 +31,8 @@ QUADS = 4
 RUN = 4
 ALIGN = 64
 SIGN_TOKENS = 128
-FILLER_ROWS = 32 - K_PASSES * PACK
-MOVED_ROWS = 32 * (QUADS - 1) + PACK
+QUAD_ROWS = K_PASSES * PACK
+FILLER_ROWS = P - QUADS * QUAD_ROWS
 
 FIRST_BLOCK = (0, 0)
 SCALAR_SIGNED = (1, 1)
@@ -81,27 +81,20 @@ def tile_list_modp_relu2_mix_resb_kernel(
             return slice(32 * q, 32 * q + count)
 
         tab_sc = early_tile([P, EARLY_BYTES // 4], I32, "tab_sc", 0)[:, 0 : T // 4]
-        for q in range(QUADS):
-            rows = slice(32 * q + FILLER_ROWS, 32 * (q + 1))
-            nc.sync.dma_start(tab_sc[rows, :], tab_scales.bitcast(I32)[:, PACK * q : PACK * (q + 1), :])
-        sm_sb = shared("sm", [P, R_BLOCKS, PACK], F32, "sm_sb")
-        nc.sync.dma_start(sm_sb[:], sm.rearrange("(b p i) -> p b i", b=R_BLOCKS, i=PACK))
+        nc.sync.dma_start(tab_sc[FILLER_ROWS:P, :], tab_scales.bitcast(I32).rearrange("a q t -> q a t"))
+        sm_flat = shared("sm", [P, 2 * T], F32, "sm_sb")[:, 0 : R_BLOCKS * PACK]
+        nc.sync.dma_start(sm_flat.rearrange("p (b i) -> p b i", i=PACK), sm.rearrange("(b p i) -> p b i", b=R_BLOCKS, i=PACK))
         wu_view = wu_words.rearrange("a p r i -> p a (r i)").bitcast(I32)
         tab_w = keep.tile([P, T], I32, name="tab_w", align_bytes=ALIGN)
         nc.sync.dma_start(tab_w[:], tab_words[0].rearrange("p t f -> p (t f)").bitcast(I32))
-        wu_raw = [keep.tile([P, K_PASSES, PASS], I32, name=f"wu_raw{rb}", align_bytes=ALIGN) for rb in range(R_BLOCKS)]
-        nc.sync.dma_start(wu_raw[0][:], wu_view[:, :, 0:PASS])
 
-        wu_sc = shared("words", [P, K_PASSES, R // 4], I32, "wu_sc", offset=CHUNK_BYTES)
+        wu_sc = shared("words", [P, K_PASSES, R // 4], I32, "wu_sc", offset=ROW_BYTES - R)
         nc.gpsimd.memset(wu_sc[:], 0)
-        for q in range(QUADS):
-            nc.vector.memset(tab_sc[quad_rows(q, FILLER_ROWS), :], 0)
+        nc.vector.memset(tab_sc[0:FILLER_ROWS, :], 0)
         wu_sc_view = wu_scales.bitcast(I32).rearrange("a q r -> q a r")
         for q in range(QUADS):
             nc.sync.dma_start(wu_sc[quad_rows(q, PACK), :, :], wu_sc_view[PACK * q : PACK * (q + 1), :, :])
-        nc.sync.dma_start(wu_raw[1][:], wu_view[:, :, PASS : 2 * PASS])
 
-        sm_flat = sm_sb[:].rearrange("p b i -> p (b i)")
         magnitude = keep.tile([P, R_BLOCKS * PACK], F32, name="magnitude")
         sign = keep.tile([P, R_BLOCKS * PACK], F32, name="sign")
         root = keep.tile([P, R_BLOCKS * PACK], F32, name="root")
@@ -115,15 +108,19 @@ def tile_list_modp_relu2_mix_resb_kernel(
                 sign[:, rb * PACK : (rb + 1) * PACK].unsqueeze(1).to_broadcast([P, SIGN_TOKENS, PACK]),
                 ACT.Copy,
             )
+        wu_raw = []
+        for rb in range(R_BLOCKS):
+            wu_raw.append(shared("sm", [P, K_PASSES, PASS], I32, f"wu_raw{rb}", offset=ROW_BYTES + rb * K_PASSES * PASS * 4))
+            nc.sync.dma_start(wu_raw[rb][:], wu_view[:, :, rb * PASS : (rb + 1) * PASS])
         windows = {3: shared("sm", [P, T], F32, "window3")}
         nc.gpsimd.memset(windows[3][:], 0.0)
 
         picked_sc = shared("picked_sc", [P, J], U8, "picked_sc")
         tab_planes = early_tile([P, K_PASSES, J // 4], I32, "tab_planes", 0)
         nc.vector.tensor_copy(picked_sc[:], tab_sc.bitcast(U8).indirect(offsets[:]))
-        for a in range(K_PASSES):
-            row = FILLER_ROWS + PACK * a
-            nc.sync.dma_start(tab_planes[0:MOVED_ROWS, a, :], picked_sc[:].bitcast(I32)[row : row + MOVED_ROWS, :])
+        for q in range(QUADS):
+            row = FILLER_ROWS + QUAD_ROWS * q
+            nc.sync.dma_start(tab_planes[quad_rows(q, PACK), :, :], picked_sc[:].bitcast(I32)[row : row + QUAD_ROWS, :])
         tab_plane_bytes = tab_planes[:].rearrange("p a j -> p (a j)").bitcast(U8)
 
         r_sb = [early_tile([P, T], F32, f"r_sb{t}", EARLY_RESIDUAL + t * ROW_BYTES) for t in range(N_TILES)]
@@ -163,31 +160,30 @@ def tile_list_modp_relu2_mix_resb_kernel(
             nc.vector.tensor_copy(words[:], picked_w.bitcast(U16).rearrange("p (j a) -> p a j", a=K_PASSES))
             parted.append(words)
 
-        def reorder_wu_words(rb):
+        def reorder_wu_words(rb, move):
             words = keep.tile([P, K_PASSES, PASS], I32, name=f"wu_codes{rb}", align_bytes=ALIGN)
-            nc.vector.tensor_copy(
-                words[:].rearrange("p a (i m) -> p a m i", i=PACK),
-                wu_raw[rb][:].rearrange("p a (m i) -> p a m i", i=PACK),
+            move(
+                words[:].bitcast(U32).rearrange("p a (i m) -> p a m i", i=PACK),
+                wu_raw[rb][:].bitcast(U32).rearrange("p a (m i) -> p a m i", i=PACK),
             )
             wu_codes.append(words)
 
-        def reorder_wu_scales(rb):
-            plane = keep.tile([P, K_PASSES, PASS], U8, name=f"wu_plane{rb}", align_bytes=ALIGN)
+        def reorder_wu_scales(rb, plane):
             loaded = wu_sc[:].rearrange("p a r -> p (a r)").bitcast(U8)
             loaded = loaded.rearrange("p (a b m i) -> p b a i m", a=K_PASSES, b=R_BLOCKS, i=PACK)
-            nc.vector.tensor_copy(plane[:].rearrange("p a (i m) -> p a i m", i=PACK), loaded[:, rb])
+            nc.gpsimd.tensor_copy(plane[:].rearrange("p a (i m) -> p a i m", i=PACK), loaded[:, rb])
             wu_planes.append(plane)
 
-        picked_w0 = shared("words", [P, CHUNK], U32, "picked_w0")[:]
+        picked_w0 = shared("picked", [P, CHUNK], U32, "picked_w0")[:]
         gather_words(0, picked_w0)
-        reorder_wu_words(0)
+        reorder_wu_words(0, nc.scalar.copy)
         part_words(0, picked_w0)
-        reorder_wu_scales(0)
-        reorder_wu_scales(1)
-        reorder_wu_words(1)
-        picked_w1 = shared("words", [P, 2 * T], U32, "picked_w1")[:, 0:CHUNK]
+        reorder_wu_scales(0, keep.tile([P, K_PASSES, PASS], U8, name="wu_plane0", align_bytes=ALIGN))
+        picked_w1 = shared("picked", [P, CHUNK], U32, "picked_w1")[:]
         gather_words(1, picked_w1)
         part_words(1, picked_w1)
+        reorder_wu_words(1, nc.vector.tensor_copy)
+        reorder_wu_scales(1, shared("picked", [P, K_PASSES, PASS], U8, "wu_plane1"))
         for t in range(2):
             windows[t] = shared("words", [P, T], F32, f"window{t}", offset=t * ROW_BYTES)
             nc.gpsimd.memset(windows[t][:], 0.0)
@@ -222,34 +218,34 @@ def tile_list_modp_relu2_mix_resb_kernel(
                 col = rb * PACK + i
                 nc.scalar.activation(rooted[:, i, lo:hi], acc[:, lo:hi], ACT.Relu, scale=root[:, col : col + 1])
 
-        def hidden_unsigned(c, rb, place):
+        def hidden_unsigned(c, rb, place, first_bank=0):
             rooted = ring.tile([P, PACK, CHUNK], F32, name="rooted")
             unsigned[c, rb] = shared(place, [P, CHUNK * PACK], BF16, f"unsigned{c}{rb}")
             for first, last in HALVES if (c, rb) == FIRST_BLOCK else WHOLE:
-                rectify(c, rb, rooted, first, last, PACK if first > 0 else 0)
+                rectify(c, rb, rooted, first, last, PACK if first > 0 else first_bank)
                 for lo in range(first, last, HALF):
                     values = unsigned[c, rb][:, token_columns(lo, lo + HALF)]
                     nc.scalar.activation(interleaved(values), by_output(rooted[:, :, lo : lo + HALF]), ACT.Square)
 
-        def hidden_signed(c, rb):
+        def hidden_half_signed(c, rb, into):
             rooted = ring.tile([P, PACK, CHUNK], F32, name="rooted")
             rectify(c, rb, rooted, 0, CHUNK, PACK)
-            squares = keep.tile([P, PACK, CHUNK], F32, name="squares")
-            rounded = shared("rounded", [P, PACK, CHUNK], BF16, "rounded")
-            signed[c, rb] = keep.tile([P, CHUNK * PACK], BF16, name=f"signed{c}{rb}", align_bytes=ALIGN)
-            nc.scalar.activation(squares[:], rooted[:], ACT.Square)
+            unsigned[c, rb] = keep.tile([P, HALF * PACK], BF16, name=f"unsigned{c}{rb}", align_bytes=ALIGN)
+            nc.scalar.activation(interleaved(unsigned[c, rb][:]), by_output(rooted[:, :, 0:HALF]), ACT.Square)
+            squares = keep.tile([P, PACK, HALF], F32, name="squares")
+            rounded = shared("rounded", [P, 3 * PACK, HALF], BF16, "rounded")[:, 0:PACK, :]
+            nc.scalar.activation(squares[:], rooted[:, :, HALF:CHUNK], ACT.Square)
             for i in range(PACK):
                 col = rb * PACK + i
                 nc.scalar.activation(rounded[:, i, :], squares[:, i, :], ACT.Copy, scale=sign[:, col : col + 1])
-            for lo, hi in HALVES:
-                nc.scalar.copy(interleaved(signed[c, rb][:, token_columns(lo, hi)]), by_output(rounded[:, :, lo:hi]))
+            nc.scalar.copy(interleaved(into[:]), by_output(rounded))
 
-        def apply_sign(c, rb, into):
-            signed[c, rb] = into
+        def apply_sign(c, rb, into, parts=HALVES):
             width = SIGN_TOKENS * PACK
-            for lo, hi in HALVES:
+            for lo, hi in parts:
+                signed[c, rb, lo] = into[:, token_columns(lo - parts[0][0], hi - parts[0][0])]
                 nc.vector.tensor_tensor(
-                    into[:, token_columns(lo, hi)].rearrange("p (g x) -> p g x", x=width),
+                    signed[c, rb, lo].rearrange("p (g x) -> p g x", x=width),
                     unsigned[c, rb][:, token_columns(lo, hi)].rearrange("p (g x) -> p g x", x=width),
                     sign_wide[:, rb, :].unsqueeze(1).to_broadcast([P, HALF // SIGN_TOKENS, width]),
                     ALU.mult,
@@ -265,7 +261,7 @@ def tile_list_modp_relu2_mix_resb_kernel(
             nc.vector.quantize_mx(
                 out=h_codes[c, rb][:, lo:hi].bitcast(FP8X4),
                 scales=h_scales[c, rb, lo][:, 0 : hi - lo],
-                in_=signed[c, rb][:, token_columns(lo, hi)],
+                in_=signed[c, rb, lo],
             )
 
         def gather_residual(t, lo, hi, into):
@@ -285,8 +281,8 @@ def tile_list_modp_relu2_mix_resb_kernel(
                 apply_sign(0, rb, shared("signed01", [P, CHUNK * PACK], BF16, "signed01"))
             for lo, hi in HALVES:
                 quantise(0, rb, lo, hi)
-            gather_residual(2, rb * CHUNK, (rb + 1) * CHUNK, shared(f"unsigned{rb}", [P, CHUNK], F32, f"picked_r2{rb}"))
             if rb == 0:
+                gather_residual(2, 0, J, shared("unsigned0", [P, J], F32, "picked_r2"))
                 windows[2] = early_tile([P, T], F32, "window2", second_residual)
                 nc.gpsimd.memset(windows[2][:], 0.0)
         gather_residual(3, 0, J, shared("signed01", [P, J], F32, "picked_r3"))
@@ -344,23 +340,28 @@ def tile_list_modp_relu2_mix_resb_kernel(
         for t in range(N_TILES):
             finish(0, t, shared(f"total0{t}", [P, CHUNK], F32, f"total0{t}"))
         hidden_unsigned(1, 0, "codes01")
-        hidden_signed(*SCALAR_SIGNED)
+        last_signed = keep.tile([P, HALF * PACK], BF16, name="last_signed", align_bytes=ALIGN)
+        hidden_half_signed(*SCALAR_SIGNED, last_signed)
+        signed[1, 1, HALF] = last_signed[:]
         for t in range(last_free + 1):
             scatter(0, t)
 
         for rb in range(R_BLOCKS):
             code_tiles(1, rb, f"codes1{rb}")
-        h_scales[1, 0, HALF] = shared("rounded", [P, HALF], U8, "late_scales", offset=CHUNK_BYTES)[:]
-        apply_sign(1, 0, shared(f"total0{last_free}", [P, CHUNK * PACK], BF16, "signed10"))
-        for lo, hi in HALVES:
-            for rb in range(R_BLOCKS):
-                quantise(1, rb, lo, hi)
+        signed1 = shared(f"total0{last_free}", [P, R_BLOCKS, HALF * PACK], BF16, "signed1")
+        for rb in range(R_BLOCKS):
+            apply_sign(1, rb, signed1[:, rb, :], HALVES[0:1])
+        for rb in range(R_BLOCKS):
+            quantise(1, rb, *HALVES[0])
+        apply_sign(1, 0, shared("rounded", [P, HALF * PACK], BF16, "signed10b", offset=2 * CHUNK_BYTES), HALVES[1:2])
+        for rb in (1, 0):
+            quantise(1, rb, *HALVES[1])
         held = shared("rounded", [P, CHUNK], F32, "held")
         nc.scalar.copy(held[:], weighed[HELD_STEP][:])
         weighed[HELD_STEP] = held
         scatter(*HELD_STEP)
 
-        finish(1, 0, shared("rounded", [P, CHUNK], F32, "total10", offset=CHUNK_BYTES + HALF))
+        finish(1, 0, shared("rounded", [P, CHUNK], F32, "total10", offset=CHUNK_BYTES))
         for t in range(1, N_TILES):
             finish(1, t, keep.tile([P, CHUNK], F32, name=f"total1{t}"))
         for t in range(N_TILES):

@@ -82,15 +82,20 @@ def tile_list_modp_relu2_mix_resb_kernel(
 
         tab_sc = early_tile([P, EARLY_BYTES // 4], I32, "tab_sc", 0)[:, 0 : T // 4]
         nc.sync.dma_start(tab_sc[FILLER_ROWS:P, :], tab_scales.bitcast(I32).rearrange("a q t -> q a t"))
-        sm_flat = shared("sm", [P, 2 * T], F32, "sm_sb")[:, 0 : R_BLOCKS * PACK]
+        sm_flat = shared("sm", [P, T], F32, "sm_sb")[:, 0 : R_BLOCKS * PACK]
         nc.sync.dma_start(sm_flat.rearrange("p (b i) -> p b i", i=PACK), sm.rearrange("(b p i) -> p b i", b=R_BLOCKS, i=PACK))
         wu_view = wu_words.rearrange("a p r i -> p a (r i)").bitcast(I32)
         tab_w = keep.tile([P, T], I32, name="tab_w", align_bytes=ALIGN)
         nc.sync.dma_start(tab_w[:], tab_words[0].rearrange("p t f -> p (t f)").bitcast(I32))
 
-        wu_sc = shared("words", [P, K_PASSES, R // 4], I32, "wu_sc", offset=ROW_BYTES - R)
+        wu_sc = keep.tile([P, K_PASSES, R // 4], I32, name="wu_sc", align_bytes=ALIGN)
         nc.gpsimd.memset(wu_sc[:], 0)
-        nc.vector.memset(tab_sc[0:FILLER_ROWS, :], 0)
+        nc.gpsimd.memset(tab_sc[0:FILLER_ROWS, :], 0)
+        windows = {t: keep.tile([P, T], F32, name=f"window{t}", align_bytes=ALIGN) for t in range(N_TILES - 1)}
+        nc.gpsimd.memset(windows[0][:], 0.0)
+        nc.gpsimd.memset(windows[1][:], 0.0)
+        nc.vector.memset(windows[2][:, 0 : T // 2 - 1], 0.0)
+        nc.vector.memset(windows[2][:, T // 2 - 1 : T], 0.0)
         wu_sc_view = wu_scales.bitcast(I32).rearrange("a q r -> q a r")
         for q in range(QUADS):
             nc.sync.dma_start(wu_sc[quad_rows(q, PACK), :, :], wu_sc_view[PACK * q : PACK * (q + 1), :, :])
@@ -110,10 +115,8 @@ def tile_list_modp_relu2_mix_resb_kernel(
             )
         wu_raw = []
         for rb in range(R_BLOCKS):
-            wu_raw.append(shared("sm", [P, K_PASSES, PASS], I32, f"wu_raw{rb}", offset=ROW_BYTES + rb * K_PASSES * PASS * 4))
+            wu_raw.append(shared("sm", [P, K_PASSES, PASS], I32, f"wu_raw{rb}", offset=rb * K_PASSES * PASS * 4))
             nc.sync.dma_start(wu_raw[rb][:], wu_view[:, :, rb * PASS : (rb + 1) * PASS])
-        windows = {3: shared("sm", [P, T], F32, "window3")}
-        nc.gpsimd.memset(windows[3][:], 0.0)
 
         picked_sc = shared("picked_sc", [P, J], U8, "picked_sc")
         tab_planes = early_tile([P, K_PASSES, J // 4], I32, "tab_planes", 0)
@@ -150,22 +153,24 @@ def tile_list_modp_relu2_mix_resb_kernel(
         with nc.allow_non_contiguous_dma(reason="one bias value to a partition"):
             nc.sync.dma_start(b_sb[:], b.rearrange("(t p) -> p t", p=P))
 
-        parted, wu_codes, wu_planes = [], [], []
+        parted = [keep.tile([P, K_PASSES, CHUNK], U16, name=f"parted{c}", align_bytes=ALIGN) for c in range(CHUNKS)]
+        wu_codes, wu_planes = [], []
 
-        def gather_words(c, picked_w):
-            nc.vector.tensor_copy(picked_w, tab_w[:].bitcast(U32).indirect(list_slice(c * CHUNK, (c + 1) * CHUNK)))
+        def gather_words(lo, hi, picked_w):
+            nc.vector.tensor_copy(picked_w[:], tab_w[:].bitcast(U32).indirect(list_slice(lo, hi)))
 
-        def part_words(c, picked_w):
-            words = keep.tile([P, K_PASSES, CHUNK], U16, name=f"parted{c}", align_bytes=ALIGN)
-            nc.vector.tensor_copy(words[:], picked_w.bitcast(U16).rearrange("p (j a) -> p a j", a=K_PASSES))
-            parted.append(words)
+        def part_words(c, lo, hi, picked_w):
+            halves = picked_w[:].bitcast(U16).rearrange("p (j a) -> p a j", a=K_PASSES)
+            nc.vector.tensor_copy(parted[c][:, :, lo:hi], halves)
 
-        def reorder_wu_words(rb, move):
+        def reorder_wu_words(rb, move, steps):
             words = keep.tile([P, K_PASSES, PASS], I32, name=f"wu_codes{rb}", align_bytes=ALIGN)
-            move(
-                words[:].bitcast(U32).rearrange("p a (i m) -> p a m i", i=PACK),
-                wu_raw[rb][:].bitcast(U32).rearrange("p a (m i) -> p a m i", i=PACK),
-            )
+            for first in range(0, PACK, PACK // steps):
+                outputs = slice(first, first + PACK // steps)
+                move(
+                    words[:].bitcast(U32).rearrange("p a (i m) -> p a m i", i=PACK)[:, :, :, outputs],
+                    wu_raw[rb][:].bitcast(U32).rearrange("p a (m i) -> p a m i", i=PACK)[:, :, :, outputs],
+                )
             wu_codes.append(words)
 
         def reorder_wu_scales(rb, plane):
@@ -174,19 +179,18 @@ def tile_list_modp_relu2_mix_resb_kernel(
             nc.gpsimd.tensor_copy(plane[:].rearrange("p a (i m) -> p a i m", i=PACK), loaded[:, rb])
             wu_planes.append(plane)
 
-        picked_w0 = shared("picked", [P, CHUNK], U32, "picked_w0")[:]
-        gather_words(0, picked_w0)
-        reorder_wu_words(0, nc.scalar.copy)
-        part_words(0, picked_w0)
+        picked_w0 = [shared("picked", [P, HALF], U32, "picked_w0a"), shared("picked_b", [P, HALF], U32, "picked_w0b")]
+        for (lo, hi), picked_w in zip(HALVES, picked_w0):
+            gather_words(lo, hi, picked_w)
+        reorder_wu_words(0, nc.scalar.copy, 2)
+        for (lo, hi), picked_w in zip(HALVES, picked_w0):
+            part_words(0, lo, hi, picked_w)
         reorder_wu_scales(0, keep.tile([P, K_PASSES, PASS], U8, name="wu_plane0", align_bytes=ALIGN))
-        picked_w1 = shared("picked", [P, CHUNK], U32, "picked_w1")[:]
-        gather_words(1, picked_w1)
-        part_words(1, picked_w1)
-        reorder_wu_words(1, nc.vector.tensor_copy)
-        reorder_wu_scales(1, shared("picked", [P, K_PASSES, PASS], U8, "wu_plane1"))
-        for t in range(2):
-            windows[t] = shared("words", [P, T], F32, f"window{t}", offset=t * ROW_BYTES)
-            nc.gpsimd.memset(windows[t][:], 0.0)
+        picked_w1 = shared("picked", [P, CHUNK], U32, "picked_w1")
+        gather_words(CHUNK, J, picked_w1)
+        part_words(1, 0, CHUNK, picked_w1)
+        reorder_wu_words(1, nc.vector.tensor_copy, 1)
+        reorder_wu_scales(1, shared("picked_b", [P, K_PASSES, PASS], U8, "wu_plane1"))
 
         unsigned, signed, h_codes, h_scales, picked_r, weighed = {}, {}, {}, {}, {}, {}
 
@@ -200,7 +204,7 @@ def tile_list_modp_relu2_mix_resb_kernel(
             return slice(lo * PACK, hi * PACK)
 
         def rectify(c, rb, rooted, lo, hi, first_bank):
-            width = CHUNK if hi - lo == CHUNK else P
+            width = hi - lo
             for i in range(PACK):
                 acc = bank_tile(f"acc_a{c}{rb}{i}{lo}", first_bank + i)
                 for group in range(lo, hi, width):
@@ -216,29 +220,38 @@ def tile_list_modp_relu2_mix_resb_kernel(
                             stop=(a == K_PASSES - 1),
                         )
                 col = rb * PACK + i
-                nc.scalar.activation(rooted[:, i, lo:hi], acc[:, lo:hi], ACT.Relu, scale=root[:, col : col + 1])
+                nc.scalar.activation(rooted[:, i, :], acc[:, lo:hi], ACT.Relu, scale=root[:, col : col + 1])
 
         def hidden_unsigned(c, rb, place, first_bank=0):
-            rooted = ring.tile([P, PACK, CHUNK], F32, name="rooted")
             unsigned[c, rb] = shared(place, [P, CHUNK * PACK], BF16, f"unsigned{c}{rb}")
             for first, last in HALVES if (c, rb) == FIRST_BLOCK else WHOLE:
+                if (c, rb) == FIRST_BLOCK:
+                    rooted = keep.tile([P, PACK, HALF], F32, name=f"first_rooted{first}")
+                else:
+                    rooted = ring.tile([P, PACK, CHUNK], F32, name="rooted")
                 rectify(c, rb, rooted, first, last, PACK if first > 0 else first_bank)
                 for lo in range(first, last, HALF):
                     values = unsigned[c, rb][:, token_columns(lo, lo + HALF)]
-                    nc.scalar.activation(interleaved(values), by_output(rooted[:, :, lo : lo + HALF]), ACT.Square)
+                    factor = by_output(rooted[:, :, lo - first : lo - first + HALF])
+                    if (c, rb, lo) == (*FIRST_BLOCK, 0):
+                        nc.gpsimd.tensor_tensor(interleaved(values), factor, factor, ALU.mult)
+                    else:
+                        nc.scalar.activation(interleaved(values), factor, ACT.Square)
 
-        def hidden_half_signed(c, rb, into):
+        def hidden_signed(c, rb):
             rooted = ring.tile([P, PACK, CHUNK], F32, name="rooted")
             rectify(c, rb, rooted, 0, CHUNK, PACK)
-            unsigned[c, rb] = keep.tile([P, HALF * PACK], BF16, name=f"unsigned{c}{rb}", align_bytes=ALIGN)
-            nc.scalar.activation(interleaved(unsigned[c, rb][:]), by_output(rooted[:, :, 0:HALF]), ACT.Square)
-            squares = keep.tile([P, PACK, HALF], F32, name="squares")
-            rounded = shared("rounded", [P, 3 * PACK, HALF], BF16, "rounded")[:, 0:PACK, :]
-            nc.scalar.activation(squares[:], rooted[:, :, HALF:CHUNK], ACT.Square)
+            squares = keep.tile([P, PACK, CHUNK], F32, name="squares")
+            rounded = shared("rounded", [P, 3 * PACK, HALF], BF16, "rounded")
+            rounded = rounded[:, 0 : 2 * PACK, :].rearrange("p (i h) j -> p i (h j)", i=PACK)
+            into = keep.tile([P, CHUNK * PACK], BF16, name=f"signed{c}{rb}", align_bytes=ALIGN)
+            nc.scalar.activation(squares[:], rooted[:], ACT.Square)
             for i in range(PACK):
                 col = rb * PACK + i
                 nc.scalar.activation(rounded[:, i, :], squares[:, i, :], ACT.Copy, scale=sign[:, col : col + 1])
-            nc.scalar.copy(interleaved(into[:]), by_output(rounded))
+            for lo, hi in HALVES:
+                signed[c, rb, lo] = into[:, token_columns(lo, hi)]
+                nc.scalar.copy(interleaved(signed[c, rb, lo]), by_output(rounded[:, :, lo:hi]))
 
         def apply_sign(c, rb, into, parts=HALVES):
             width = SIGN_TOKENS * PACK
@@ -275,16 +288,12 @@ def tile_list_modp_relu2_mix_resb_kernel(
         for rb in range(R_BLOCKS):
             hidden_unsigned(0, rb, f"unsigned{rb}")
             code_tiles(0, rb, f"codes0{rb}")
-            if rb == 0:
-                apply_sign(0, rb, early_tile([P, CHUNK * PACK], BF16, "signed00", second_residual))
-            else:
-                apply_sign(0, rb, shared("signed01", [P, CHUNK * PACK], BF16, "signed01"))
-            for lo, hi in HALVES:
+        apply_sign(0, 0, early_tile([P, CHUNK * PACK], BF16, "signed00", second_residual))
+        apply_sign(0, 1, shared("signed01", [P, 2 * CHUNK * PACK], BF16, "signed01"))
+        for lo, hi in HALVES:
+            for rb in range(R_BLOCKS):
                 quantise(0, rb, lo, hi)
-            if rb == 0:
-                gather_residual(2, 0, J, shared("unsigned0", [P, J], F32, "picked_r2"))
-                windows[2] = early_tile([P, T], F32, "window2", second_residual)
-                nc.gpsimd.memset(windows[2][:], 0.0)
+        gather_residual(2, 0, J, shared("signed01", [P, J], F32, "picked_r2", offset=J * 4))
         gather_residual(3, 0, J, shared("signed01", [P, J], F32, "picked_r3"))
 
         wd_planes = wd_sc[:].rearrange("p b n -> p (b n)").bitcast(U8)
@@ -311,7 +320,7 @@ def tile_list_modp_relu2_mix_resb_kernel(
                 for first, last in HALVES:
                     second_layer_pass(c, t, 0, acc, first, last, False, last == hi)
                 return
-            width = CHUNK if hi - lo == CHUNK else P
+            width = hi - lo
             for group in range(lo, hi, width):
                 for rb in range(R_BLOCKS):
                     second_layer_pass(c, t, rb, acc, group, group + width, rb == 0, rb == R_BLOCKS - 1)
@@ -325,10 +334,11 @@ def tile_list_modp_relu2_mix_resb_kernel(
                 acc = bank_tile(f"acc_y{c}{t}{lo}", first_bank + (t if lo == 0 else N_TILES - 1))
                 second_layer(c, t, acc, lo, hi)
                 nc.scalar.activation(total[:, lo:hi], acc[:, lo:hi], ACT.Identity, bias=b_sb[:, t : t + 1])
-                with_residual = shared("sum", [P, hi - lo], F32, f"sum{c}{t}{lo}")
-                nc.gpsimd.tensor_tensor(with_residual[:], total[:, lo:hi], picked_r[c, t][:, lo:hi], ALU.add)
+                span = CHUNK + T if (c, t) == HELD_STEP else hi - lo
+                with_residual = shared("sum", [P, span], F32, f"sum{c}{t}{lo}")[:, 0 : hi - lo]
+                nc.gpsimd.tensor_tensor(with_residual, total[:, lo:hi], picked_r[c, t][:, lo:hi], ALU.add)
                 weights = wgo_sb[:, c * CHUNK + lo : c * CHUNK + hi]
-                nc.gpsimd.tensor_tensor(total[:, lo:hi], with_residual[:], weights, ALU.mult)
+                nc.gpsimd.tensor_tensor(total[:, lo:hi], with_residual, weights, ALU.mult)
             weighed[c, t] = total
 
         def scatter(c, t):
@@ -339,23 +349,22 @@ def tile_list_modp_relu2_mix_resb_kernel(
         last_free = HELD_STEP[1] - 1
         for t in range(N_TILES):
             finish(0, t, shared(f"total0{t}", [P, CHUNK], F32, f"total0{t}"))
+        windows[3] = shared("sum", [P, T], F32, "window3", offset=CHUNK_BYTES)
+        nc.gpsimd.memset(windows[3][:], 0.0)
         hidden_unsigned(1, 0, "codes01")
-        last_signed = keep.tile([P, HALF * PACK], BF16, name="last_signed", align_bytes=ALIGN)
-        hidden_half_signed(*SCALAR_SIGNED, last_signed)
-        signed[1, 1, HALF] = last_signed[:]
+        hidden_signed(*SCALAR_SIGNED)
         for t in range(last_free + 1):
             scatter(0, t)
 
         for rb in range(R_BLOCKS):
             code_tiles(1, rb, f"codes1{rb}")
-        signed1 = shared(f"total0{last_free}", [P, R_BLOCKS, HALF * PACK], BF16, "signed1")
-        for rb in range(R_BLOCKS):
-            apply_sign(1, rb, signed1[:, rb, :], HALVES[0:1])
-        for rb in range(R_BLOCKS):
-            quantise(1, rb, *HALVES[0])
-        apply_sign(1, 0, shared("rounded", [P, HALF * PACK], BF16, "signed10b", offset=2 * CHUNK_BYTES), HALVES[1:2])
-        for rb in (1, 0):
-            quantise(1, rb, *HALVES[1])
+        h_scales[1, 0, HALF] = shared("rounded", [P, HALF], U8, "late_scales", offset=2 * CHUNK_BYTES)[:]
+        h_scales[1, 1, 0] = shared(f"total0{last_free}", [P, CHUNK], U8, "scales11", offset=0)[:]
+        h_scales[1, 1, HALF] = h_scales[1, 1, 0][:, HALF:CHUNK]
+        apply_sign(1, 0, shared(f"total0{last_free}", [P, CHUNK * PACK], BF16, "signed10", offset=CHUNK))
+        for lo, hi in HALVES:
+            for rb in range(R_BLOCKS):
+                quantise(1, rb, lo, hi)
         held = shared("rounded", [P, CHUNK], F32, "held")
         nc.scalar.copy(held[:], weighed[HELD_STEP][:])
         weighed[HELD_STEP] = held

@@ -226,7 +226,7 @@ def tile_list_modp_relu2_mix_resb_kernel(
             unsigned[c, rb] = shared(place, [P, CHUNK * PACK], BF16, f"unsigned{c}{rb}")
             for first, last in HALVES if (c, rb) == FIRST_BLOCK else WHOLE:
                 if (c, rb) == FIRST_BLOCK:
-                    rooted = keep.tile([P, PACK, HALF], F32, name=f"first_rooted{first}")
+                    rooted = shared(f"first_rooted{first}", [P, PACK, HALF], F32, f"first_rooted{first}")
                 else:
                     rooted = ring.tile([P, PACK, CHUNK], F32, name="rooted")
                 rectify(c, rb, rooted, first, last, PACK if first > 0 else first_bank)
@@ -260,7 +260,7 @@ def tile_list_modp_relu2_mix_resb_kernel(
                 nc.vector.tensor_tensor(
                     signed[c, rb, lo].rearrange("p (g x) -> p g x", x=width),
                     unsigned[c, rb][:, token_columns(lo, hi)].rearrange("p (g x) -> p g x", x=width),
-                    sign_wide[:, rb, :].unsqueeze(1).to_broadcast([P, HALF // SIGN_TOKENS, width]),
+                    sign_wide[:, rb, :].unsqueeze(1).to_broadcast([P, (hi - lo) // SIGN_TOKENS, width]),
                     ALU.mult,
                 )
 
@@ -282,19 +282,22 @@ def tile_list_modp_relu2_mix_resb_kernel(
             for c in range(lo // CHUNK, hi // CHUNK):
                 picked_r[c, t] = into[:, c * CHUNK - lo : (c + 1) * CHUNK - lo]
 
+        picked_pair = keep.tile([P, 2, J], F32, name="picked_pair")
         for t in range(2):
-            gather_residual(t, 0, J, keep.tile([P, J], F32, name=f"picked_r{t}"))
+            gather_residual(t, 0, J, picked_pair[:, t, :])
         second_residual = EARLY_RESIDUAL + ROW_BYTES
         for rb in range(R_BLOCKS):
             hidden_unsigned(0, rb, f"unsigned{rb}")
             code_tiles(0, rb, f"codes0{rb}")
-        apply_sign(0, 0, early_tile([P, CHUNK * PACK], BF16, "signed00", second_residual))
-        apply_sign(0, 1, shared("signed01", [P, 2 * CHUNK * PACK], BF16, "signed01"))
+        windows[3] = shared("first_rooted0", [P, T], F32, "window3")
+        nc.gpsimd.memset(windows[3][:], 0.0)
+        apply_sign(0, 0, early_tile([P, CHUNK * PACK], BF16, "signed00", second_residual), WHOLE)
+        quantise(0, 0, 0, CHUNK)
+        apply_sign(0, 1, early_tile([P, 2 * CHUNK * PACK], BF16, "signed01", second_residual))
         for lo, hi in HALVES:
-            for rb in range(R_BLOCKS):
-                quantise(0, rb, lo, hi)
-        gather_residual(2, 0, J, shared("signed01", [P, J], F32, "picked_r2", offset=J * 4))
-        gather_residual(3, 0, J, shared("signed01", [P, J], F32, "picked_r3"))
+            quantise(0, 1, lo, hi)
+        gather_residual(2, 0, J, early_tile([P, J], F32, "picked_r2", second_residual + J * 4))
+        gather_residual(3, 0, J, early_tile([P, J], F32, "picked_r3", second_residual))
 
         wd_planes = wd_sc[:].rearrange("p b n -> p (b n)").bitcast(U8)
         wd_codes = (
@@ -315,7 +318,7 @@ def tile_list_modp_relu2_mix_resb_kernel(
             )
 
         def second_layer(c, t, acc, lo, hi):
-            if t > 0 and c > 0:
+            if c > 0 and hi - lo == CHUNK:
                 second_layer_pass(c, t, 1, acc, lo, hi, True, False)
                 for first, last in HALVES:
                     second_layer_pass(c, t, 0, acc, first, last, False, last == hi)
@@ -329,28 +332,36 @@ def tile_list_modp_relu2_mix_resb_kernel(
             return HALVES if t == 0 else WHOLE
 
         def finish(c, t, total):
-            first_bank = (1 - c) * PACK
+            first_bank = PACK
             for lo, hi in pieces(t):
                 acc = bank_tile(f"acc_y{c}{t}{lo}", first_bank + (t if lo == 0 else N_TILES - 1))
                 second_layer(c, t, acc, lo, hi)
                 nc.scalar.activation(total[:, lo:hi], acc[:, lo:hi], ACT.Identity, bias=b_sb[:, t : t + 1])
-                span = CHUNK + T if (c, t) == HELD_STEP else hi - lo
-                with_residual = shared("sum", [P, span], F32, f"sum{c}{t}{lo}")[:, 0 : hi - lo]
+                with_residual = shared("sum", [P, hi - lo], F32, f"sum{c}{t}{lo}")[:]
                 nc.gpsimd.tensor_tensor(with_residual, total[:, lo:hi], picked_r[c, t][:, lo:hi], ALU.add)
                 weights = wgo_sb[:, c * CHUNK + lo : c * CHUNK + hi]
                 nc.gpsimd.tensor_tensor(total[:, lo:hi], with_residual, weights, ALU.mult)
             weighed[c, t] = total
 
+        def finish_pair(c, lo, hi, total, first_bank):
+            for t in range(2):
+                acc = bank_tile(f"acc_y{c}{t}{lo}", first_bank + t)
+                second_layer(c, t, acc, lo, hi)
+                nc.scalar.activation(total[:, t, :], acc[:, lo:hi], ACT.Identity, bias=b_sb[:, t : t + 1])
+            tokens = slice(c * CHUNK + lo, c * CHUNK + hi)
+            with_residual = shared("sum", [P, 2, hi - lo], F32, f"sum{c}{lo}")
+            nc.gpsimd.tensor_tensor(with_residual[:], total[:], picked_pair[:, :, tokens], ALU.add)
+            weights = wgo_sb[:, tokens].unsqueeze(1).to_broadcast([P, 2, hi - lo])
+            nc.gpsimd.tensor_tensor(total[:], with_residual[:], weights, ALU.mult)
+
         def scatter(c, t):
-            for lo, hi in pieces(t):
+            for lo, hi in pieces(t) if c > 0 else WHOLE:
                 window = windows[t][:].indirect(list_slice(c * CHUNK + lo, c * CHUNK + hi))
                 nc.vector.tensor_copy(window, weighed[c, t][:, lo:hi])
 
         last_free = HELD_STEP[1] - 1
         for t in range(N_TILES):
             finish(0, t, shared(f"total0{t}", [P, CHUNK], F32, f"total0{t}"))
-        windows[3] = shared("sum", [P, T], F32, "window3", offset=CHUNK_BYTES)
-        nc.gpsimd.memset(windows[3][:], 0.0)
         hidden_unsigned(1, 0, "codes01")
         hidden_signed(*SCALAR_SIGNED)
         for t in range(last_free + 1):
@@ -358,21 +369,33 @@ def tile_list_modp_relu2_mix_resb_kernel(
 
         for rb in range(R_BLOCKS):
             code_tiles(1, rb, f"codes1{rb}")
-        h_scales[1, 0, HALF] = shared("rounded", [P, HALF], U8, "late_scales", offset=2 * CHUNK_BYTES)[:]
         h_scales[1, 1, 0] = shared(f"total0{last_free}", [P, CHUNK], U8, "scales11", offset=0)[:]
         h_scales[1, 1, HALF] = h_scales[1, 1, 0][:, HALF:CHUNK]
-        apply_sign(1, 0, shared(f"total0{last_free}", [P, CHUNK * PACK], BF16, "signed10", offset=CHUNK))
-        for lo, hi in HALVES:
-            for rb in range(R_BLOCKS):
-                quantise(1, rb, lo, hi)
+        apply_sign(1, 0, shared(f"total0{last_free}", [P, HALF * PACK], BF16, "signed10a", offset=CHUNK), HALVES[0:1])
+        for rb in range(R_BLOCKS):
+            quantise(1, rb, *HALVES[0])
+        apply_sign(1, 0, shared("rounded", [P, HALF * PACK], BF16, "signed10b", offset=2 * CHUNK_BYTES), HALVES[1:2])
+        for rb in (1, 0):
+            quantise(1, rb, *HALVES[1])
         held = shared("rounded", [P, CHUNK], F32, "held")
         nc.scalar.copy(held[:], weighed[HELD_STEP][:])
         weighed[HELD_STEP] = held
         scatter(*HELD_STEP)
 
-        finish(1, 0, shared("rounded", [P, CHUNK], F32, "total10", offset=CHUNK_BYTES))
-        for t in range(1, N_TILES):
+        pairs = [
+            shared("rounded", [P, 2, HALF], F32, "pair0", offset=CHUNK_BYTES),
+            keep.tile([P, 2, HALF], F32, name="pair1"),
+        ]
+        for half, (lo, hi) in enumerate(HALVES):
+            finish_pair(1, lo, hi, pairs[half], 2 * half)
+        for t in range(2, N_TILES):
             finish(1, t, keep.tile([P, CHUNK], F32, name=f"total1{t}"))
-        for t in range(N_TILES):
+        for half, (lo, hi) in enumerate(HALVES):
+            for t in range(2):
+                window = windows[t][:].indirect(list_slice(CHUNK + lo, CHUNK + hi))
+                nc.vector.tensor_copy(window, pairs[half][:, t, :])
+                if hi == CHUNK:
+                    nc.sync.dma_start(out[t * P : (t + 1) * P, :], windows[t][:])
+        for t in range(2, N_TILES):
             scatter(1, t)
             nc.sync.dma_start(out[t * P : (t + 1) * P, :], windows[t][:])

@@ -34,6 +34,7 @@ SIGN_TOKENS = 128
 QUAD_ROWS = K_PASSES * PACK
 FILLER_ROWS = P - QUADS * QUAD_ROWS
 
+LOW_BANKS, HIGH_BANKS = (0, 1, 2, 3), (4, 5, 6, 7)
 FIRST_BLOCK = (0, 0)
 SCALAR_SIGNED = (1, 1)
 HELD_STEP = (0, N_TILES - 1)
@@ -203,10 +204,10 @@ def tile_list_modp_relu2_mix_resb_kernel(
         def token_columns(lo, hi):
             return slice(lo * PACK, hi * PACK)
 
-        def rectify(c, rb, rooted, lo, hi, first_bank):
+        def rectify(c, rb, rooted, lo, hi, banks):
             width = hi - lo
             for i in range(PACK):
-                acc = bank_tile(f"acc_a{c}{rb}{i}{lo}", first_bank + i)
+                acc = bank_tile(f"acc_a{c}{rb}{i}{lo}", banks[i])
                 for group in range(lo, hi, width):
                     token = c * CHUNK + group
                     for a in range(K_PASSES):
@@ -222,14 +223,14 @@ def tile_list_modp_relu2_mix_resb_kernel(
                 col = rb * PACK + i
                 nc.scalar.activation(rooted[:, i, :], acc[:, lo:hi], ACT.Relu, scale=root[:, col : col + 1])
 
-        def hidden_unsigned(c, rb, place, first_bank=0):
+        def hidden_unsigned(c, rb, place, banks=LOW_BANKS):
             unsigned[c, rb] = shared(place, [P, CHUNK * PACK], BF16, f"unsigned{c}{rb}")
             for first, last in HALVES if (c, rb) == FIRST_BLOCK else WHOLE:
                 if (c, rb) == FIRST_BLOCK:
                     rooted = shared(f"first_rooted{first}", [P, PACK, HALF], F32, f"first_rooted{first}")
                 else:
                     rooted = ring.tile([P, PACK, CHUNK], F32, name="rooted")
-                rectify(c, rb, rooted, first, last, PACK if first > 0 else first_bank)
+                rectify(c, rb, rooted, first, last, HIGH_BANKS if first > 0 else banks)
                 for lo in range(first, last, HALF):
                     values = unsigned[c, rb][:, token_columns(lo, lo + HALF)]
                     factor = by_output(rooted[:, :, lo - first : lo - first + HALF])
@@ -240,7 +241,7 @@ def tile_list_modp_relu2_mix_resb_kernel(
 
         def hidden_signed(c, rb):
             rooted = ring.tile([P, PACK, CHUNK], F32, name="rooted")
-            rectify(c, rb, rooted, 0, CHUNK, PACK)
+            rectify(c, rb, rooted, 0, CHUNK, (3, 5, 6, 7))
             squares = keep.tile([P, PACK, CHUNK], F32, name="squares")
             rounded = shared("rounded", [P, 3 * PACK, HALF], BF16, "rounded")
             rounded = rounded[:, 0 : 2 * PACK, :].rearrange("p (i h) j -> p i (h j)", i=PACK)
@@ -293,10 +294,11 @@ def tile_list_modp_relu2_mix_resb_kernel(
         nc.gpsimd.memset(windows[3][:], 0.0)
         apply_sign(0, 0, early_tile([P, CHUNK * PACK], BF16, "signed00", second_residual), WHOLE)
         quantise(0, 0, 0, CHUNK)
+        gather_residual(2, 0, CHUNK, shared("unsigned0", [P, CHUNK], F32, "picked_r20"))
         apply_sign(0, 1, early_tile([P, 2 * CHUNK * PACK], BF16, "signed01", second_residual))
         for lo, hi in HALVES:
             quantise(0, 1, lo, hi)
-        gather_residual(2, 0, J, early_tile([P, J], F32, "picked_r2", second_residual + J * 4))
+        gather_residual(2, CHUNK, J, early_tile([P, CHUNK], F32, "picked_r21", second_residual + J * 4))
         gather_residual(3, 0, J, early_tile([P, J], F32, "picked_r3", second_residual))
 
         wd_planes = wd_sc[:].rearrange("p b n -> p (b n)").bitcast(U8)
@@ -328,44 +330,45 @@ def tile_list_modp_relu2_mix_resb_kernel(
                 for rb in range(R_BLOCKS):
                     second_layer_pass(c, t, rb, acc, group, group + width, rb == 0, rb == R_BLOCKS - 1)
 
-        def pieces(t):
-            return HALVES if t == 0 else WHOLE
-
-        def finish(c, t, total):
-            first_bank = PACK
-            for lo, hi in pieces(t):
-                acc = bank_tile(f"acc_y{c}{t}{lo}", first_bank + (t if lo == 0 else N_TILES - 1))
-                second_layer(c, t, acc, lo, hi)
-                nc.scalar.activation(total[:, lo:hi], acc[:, lo:hi], ACT.Identity, bias=b_sb[:, t : t + 1])
-                with_residual = shared("sum", [P, hi - lo], F32, f"sum{c}{t}{lo}")[:]
-                nc.gpsimd.tensor_tensor(with_residual, total[:, lo:hi], picked_r[c, t][:, lo:hi], ALU.add)
-                weights = wgo_sb[:, c * CHUNK + lo : c * CHUNK + hi]
-                nc.gpsimd.tensor_tensor(total[:, lo:hi], with_residual, weights, ALU.mult)
+        def finish(c, t, total, bank):
+            acc = bank_tile(f"acc_y{c}{t}", bank)
+            second_layer(c, t, acc, 0, CHUNK)
+            nc.scalar.activation(total[:], acc[:], ACT.Identity, bias=b_sb[:, t : t + 1])
+            with_residual = shared("sum", [P, CHUNK], F32, f"sum{c}{t}")
+            nc.gpsimd.tensor_tensor(with_residual[:], total[:], picked_r[c, t], ALU.add)
+            nc.gpsimd.tensor_tensor(total[:], with_residual[:], wgo_sb[:, c * CHUNK : (c + 1) * CHUNK], ALU.mult)
             weighed[c, t] = total
 
-        def finish_pair(c, lo, hi, total, first_bank):
+        def finish_pair(c, lo, hi, total, banks):
             for t in range(2):
-                acc = bank_tile(f"acc_y{c}{t}{lo}", first_bank + t)
+                acc = bank_tile(f"acc_y{c}{t}{lo}", banks[t])
                 second_layer(c, t, acc, lo, hi)
                 nc.scalar.activation(total[:, t, :], acc[:, lo:hi], ACT.Identity, bias=b_sb[:, t : t + 1])
             tokens = slice(c * CHUNK + lo, c * CHUNK + hi)
-            with_residual = shared("sum", [P, 2, hi - lo], F32, f"sum{c}{lo}")
+            with_residual = shared("sum", [P, 2, hi - lo], F32, f"pair_sum{c}{lo}")
             nc.gpsimd.tensor_tensor(with_residual[:], total[:], picked_pair[:, :, tokens], ALU.add)
             weights = wgo_sb[:, tokens].unsqueeze(1).to_broadcast([P, 2, hi - lo])
             nc.gpsimd.tensor_tensor(total[:], with_residual[:], weights, ALU.mult)
 
-        def scatter(c, t):
-            for lo, hi in pieces(t) if c > 0 else WHOLE:
-                window = windows[t][:].indirect(list_slice(c * CHUNK + lo, c * CHUNK + hi))
-                nc.vector.tensor_copy(window, weighed[c, t][:, lo:hi])
+        def scatter(c, t, lo, hi, values):
+            window = windows[t][:].indirect(list_slice(c * CHUNK + lo, c * CHUNK + hi))
+            nc.vector.tensor_copy(window, values)
+
+        def store(t):
+            nc.sync.dma_start(out[t * P : (t + 1) * P, :], windows[t][:])
 
         last_free = HELD_STEP[1] - 1
-        for t in range(N_TILES):
-            finish(0, t, shared(f"total0{t}", [P, CHUNK], F32, f"total0{t}"))
-        hidden_unsigned(1, 0, "codes01")
+        pairs = [keep.tile([P, 2, HALF], F32, name=f"first_pair{half}") for half in range(2)]
+        finish_pair(0, *HALVES[0], pairs[0], (4, 5))
+        finish_pair(0, *HALVES[1], pairs[1], (3, 6))
+        finish(0, 2, shared("total02", [P, CHUNK], F32, "total02"), 7)
+        finish(0, 3, keep.tile([P, CHUNK], F32, name="total03"), 5)
+        hidden_unsigned(1, 0, "codes01", (0, 1, 2, PACK))
         hidden_signed(*SCALAR_SIGNED)
-        for t in range(last_free + 1):
-            scatter(0, t)
+        for half, (lo, hi) in enumerate(HALVES):
+            for t in range(2):
+                scatter(0, t, lo, hi, pairs[half][:, t, :])
+        scatter(0, 2, 0, CHUNK, weighed[0, 2][:])
 
         for rb in range(R_BLOCKS):
             code_tiles(1, rb, f"codes1{rb}")
@@ -379,23 +382,21 @@ def tile_list_modp_relu2_mix_resb_kernel(
             quantise(1, rb, *HALVES[1])
         held = shared("rounded", [P, CHUNK], F32, "held")
         nc.scalar.copy(held[:], weighed[HELD_STEP][:])
-        weighed[HELD_STEP] = held
-        scatter(*HELD_STEP)
+        scatter(*HELD_STEP, 0, CHUNK, held[:])
 
         pairs = [
             shared("rounded", [P, 2, HALF], F32, "pair0", offset=CHUNK_BYTES),
             keep.tile([P, 2, HALF], F32, name="pair1"),
         ]
         for half, (lo, hi) in enumerate(HALVES):
-            finish_pair(1, lo, hi, pairs[half], 2 * half)
+            finish_pair(1, lo, hi, pairs[half], (2 * half, 2 * half + 1))
         for t in range(2, N_TILES):
-            finish(1, t, keep.tile([P, CHUNK], F32, name=f"total1{t}"))
+            finish(1, t, keep.tile([P, CHUNK], F32, name=f"total1{t}"), PACK + t)
         for half, (lo, hi) in enumerate(HALVES):
             for t in range(2):
-                window = windows[t][:].indirect(list_slice(CHUNK + lo, CHUNK + hi))
-                nc.vector.tensor_copy(window, pairs[half][:, t, :])
+                scatter(1, t, lo, hi, pairs[half][:, t, :])
                 if hi == CHUNK:
-                    nc.sync.dma_start(out[t * P : (t + 1) * P, :], windows[t][:])
+                    store(t)
         for t in range(2, N_TILES):
-            scatter(1, t)
-            nc.sync.dma_start(out[t * P : (t + 1) * P, :], windows[t][:])
+            scatter(1, t, 0, CHUNK, weighed[1, t][:])
+            store(t)

@@ -26,21 +26,19 @@ CHUNK = 512
 CHUNKS = J // CHUNK
 HALF = CHUNK // 2
 HALVES = ((0, HALF), (HALF, CHUNK))
-WHOLE = ((0, CHUNK),)
 QUADS = 4
 RUN = 4
 ALIGN = 64
 SIGN_TOKENS = 128
 QUAD_ROWS = K_PASSES * PACK
 FILLER_ROWS = P - QUADS * QUAD_ROWS
-
+PAIR = 2
+ODD_CUT = T // 2 - 1
 LOW_BANKS, HIGH_BANKS = (0, 1, 2, 3), (4, 5, 6, 7)
-FIRST_BLOCK = (0, 0)
-SCALAR_SIGNED = (1, 1)
-HELD_STEP = (0, N_TILES - 1)
 
 ROW_BYTES = T * 4
 CHUNK_BYTES = CHUNK * 4
+WU_BLOCK_BYTES = K_PASSES * PASS * 4
 EARLY_RESIDUAL = K_PASSES * J
 EARLY_WD8 = EARLY_RESIDUAL + N_TILES * ROW_BYTES
 EARLY_WD4 = EARLY_WD8 + N * 4
@@ -66,6 +64,9 @@ def tile_list_modp_relu2_mix_resb_kernel(
                 places[place] = ctx.enter_context(tc.tile_pool(name=place, bufs=1))
             return places[place].tile(shape, dtype, name=name, align_bytes=ALIGN, offset=offset)
 
+        def own(shape, dtype, name):
+            return keep.tile(shape, dtype, name=name, align_bytes=ALIGN)
+
         def early_tile(shape, dtype, name, offset):
             return early.tile(shape, dtype, name=name, align_bytes=ALIGN, offset=offset)
 
@@ -78,35 +79,35 @@ def tile_list_modp_relu2_mix_resb_kernel(
         def list_slice(lo, hi):
             return offsets[:, lo // 16 : hi // 16]
 
-        def quad_rows(q, count):
-            return slice(32 * q, 32 * q + count)
+        def quad_rows(q):
+            return slice(32 * q, 32 * q + PACK)
 
         tab_sc = early_tile([P, EARLY_BYTES // 4], I32, "tab_sc", 0)[:, 0 : T // 4]
         nc.sync.dma_start(tab_sc[FILLER_ROWS:P, :], tab_scales.bitcast(I32).rearrange("a q t -> q a t"))
-        sm_flat = shared("sm", [P, T], F32, "sm_sb")[:, 0 : R_BLOCKS * PACK]
-        nc.sync.dma_start(sm_flat.rearrange("p (b i) -> p b i", i=PACK), sm.rearrange("(b p i) -> p b i", b=R_BLOCKS, i=PACK))
-        wu_view = wu_words.rearrange("a p r i -> p a (r i)").bitcast(I32)
-        tab_w = keep.tile([P, T], I32, name="tab_w", align_bytes=ALIGN)
+        sm_sb = shared("sm", [P, R_BLOCKS * WU_BLOCK_BYTES // 4], F32, "sm_sb")[:, 0 : R_BLOCKS * PACK]
+        sm_view = sm.rearrange("(b p i) -> p b i", b=R_BLOCKS, i=PACK)
+        nc.sync.dma_start(sm_sb.rearrange("p (b i) -> p b i", i=PACK), sm_view)
+        tab_w = own([P, T], I32, "tab_w")
         nc.sync.dma_start(tab_w[:], tab_words[0].rearrange("p t f -> p (t f)").bitcast(I32))
 
-        wu_sc = keep.tile([P, K_PASSES, R // 4], I32, name="wu_sc", align_bytes=ALIGN)
+        wu_sc = own([P, K_PASSES, R // 4], I32, "wu_sc")
         nc.gpsimd.memset(wu_sc[:], 0)
         nc.gpsimd.memset(tab_sc[0:FILLER_ROWS, :], 0)
-        windows = {t: keep.tile([P, T], F32, name=f"window{t}", align_bytes=ALIGN) for t in range(N_TILES - 1)}
+        windows = [own([P, T], F32, f"window{t}") for t in range(N_TILES - 1)]
         nc.gpsimd.memset(windows[0][:], 0.0)
         nc.gpsimd.memset(windows[1][:], 0.0)
-        nc.vector.memset(windows[2][:, 0 : T // 2 - 1], 0.0)
-        nc.vector.memset(windows[2][:, T // 2 - 1 : T], 0.0)
+        nc.vector.memset(windows[2][:, 0:ODD_CUT], 0.0)
+        nc.vector.memset(windows[2][:, ODD_CUT:T], 0.0)
         wu_sc_view = wu_scales.bitcast(I32).rearrange("a q r -> q a r")
         for q in range(QUADS):
-            nc.sync.dma_start(wu_sc[quad_rows(q, PACK), :, :], wu_sc_view[PACK * q : PACK * (q + 1), :, :])
+            nc.sync.dma_start(wu_sc[quad_rows(q), :, :], wu_sc_view[PACK * q : PACK * (q + 1), :, :])
 
         magnitude = keep.tile([P, R_BLOCKS * PACK], F32, name="magnitude")
         sign = keep.tile([P, R_BLOCKS * PACK], F32, name="sign")
         root = keep.tile([P, R_BLOCKS * PACK], F32, name="root")
-        sign_wide = keep.tile([P, R_BLOCKS, SIGN_TOKENS * PACK], BF16, name="sign_wide", align_bytes=ALIGN)
-        nc.scalar.activation(magnitude[:], sm_flat, ACT.Abs)
-        nc.scalar.activation(sign[:], sm_flat, ACT.Sign)
+        sign_wide = own([P, R_BLOCKS, SIGN_TOKENS * PACK], BF16, "sign_wide")
+        nc.scalar.activation(magnitude[:], sm_sb, ACT.Abs)
+        nc.scalar.activation(sign[:], sm_sb, ACT.Sign)
         nc.scalar.activation(root[:], magnitude[:], ACT.Sqrt)
         for rb in range(R_BLOCKS):
             nc.scalar.activation(
@@ -114,9 +115,11 @@ def tile_list_modp_relu2_mix_resb_kernel(
                 sign[:, rb * PACK : (rb + 1) * PACK].unsqueeze(1).to_broadcast([P, SIGN_TOKENS, PACK]),
                 ACT.Copy,
             )
+
+        wu_view = wu_words.rearrange("a p r i -> p a (r i)").bitcast(I32)
         wu_raw = []
         for rb in range(R_BLOCKS):
-            wu_raw.append(shared("sm", [P, K_PASSES, PASS], I32, f"wu_raw{rb}", offset=rb * K_PASSES * PASS * 4))
+            wu_raw.append(shared("sm", [P, K_PASSES, PASS], I32, f"wu_raw{rb}", offset=rb * WU_BLOCK_BYTES))
             nc.sync.dma_start(wu_raw[rb][:], wu_view[:, :, rb * PASS : (rb + 1) * PASS])
 
         picked_sc = shared("picked_sc", [P, J], U8, "picked_sc")
@@ -124,7 +127,7 @@ def tile_list_modp_relu2_mix_resb_kernel(
         nc.vector.tensor_copy(picked_sc[:], tab_sc.bitcast(U8).indirect(offsets[:]))
         for q in range(QUADS):
             row = FILLER_ROWS + QUAD_ROWS * q
-            nc.sync.dma_start(tab_planes[quad_rows(q, PACK), :, :], picked_sc[:].bitcast(I32)[row : row + QUAD_ROWS, :])
+            nc.sync.dma_start(tab_planes[quad_rows(q), :, :], picked_sc[:].bitcast(I32)[row : row + QUAD_ROWS, :])
         tab_plane_bytes = tab_planes[:].rearrange("p a j -> p (a j)").bitcast(U8)
 
         r_sb = [early_tile([P, T], F32, f"r_sb{t}", EARLY_RESIDUAL + t * ROW_BYTES) for t in range(N_TILES)]
@@ -139,40 +142,35 @@ def tile_list_modp_relu2_mix_resb_kernel(
 
         def load_wd_scales(rb, scales):
             for q in range(QUADS):
-                nc.sync.dma_start(
-                    wd_sc[quad_rows(q, PACK), rb, :], scales[0].bitcast(I32)[PACK * q : PACK * (q + 1), :]
-                )
+                nc.sync.dma_start(wd_sc[quad_rows(q), rb, :], scales[0].bitcast(I32)[PACK * q : PACK * (q + 1), :])
 
         for t in range(N_TILES - 1):
             load_residual(t)
         load_wd_scales(0, wd8_scales)
         nc.sync.dma_start(wd8_w[:], wd8_words[0].rearrange("p n i -> p (n i)").bitcast(I32))
         nc.sync.dma_start(wd4_w[:], wd4_words[0].bitcast(I32))
-        load_residual(N_TILES - 1)
-        nc.sync.dma_start(wgo_sb[:], wgo)
         load_wd_scales(1, wd4_scales)
         with nc.allow_non_contiguous_dma(reason="one bias value to a partition"):
             nc.sync.dma_start(b_sb[:], b.rearrange("(t p) -> p t", p=P))
+        load_residual(N_TILES - 1)
+        nc.sync.dma_start(wgo_sb[:], wgo)
 
-        parted = [keep.tile([P, K_PASSES, CHUNK], U16, name=f"parted{c}", align_bytes=ALIGN) for c in range(CHUNKS)]
-        wu_codes, wu_planes = [], []
+        parted = [own([P, K_PASSES, CHUNK], U16, f"parted{c}") for c in range(CHUNKS)]
+        wu_codes = [own([P, K_PASSES, PASS], U32, f"wu_codes{rb}") for rb in range(R_BLOCKS)]
+        wu_planes = []
 
         def gather_words(lo, hi, picked_w):
             nc.vector.tensor_copy(picked_w[:], tab_w[:].bitcast(U32).indirect(list_slice(lo, hi)))
 
         def part_words(c, lo, hi, picked_w):
-            halves = picked_w[:].bitcast(U16).rearrange("p (j a) -> p a j", a=K_PASSES)
-            nc.vector.tensor_copy(parted[c][:, :, lo:hi], halves)
+            by_pass = picked_w[:].bitcast(U16).rearrange("p (j a) -> p a j", a=K_PASSES)
+            nc.vector.tensor_copy(parted[c][:, :, lo:hi], by_pass)
 
-        def reorder_wu_words(rb, move, steps):
-            words = keep.tile([P, K_PASSES, PASS], I32, name=f"wu_codes{rb}", align_bytes=ALIGN)
-            for first in range(0, PACK, PACK // steps):
-                outputs = slice(first, first + PACK // steps)
-                move(
-                    words[:].bitcast(U32).rearrange("p a (i m) -> p a m i", i=PACK)[:, :, :, outputs],
-                    wu_raw[rb][:].bitcast(U32).rearrange("p a (m i) -> p a m i", i=PACK)[:, :, :, outputs],
-                )
-            wu_codes.append(words)
+        def reorder_wu_words(rb, move, outputs):
+            move(
+                wu_codes[rb][:].rearrange("p a (i m) -> p a m i", i=PACK)[:, :, :, outputs],
+                wu_raw[rb][:].bitcast(U32).rearrange("p a (m i) -> p a m i", i=PACK)[:, :, :, outputs],
+            )
 
         def reorder_wu_scales(rb, plane):
             loaded = wu_sc[:].rearrange("p a r -> p (a r)").bitcast(U8)
@@ -180,20 +178,21 @@ def tile_list_modp_relu2_mix_resb_kernel(
             nc.gpsimd.tensor_copy(plane[:].rearrange("p a (i m) -> p a i m", i=PACK), loaded[:, rb])
             wu_planes.append(plane)
 
-        picked_w0 = [shared("picked", [P, HALF], U32, "picked_w0a"), shared("picked_b", [P, HALF], U32, "picked_w0b")]
-        for (lo, hi), picked_w in zip(HALVES, picked_w0):
-            gather_words(lo, hi, picked_w)
-        reorder_wu_words(0, nc.scalar.copy, 2)
-        for (lo, hi), picked_w in zip(HALVES, picked_w0):
-            part_words(0, lo, hi, picked_w)
-        reorder_wu_scales(0, keep.tile([P, K_PASSES, PASS], U8, name="wu_plane0", align_bytes=ALIGN))
-        picked_w1 = shared("picked", [P, CHUNK], U32, "picked_w1")
-        gather_words(CHUNK, J, picked_w1)
-        part_words(1, 0, CHUNK, picked_w1)
-        reorder_wu_words(1, nc.vector.tensor_copy, 1)
-        reorder_wu_scales(1, shared("picked_b", [P, K_PASSES, PASS], U8, "wu_plane1"))
+        first_words = [shared(f"words{half}", [P, HALF], U32, f"first_words{half}") for half in range(2)]
+        for half, (lo, hi) in enumerate(HALVES):
+            gather_words(lo, hi, first_words[half])
+        reorder_wu_words(0, nc.scalar.copy, slice(0, PACK // 2))
+        reorder_wu_words(0, nc.scalar.copy, slice(PACK // 2, PACK))
+        for half, (lo, hi) in enumerate(HALVES):
+            part_words(0, lo, hi, first_words[half])
+        reorder_wu_scales(0, own([P, K_PASSES, PASS], U8, "wu_plane0"))
+        second_words = shared("words0", [P, CHUNK], U32, "second_words")
+        gather_words(CHUNK, J, second_words)
+        part_words(1, 0, CHUNK, second_words)
+        reorder_wu_words(1, nc.vector.tensor_copy, slice(0, PACK))
+        reorder_wu_scales(1, shared("words1", [P, K_PASSES, PASS], U8, "wu_plane1"))
 
-        unsigned, signed, h_codes, h_scales, picked_r, weighed = {}, {}, {}, {}, {}, {}
+        unsigned, signed, h_codes, h_scales, picked_r = {}, {}, {}, {}, {}
 
         def interleaved(values):
             return values.rearrange("p (g k i) -> p g i k", k=RUN, i=PACK)
@@ -205,47 +204,48 @@ def tile_list_modp_relu2_mix_resb_kernel(
             return slice(lo * PACK, hi * PACK)
 
         def rectify(c, rb, rooted, lo, hi, banks):
-            width = hi - lo
             for i in range(PACK):
                 acc = bank_tile(f"acc_a{c}{rb}{i}{lo}", banks[i])
-                for group in range(lo, hi, width):
-                    token = c * CHUNK + group
-                    for a in range(K_PASSES):
-                        nc.tensor.matmul_mx(
-                            out=acc[:, group : group + width],
-                            lhsT=wu_codes[rb][:, a, i * P : (i + 1) * P].bitcast(FP8X4),
-                            lhsT_scale=wu_planes[rb][:, a, i * P : (i + 1) * P],
-                            rhs=parted[c][:, a, group : group + width].bitcast(FP4X4),
-                            rhs_scale=tab_plane_bytes[:, a * J + token : a * J + token + width],
-                            start=(a == 0),
-                            stop=(a == K_PASSES - 1),
-                        )
+                for a in range(K_PASSES):
+                    token = a * J + c * CHUNK
+                    nc.tensor.matmul_mx(
+                        out=acc[:, lo:hi],
+                        lhsT=wu_codes[rb][:, a, i * P : (i + 1) * P].bitcast(FP8X4),
+                        lhsT_scale=wu_planes[rb][:, a, i * P : (i + 1) * P],
+                        rhs=parted[c][:, a, lo:hi].bitcast(FP4X4),
+                        rhs_scale=tab_plane_bytes[:, token + lo : token + hi],
+                        start=(a == 0),
+                        stop=(a == K_PASSES - 1),
+                    )
                 col = rb * PACK + i
                 nc.scalar.activation(rooted[:, i, :], acc[:, lo:hi], ACT.Relu, scale=root[:, col : col + 1])
 
-        def hidden_unsigned(c, rb, place, banks=LOW_BANKS):
-            unsigned[c, rb] = shared(place, [P, CHUNK * PACK], BF16, f"unsigned{c}{rb}")
-            for first, last in HALVES if (c, rb) == FIRST_BLOCK else WHOLE:
-                if (c, rb) == FIRST_BLOCK:
-                    rooted = shared(f"first_rooted{first}", [P, PACK, HALF], F32, f"first_rooted{first}")
-                else:
-                    rooted = ring.tile([P, PACK, CHUNK], F32, name="rooted")
-                rectify(c, rb, rooted, first, last, HIGH_BANKS if first > 0 else banks)
-                for lo in range(first, last, HALF):
-                    values = unsigned[c, rb][:, token_columns(lo, lo + HALF)]
-                    factor = by_output(rooted[:, :, lo - first : lo - first + HALF])
-                    if (c, rb, lo) == (*FIRST_BLOCK, 0):
-                        nc.gpsimd.tensor_tensor(interleaved(values), factor, factor, ALU.mult)
-                    else:
-                        nc.scalar.activation(interleaved(values), factor, ACT.Square)
+        def first_block():
+            unsigned[0, 0] = shared("unsigned00", [P, CHUNK * PACK], BF16, "unsigned00")
+            rooted = shared("first_rooted", [P, PACK, HALF], F32, "first_rooted")
+            rectify(0, 0, rooted, 0, HALF, LOW_BANKS)
+            values = interleaved(unsigned[0, 0][:, token_columns(0, HALF)])
+            nc.gpsimd.tensor_tensor(values, by_output(rooted[:]), by_output(rooted[:]), ALU.mult)
+            rooted = own([P, PACK, HALF], F32, "second_rooted")
+            rectify(0, 0, rooted, HALF, CHUNK, HIGH_BANKS)
+            values = interleaved(unsigned[0, 0][:, token_columns(HALF, CHUNK)])
+            nc.scalar.activation(values, by_output(rooted[:]), ACT.Square)
 
-        def hidden_signed(c, rb):
+        def hidden_unsigned(c, rb, into, banks):
+            unsigned[c, rb] = into
             rooted = ring.tile([P, PACK, CHUNK], F32, name="rooted")
-            rectify(c, rb, rooted, 0, CHUNK, (3, 5, 6, 7))
+            rectify(c, rb, rooted, 0, CHUNK, banks)
+            for lo, hi in HALVES:
+                values = interleaved(into[:, token_columns(lo, hi)])
+                nc.scalar.activation(values, by_output(rooted[:, :, lo:hi]), ACT.Square)
+
+        def hidden_signed(c, rb, banks):
+            rooted = ring.tile([P, PACK, CHUNK], F32, name="rooted")
+            rectify(c, rb, rooted, 0, CHUNK, banks)
             squares = keep.tile([P, PACK, CHUNK], F32, name="squares")
-            rounded = shared("rounded", [P, 3 * PACK, HALF], BF16, "rounded")
-            rounded = rounded[:, 0 : 2 * PACK, :].rearrange("p (i h) j -> p i (h j)", i=PACK)
-            into = keep.tile([P, CHUNK * PACK], BF16, name=f"signed{c}{rb}", align_bytes=ALIGN)
+            rounded = shared("rounded", [P, 3 * CHUNK_BYTES // 2], BF16, "rounded")[:, 0 : PACK * CHUNK]
+            rounded = rounded.rearrange("p (i j) -> p i j", i=PACK)
+            into = own([P, CHUNK * PACK], BF16, f"signed{c}{rb}")
             nc.scalar.activation(squares[:], rooted[:], ACT.Square)
             for i in range(PACK):
                 col = rb * PACK + i
@@ -254,52 +254,49 @@ def tile_list_modp_relu2_mix_resb_kernel(
                 signed[c, rb, lo] = into[:, token_columns(lo, hi)]
                 nc.scalar.copy(interleaved(signed[c, rb, lo]), by_output(rounded[:, :, lo:hi]))
 
-        def apply_sign(c, rb, into, parts=HALVES):
+        def apply_sign(c, rb, lo, hi, into):
+            signed[c, rb, lo] = into
             width = SIGN_TOKENS * PACK
-            for lo, hi in parts:
-                signed[c, rb, lo] = into[:, token_columns(lo - parts[0][0], hi - parts[0][0])]
-                nc.vector.tensor_tensor(
-                    signed[c, rb, lo].rearrange("p (g x) -> p g x", x=width),
-                    unsigned[c, rb][:, token_columns(lo, hi)].rearrange("p (g x) -> p g x", x=width),
-                    sign_wide[:, rb, :].unsqueeze(1).to_broadcast([P, (hi - lo) // SIGN_TOKENS, width]),
-                    ALU.mult,
-                )
-
-        def code_tiles(c, rb, place):
-            h_codes[c, rb] = shared(place, [P, CHUNK], U32, f"h_codes{c}{rb}")
-            scales = keep.tile([P, CHUNK], U8, name=f"h_scales{c}{rb}", align_bytes=ALIGN)
-            for lo, hi in HALVES:
-                h_scales[c, rb, lo] = scales[:, lo:CHUNK]
+            nc.vector.tensor_tensor(
+                into.rearrange("p (g x) -> p g x", x=width),
+                unsigned[c, rb][:, token_columns(lo, hi)].rearrange("p (g x) -> p g x", x=width),
+                sign_wide[:, rb, :].unsqueeze(1).to_broadcast([P, (hi - lo) // SIGN_TOKENS, width]),
+                ALU.mult,
+            )
 
         def quantise(c, rb, lo, hi):
             nc.vector.quantize_mx(
                 out=h_codes[c, rb][:, lo:hi].bitcast(FP8X4),
-                scales=h_scales[c, rb, lo][:, 0 : hi - lo],
+                scales=h_scales[c, rb][:, lo:hi],
                 in_=signed[c, rb, lo],
             )
 
         def gather_residual(t, lo, hi, into):
-            nc.vector.tensor_copy(into[:], r_sb[t][:].indirect(list_slice(lo, hi)))
+            nc.vector.tensor_copy(into, r_sb[t][:].indirect(list_slice(lo, hi)))
             for c in range(lo // CHUNK, hi // CHUNK):
                 picked_r[c, t] = into[:, c * CHUNK - lo : (c + 1) * CHUNK - lo]
 
-        picked_pair = keep.tile([P, 2, J], F32, name="picked_pair")
-        for t in range(2):
+        picked_pair = keep.tile([P, PAIR, J], F32, name="picked_pair")
+        for t in range(PAIR):
             gather_residual(t, 0, J, picked_pair[:, t, :])
         second_residual = EARLY_RESIDUAL + ROW_BYTES
+        first_block()
+        hidden_unsigned(0, 1, own([P, CHUNK * PACK], BF16, "unsigned01"), LOW_BANKS)
         for rb in range(R_BLOCKS):
-            hidden_unsigned(0, rb, f"unsigned{rb}")
-            code_tiles(0, rb, f"codes0{rb}")
-        windows[3] = shared("first_rooted0", [P, T], F32, "window3")
+            h_codes[0, rb] = shared(f"codes0{rb}", [P, CHUNK], U32, f"h_codes0{rb}")
+            h_scales[0, rb] = own([P, CHUNK], U8, f"h_scales0{rb}")
+        windows.append(shared("first_rooted", [P, T], F32, "window3"))
         nc.gpsimd.memset(windows[3][:], 0.0)
-        apply_sign(0, 0, early_tile([P, CHUNK * PACK], BF16, "signed00", second_residual), WHOLE)
+        apply_sign(0, 0, 0, CHUNK, early_tile([P, CHUNK * PACK], BF16, "signed00", second_residual)[:])
         quantise(0, 0, 0, CHUNK)
-        gather_residual(2, 0, CHUNK, shared("unsigned0", [P, CHUNK], F32, "picked_r20"))
-        apply_sign(0, 1, early_tile([P, 2 * CHUNK * PACK], BF16, "signed01", second_residual))
+        gather_residual(2, 0, CHUNK, shared("unsigned00", [P, CHUNK], F32, "picked_r20")[:])
+        signed01 = early_tile([P, ROW_BYTES // 2], BF16, "signed01", second_residual)
+        for lo, hi in HALVES:
+            apply_sign(0, 1, lo, hi, signed01[:, token_columns(lo, hi)])
         for lo, hi in HALVES:
             quantise(0, 1, lo, hi)
-        gather_residual(2, CHUNK, J, early_tile([P, CHUNK], F32, "picked_r21", second_residual + J * 4))
-        gather_residual(3, 0, J, early_tile([P, J], F32, "picked_r3", second_residual))
+        gather_residual(2, CHUNK, J, early_tile([P, CHUNK], F32, "picked_r21", second_residual + J * 4)[:])
+        gather_residual(3, 0, J, early_tile([P, J], F32, "picked_r3", second_residual)[:])
 
         wd_planes = wd_sc[:].rearrange("p b n -> p (b n)").bitcast(U8)
         wd_codes = (
@@ -307,48 +304,36 @@ def tile_list_modp_relu2_mix_resb_kernel(
             lambda t: wd4_w[:, t * P // 2 : (t + 1) * P // 2].bitcast(FP4X4),
         )
 
-        def second_layer_pass(c, t, rb, acc, lo, hi, start, stop):
-            base = lo // HALF * HALF
-            nc.tensor.matmul_mx(
-                out=acc[:, lo:hi],
-                lhsT=wd_codes[rb](t),
-                lhsT_scale=wd_planes[:, rb * N + t * P : rb * N + (t + 1) * P],
-                rhs=h_codes[c, rb][:, lo:hi].bitcast(FP8X4),
-                rhs_scale=h_scales[c, rb, base][:, lo - base : hi - base],
-                start=start,
-                stop=stop,
-            )
+        def second_layer(c, t, lo, hi, bank, into):
+            acc = bank_tile(f"acc_y{c}{t}{lo}", bank)
+            order = (1, 0) if c == 1 and hi == CHUNK else (0, 1)
+            for rb in order:
+                nc.tensor.matmul_mx(
+                    out=acc[:, lo:hi],
+                    lhsT=wd_codes[rb](t),
+                    lhsT_scale=wd_planes[:, rb * N + t * P : rb * N + (t + 1) * P],
+                    rhs=h_codes[c, rb][:, lo:hi].bitcast(FP8X4),
+                    rhs_scale=h_scales[c, rb][:, lo:hi],
+                    start=(rb == order[0]),
+                    stop=(rb == order[1]),
+                )
+            nc.scalar.activation(into, acc[:, lo:hi], ACT.Identity, bias=b_sb[:, t : t + 1])
 
-        def second_layer(c, t, acc, lo, hi):
-            if c > 0 and hi - lo == CHUNK:
-                second_layer_pass(c, t, 1, acc, lo, hi, True, False)
-                for first, last in HALVES:
-                    second_layer_pass(c, t, 0, acc, first, last, False, last == hi)
-                return
-            width = hi - lo
-            for group in range(lo, hi, width):
-                for rb in range(R_BLOCKS):
-                    second_layer_pass(c, t, rb, acc, group, group + width, rb == 0, rb == R_BLOCKS - 1)
-
-        def finish(c, t, total, bank):
-            acc = bank_tile(f"acc_y{c}{t}", bank)
-            second_layer(c, t, acc, 0, CHUNK)
-            nc.scalar.activation(total[:], acc[:], ACT.Identity, bias=b_sb[:, t : t + 1])
-            with_residual = shared("sum", [P, CHUNK], F32, f"sum{c}{t}")
-            nc.gpsimd.tensor_tensor(with_residual[:], total[:], picked_r[c, t], ALU.add)
-            nc.gpsimd.tensor_tensor(total[:], with_residual[:], wgo_sb[:, c * CHUNK : (c + 1) * CHUNK], ALU.mult)
-            weighed[c, t] = total
+        def weigh(name, total, residual, weights):
+            with_residual = shared("sum", total.shape, F32, name)
+            nc.gpsimd.tensor_tensor(with_residual[:], total[:], residual, ALU.add)
+            nc.gpsimd.tensor_tensor(total[:], with_residual[:], weights, ALU.mult)
 
         def finish_pair(c, lo, hi, total, banks):
-            for t in range(2):
-                acc = bank_tile(f"acc_y{c}{t}{lo}", banks[t])
-                second_layer(c, t, acc, lo, hi)
-                nc.scalar.activation(total[:, t, :], acc[:, lo:hi], ACT.Identity, bias=b_sb[:, t : t + 1])
+            for t in range(PAIR):
+                second_layer(c, t, lo, hi, banks[t], total[:, t, :])
             tokens = slice(c * CHUNK + lo, c * CHUNK + hi)
-            with_residual = shared("sum", [P, 2, hi - lo], F32, f"pair_sum{c}{lo}")
-            nc.gpsimd.tensor_tensor(with_residual[:], total[:], picked_pair[:, :, tokens], ALU.add)
-            weights = wgo_sb[:, tokens].unsqueeze(1).to_broadcast([P, 2, hi - lo])
-            nc.gpsimd.tensor_tensor(total[:], with_residual[:], weights, ALU.mult)
+            weights = wgo_sb[:, tokens].unsqueeze(1).to_broadcast([P, PAIR, hi - lo])
+            weigh(f"pair_sum{c}{lo}", total, picked_pair[:, :, tokens], weights)
+
+        def finish(c, t, total, bank):
+            second_layer(c, t, 0, CHUNK, bank, total[:])
+            weigh(f"sum{c}{t}", total, picked_r[c, t], wgo_sb[:, c * CHUNK : (c + 1) * CHUNK])
 
         def scatter(c, t, lo, hi, values):
             window = windows[t][:].indirect(list_slice(c * CHUNK + lo, c * CHUNK + hi))
@@ -357,46 +342,49 @@ def tile_list_modp_relu2_mix_resb_kernel(
         def store(t):
             nc.sync.dma_start(out[t * P : (t + 1) * P, :], windows[t][:])
 
-        last_free = HELD_STEP[1] - 1
-        pairs = [keep.tile([P, 2, HALF], F32, name=f"first_pair{half}") for half in range(2)]
-        finish_pair(0, *HALVES[0], pairs[0], (4, 5))
-        finish_pair(0, *HALVES[1], pairs[1], (3, 6))
-        finish(0, 2, shared("total02", [P, CHUNK], F32, "total02"), 7)
-        finish(0, 3, keep.tile([P, CHUNK], F32, name="total03"), 5)
-        hidden_unsigned(1, 0, "codes01", (0, 1, 2, PACK))
-        hidden_signed(*SCALAR_SIGNED)
+        pairs = [keep.tile([P, PAIR, HALF], F32, name=f"first_pair{half}") for half in range(2)]
+        total02 = shared("total02", [P, CHUNK], F32, "total02")
+        total03 = keep.tile([P, CHUNK], F32, name="total03")
+        finish_pair(0, 0, HALF, pairs[0], (4, 5))
+        finish_pair(0, HALF, CHUNK, pairs[1], (3, 6))
+        finish(0, 2, total02, 7)
+        finish(0, 3, total03, 5)
+        hidden_unsigned(1, 0, shared("codes01", [P, CHUNK * PACK], BF16, "unsigned10"), (0, 1, 2, 4))
+        hidden_signed(1, 1, (3, 5, 6, 7))
         for half, (lo, hi) in enumerate(HALVES):
-            for t in range(2):
+            for t in range(PAIR):
                 scatter(0, t, lo, hi, pairs[half][:, t, :])
-        scatter(0, 2, 0, CHUNK, weighed[0, 2][:])
+        scatter(0, 2, 0, CHUNK, total02[:])
 
         for rb in range(R_BLOCKS):
-            code_tiles(1, rb, f"codes1{rb}")
-        h_scales[1, 1, 0] = shared(f"total0{last_free}", [P, CHUNK], U8, "scales11", offset=0)[:]
-        h_scales[1, 1, HALF] = h_scales[1, 1, 0][:, HALF:CHUNK]
-        apply_sign(1, 0, shared(f"total0{last_free}", [P, HALF * PACK], BF16, "signed10a", offset=CHUNK), HALVES[0:1])
-        for rb in range(R_BLOCKS):
-            quantise(1, rb, *HALVES[0])
-        apply_sign(1, 0, shared("rounded", [P, HALF * PACK], BF16, "signed10b", offset=2 * CHUNK_BYTES), HALVES[1:2])
-        for rb in (1, 0):
-            quantise(1, rb, *HALVES[1])
+            h_codes[1, rb] = own([P, CHUNK], U32, f"h_codes1{rb}")
+        h_scales[1, 0] = own([P, CHUNK], U8, "h_scales10")
+        h_scales[1, 1] = shared("total02", [P, CHUNK], U8, "h_scales11")
+        apply_sign(1, 0, 0, HALF, shared("total02", [P, HALF * PACK], BF16, "signed10a", offset=CHUNK)[:])
+        quantise(1, 0, 0, HALF)
+        quantise(1, 1, 0, HALF)
+        late_signed = shared("rounded", [P, HALF * PACK], BF16, "signed10b", offset=2 * CHUNK_BYTES)
+        apply_sign(1, 0, HALF, CHUNK, late_signed[:])
+        quantise(1, 1, HALF, CHUNK)
+        quantise(1, 0, HALF, CHUNK)
         held = shared("rounded", [P, CHUNK], F32, "held")
-        nc.scalar.copy(held[:], weighed[HELD_STEP][:])
-        scatter(*HELD_STEP, 0, CHUNK, held[:])
+        nc.scalar.copy(held[:], total03[:])
+        scatter(0, 3, 0, CHUNK, held[:])
 
         pairs = [
-            shared("rounded", [P, 2, HALF], F32, "pair0", offset=CHUNK_BYTES),
-            keep.tile([P, 2, HALF], F32, name="pair1"),
+            shared("rounded", [P, PAIR, HALF], F32, "second_pair0", offset=CHUNK_BYTES),
+            keep.tile([P, PAIR, HALF], F32, name="second_pair1"),
         ]
+        totals = {t: keep.tile([P, CHUNK], F32, name=f"total1{t}") for t in range(PAIR, N_TILES)}
         for half, (lo, hi) in enumerate(HALVES):
-            finish_pair(1, lo, hi, pairs[half], (2 * half, 2 * half + 1))
-        for t in range(2, N_TILES):
-            finish(1, t, keep.tile([P, CHUNK], F32, name=f"total1{t}"), PACK + t)
-        for half, (lo, hi) in enumerate(HALVES):
-            for t in range(2):
-                scatter(1, t, lo, hi, pairs[half][:, t, :])
-                if hi == CHUNK:
-                    store(t)
-        for t in range(2, N_TILES):
-            scatter(1, t, 0, CHUNK, weighed[1, t][:])
+            finish_pair(1, lo, hi, pairs[half], LOW_BANKS[PAIR * half : PAIR * (half + 1)])
+        for t in range(PAIR, N_TILES):
+            finish(1, t, totals[t], HIGH_BANKS[t])
+        for t in range(PAIR):
+            scatter(1, t, 0, HALF, pairs[0][:, t, :])
+        for t in range(PAIR):
+            scatter(1, t, HALF, CHUNK, pairs[1][:, t, :])
+            store(t)
+        for t in range(PAIR, N_TILES):
+            scatter(1, t, 0, CHUNK, totals[t][:])
             store(t)

@@ -348,9 +348,9 @@ def tile_list_modp_relu2_mix_resb_kernel(
         finish_pair(0, 0, HALF, pairs[0], (4, 5))
         finish_pair(0, HALF, CHUNK, pairs[1], (3, 6))
         finish(0, 2, total02, 7)
-        finish(0, 3, total03, 5)
-        hidden_unsigned(1, 0, shared("codes01", [P, CHUNK * PACK], BF16, "unsigned10"), (0, 1, 2, 4))
-        hidden_signed(1, 1, (3, 5, 6, 7))
+        finish(0, 3, total03, 2)
+        hidden_unsigned(1, 0, shared("codes01", [P, CHUNK * PACK], BF16, "unsigned10"), (0, 1, 4, 5))
+        hidden_signed(1, 1, (3, 6, 7, 2))
         for half, (lo, hi) in enumerate(HALVES):
             for t in range(PAIR):
                 scatter(0, t, lo, hi, pairs[half][:, t, :])

from contextlib import ExitStack

import concourse.mybir as mybir

K, R, N, T, J = 1024, 1024, 512, 2048, 1024
FLOPS = 2 * K * R * J + 2 * R * N * J

F32 = mybir.dt.float32
BF16 = mybir.dt.bfloat16
I32 = mybir.dt.int32
U32 = mybir.dt.uint32
U16 = mybir.dt.uint16
U8 = mybir.dt.uint8
FP8X4 = mybir.dt.float8_e4m3fn_x4
FP4X4 = mybir.dt.float4_e2m1fn_x4
ALU = mybir.AluOpType
ACT = mybir.ActivationFunctionType

P = 128
PACK = 4
PASS = P * PACK
K_PASSES = K // PASS
R_BLOCKS = R // PASS
N_TILES = N // P
CHUNK = 512
CHUNKS = J // CHUNK
HALF = CHUNK // 2
HALVES = ((0, HALF), (HALF, CHUNK))
QUADS = 4
RUN = 4
ALIGN = 64
SIGN_TOKENS = 128
QUAD_ROWS = K_PASSES * PACK
FILLER_ROWS = P - QUADS * QUAD_ROWS
PAIR = 2
ODD_CUT = T // 2 - 1
LOW_BANKS, HIGH_BANKS = (0, 1, 2, 3), (4, 5, 6, 7)

ROW_BYTES = T * 4
CHUNK_BYTES = CHUNK * 4
WU_BLOCK_BYTES = K_PASSES * PASS * 4
EARLY_RESIDUAL = K_PASSES * J
EARLY_WD8 = EARLY_RESIDUAL + N_TILES * ROW_BYTES
EARLY_WD4 = EARLY_WD8 + N * 4
EARLY_WGO = EARLY_WD4 + N * 2
EARLY_B = EARLY_WGO + J * 4
EARLY_BYTES = EARLY_B + ALIGN


def tile_list_modp_relu2_mix_resb_kernel(
    tc, tab_words, tab_scales, wu_words, wu_scales, sm, wd8_words, wd8_scales,
    wd4_words, wd4_scales, rT, b, wgo, offs, out,
):
    nc = tc.nc
    with ExitStack() as ctx:
        keep = ctx.enter_context(tc.tile_pool(name="keep", bufs=1))
        ring = ctx.enter_context(tc.tile_pool(name="ring", bufs=2))
        early = ctx.enter_context(tc.tile_pool(name="early", bufs=1))
        psum = ctx.enter_context(tc.psum_pool(name="psum", bufs=1))
        places = {}

        def shared(place, shape, dtype, name, offset=0):
            if place not in places:
                places[place] = ctx.enter_context(tc.tile_pool(name=place, bufs=1))
            return places[place].tile(shape, dtype, name=name, align_bytes=ALIGN, offset=offset)

        def own(shape, dtype, name):
            return keep.tile(shape, dtype, name=name, align_bytes=ALIGN)

        def early_tile(shape, dtype, name, offset):
            return early.tile(shape, dtype, name=name, align_bytes=ALIGN, offset=offset)

        def bank_tile(name, bank):
            return psum.tile([P, CHUNK], F32, name=name, offset=bank * CHUNK_BYTES)

        offsets = keep.tile([P, J // 16], U16, name="offsets")
        nc.sync.dma_start(offsets[:], offs)

        def list_slice(lo, hi):
            return offsets[:, lo // 16 : hi // 16]

        def quad_rows(q):
            return slice(32 * q, 32 * q + PACK)

        tab_sc = early_tile([P, EARLY_BYTES // 4], I32, "tab_sc", 0)[:, 0 : T // 4]
        nc.sync.dma_start(tab_sc[FILLER_ROWS:P, :], tab_scales.bitcast(I32).rearrange("a q t -> q a t"))
        sm_sb = shared("sm", [P, R_BLOCKS * WU_BLOCK_BYTES // 4], F32, "sm_sb")[:, 0 : R_BLOCKS * PACK]
        sm_view = sm.rearrange("(b p i) -> p b i", b=R_BLOCKS, i=PACK)
        nc.sync.dma_start(sm_sb.rearrange("p (b i) -> p b i", i=PACK), sm_view)
        tab_w = own([P, T], I32, "tab_w")
        nc.sync.dma_start(tab_w[:], tab_words[0].rearrange("p t f -> p (t f)").bitcast(I32))

        wu_sc = own([P, K_PASSES, R // 4], I32, "wu_sc")
        nc.gpsimd.memset(wu_sc[:], 0)
        nc.gpsimd.memset(tab_sc[0:FILLER_ROWS, :], 0)
        windows = [own([P, T], F32, f"window{t}") for t in range(N_TILES - 1)]
        nc.gpsimd.memset(windows[0][:], 0.0)
        nc.gpsimd.memset(windows[1][:], 0.0)
        nc.vector.memset(windows[2][:, 0:ODD_CUT], 0.0)
        nc.vector.memset(windows[2][:, ODD_CUT:T], 0.0)
        wu_sc_view = wu_scales.bitcast(I32).rearrange("a q r -> q a r")
        for q in range(QUADS):
            nc.sync.dma_start(wu_sc[quad_rows(q), :, :], wu_sc_view[PACK * q : PACK * (q + 1), :, :])

        magnitude = keep.tile([P, R_BLOCKS * PACK], F32, name="magnitude")
        sign = keep.tile([P, R_BLOCKS * PACK], F32, name="sign")
        root = keep.tile([P, R_BLOCKS * PACK], F32, name="root")
        sign_wide = own([P, R_BLOCKS, SIGN_TOKENS * PACK], BF16, "sign_wide")
        nc.scalar.activation(magnitude[:], sm_sb, ACT.Abs)
        nc.scalar.activation(sign[:], sm_sb, ACT.Sign)
        nc.scalar.activation(root[:], magnitude[:], ACT.Sqrt)
        for rb in range(R_BLOCKS):
            nc.scalar.activation(
                sign_wide[:, rb, :].rearrange("p (j i) -> p j i", i=PACK),
                sign[:, rb * PACK : (rb + 1) * PACK].unsqueeze(1).to_broadcast([P, SIGN_TOKENS, PACK]),
                ACT.Copy,
            )

        wu_view = wu_words.rearrange("a p r i -> p a (r i)").bitcast(I32)
        wu_raw = []
        for rb in range(R_BLOCKS):
            wu_raw.append(shared("sm", [P, K_PASSES, PASS], I32, f"wu_raw{rb}", offset=rb * WU_BLOCK_BYTES))
            nc.sync.dma_start(wu_raw[rb][:], wu_view[:, :, rb * PASS : (rb + 1) * PASS])

        picked_sc = shared("picked_sc", [P, J], U8, "picked_sc")
        tab_planes = early_tile([P, K_PASSES, J // 4], I32, "tab_planes", 0)
        nc.vector.tensor_copy(picked_sc[:], tab_sc.bitcast(U8).indirect(offsets[:]))
        for q in range(QUADS):
            row = FILLER_ROWS + QUAD_ROWS * q
            nc.sync.dma_start(tab_planes[quad_rows(q), :, :], picked_sc[:].bitcast(I32)[row : row + QUAD_ROWS, :])
        tab_plane_bytes = tab_planes[:].rearrange("p a j -> p (a j)").bitcast(U8)

        r_sb = [early_tile([P, T], F32, f"r_sb{t}", EARLY_RESIDUAL + t * ROW_BYTES) for t in range(N_TILES)]
        wd8_w = early_tile([P, N], I32, "wd8_w", EARLY_WD8)
        wd4_w = early_tile([P, N // 2], I32, "wd4_w", EARLY_WD4)
        wd_sc = shared("picked_sc", [P, R_BLOCKS, N // 4], I32, "wd_sc")
        wgo_sb = early_tile([P, J], F32, "wgo_sb", EARLY_WGO)
        b_sb = early_tile([P, N_TILES], F32, "b_sb", EARLY_B)

        def load_residual(t):
            nc.sync.dma_start(r_sb[t][:], rT[t * P : (t + 1) * P, :])

        def load_wd_scales(rb, scales):
            for q in range(QUADS):
                nc.sync.dma_start(wd_sc[quad_rows(q), rb, :], scales[0].bitcast(I32)[PACK * q : PACK * (q + 1), :])

        for t in range(N_TILES - 1):
            load_residual(t)
        load_wd_scales(0, wd8_scales)
        nc.sync.dma_start(wd8_w[:], wd8_words[0].rearrange("p n i -> p (n i)").bitcast(I32))
        nc.sync.dma_start(wd4_w[:], wd4_words[0].bitcast(I32))
        load_wd_scales(1, wd4_scales)
        with nc.allow_non_contiguous_dma(reason="one bias value to a partition"):
            nc.sync.dma_start(b_sb[:], b.rearrange("(t p) -> p t", p=P))
        load_residual(N_TILES - 1)
        nc.sync.dma_start(wgo_sb[:], wgo)

        parted = [own([P, K_PASSES, CHUNK], U16, f"parted{c}") for c in range(CHUNKS)]
        wu_codes = [own([P, K_PASSES, PASS], U32, f"wu_codes{rb}") for rb in range(R_BLOCKS)]
        wu_planes = []

        def gather_words(lo, hi, picked_w):
            nc.vector.tensor_copy(picked_w[:], tab_w[:].bitcast(U32).indirect(list_slice(lo, hi)))

        def part_words(c, lo, hi, picked_w):
            by_pass = picked_w[:].bitcast(U16).rearrange("p (j a) -> p a j", a=K_PASSES)
            nc.vector.tensor_copy(parted[c][:, :, lo:hi], by_pass)

        def reorder_wu_words(rb, move, outputs):
            move(
                wu_codes[rb][:].rearrange("p a (i m) -> p a m i", i=PACK)[:, :, :, outputs],
                wu_raw[rb][:].bitcast(U32).rearrange("p a (m i) -> p a m i", i=PACK)[:, :, :, outputs],
            )

        def reorder_wu_scales(rb, plane):
            loaded = wu_sc[:].rearrange("p a r -> p (a r)").bitcast(U8)
            loaded = loaded.rearrange("p (a b m i) -> p b a i m", a=K_PASSES, b=R_BLOCKS, i=PACK)
            nc.gpsimd.tensor_copy(plane[:].rearrange("p a (i m) -> p a i m", i=PACK), loaded[:, rb])
            wu_planes.append(plane)

        first_words = [shared(f"words{half}", [P, HALF], U32, f"first_words{half}") for half in range(2)]
        for half, (lo, hi) in enumerate(HALVES):
            gather_words(lo, hi, first_words[half])
        reorder_wu_words(0, nc.scalar.copy, slice(0, PACK // 2))
        reorder_wu_words(0, nc.scalar.copy, slice(PACK // 2, PACK))
        for half, (lo, hi) in enumerate(HALVES):
            part_words(0, lo, hi, first_words[half])
        reorder_wu_scales(0, own([P, K_PASSES, PASS], U8, "wu_plane0"))
        second_words = shared("words0", [P, CHUNK], U32, "second_words")
        gather_words(CHUNK, J, second_words)
        part_words(1, 0, CHUNK, second_words)
        reorder_wu_words(1, nc.vector.tensor_copy, slice(0, PACK))
        reorder_wu_scales(1, shared("words1", [P, K_PASSES, PASS], U8, "wu_plane1"))

        unsigned, signed, h_codes, h_scales, picked_r = {}, {}, {}, {}, {}

        def interleaved(values):
            return values.rearrange("p (g k i) -> p g i k", k=RUN, i=PACK)

        def by_output(values):
            return values.rearrange("p i (g k) -> p g i k", k=RUN)

        def token_columns(lo, hi):
            return slice(lo * PACK, hi * PACK)

        def rectify(c, rb, rooted, lo, hi, banks):
            for i in range(PACK):
                acc = bank_tile(f"acc_a{c}{rb}{i}{lo}", banks[i])
                for a in range(K_PASSES):
                    token = a * J + c * CHUNK
                    nc.tensor.matmul_mx(
                        out=acc[:, lo:hi],
                        lhsT=wu_codes[rb][:, a, i * P : (i + 1) * P].bitcast(FP8X4),
                        lhsT_scale=wu_planes[rb][:, a, i * P : (i + 1) * P],
                        rhs=parted[c][:, a, lo:hi].bitcast(FP4X4),
                        rhs_scale=tab_plane_bytes[:, token + lo : token + hi],
                        start=(a == 0),
                        stop=(a == K_PASSES - 1),
                    )
                col = rb * PACK + i
                nc.scalar.activation(rooted[:, i, :], acc[:, lo:hi], ACT.Relu, scale=root[:, col : col + 1])

        def first_block():
            unsigned[0, 0] = shared("unsigned00", [P, CHUNK * PACK], BF16, "unsigned00")
            rooted = shared("first_rooted", [P, PACK, HALF], F32, "first_rooted")
            rectify(0, 0, rooted, 0, HALF, LOW_BANKS)
            values = interleaved(unsigned[0, 0][:, token_columns(0, HALF)])
            nc.gpsimd.tensor_tensor(values, by_output(rooted[:]), by_output(rooted[:]), ALU.mult)
            rooted = own([P, PACK, HALF], F32, "second_rooted")
            rectify(0, 0, rooted, HALF, CHUNK, HIGH_BANKS)
            values = interleaved(unsigned[0, 0][:, token_columns(HALF, CHUNK)])
            nc.scalar.activation(values, by_output(rooted[:]), ACT.Square)

        def hidden_unsigned(c, rb, into, banks):
            unsigned[c, rb] = into
            rooted = ring.tile([P, PACK, CHUNK], F32, name="rooted")
            rectify(c, rb, rooted, 0, CHUNK, banks)
            for lo, hi in HALVES:
                values = interleaved(into[:, token_columns(lo, hi)])
                nc.scalar.activation(values, by_output(rooted[:, :, lo:hi]), ACT.Square)

        def hidden_signed(c, rb, banks):
            rooted = ring.tile([P, PACK, CHUNK], F32, name="rooted")
            rectify(c, rb, rooted, 0, CHUNK, banks)
            squares = keep.tile([P, PACK, CHUNK], F32, name="squares")
            rounded = shared("rounded", [P, 3 * CHUNK_BYTES // 2], BF16, "rounded")[:, 0 : PACK * CHUNK]
            rounded = rounded.rearrange("p (i j) -> p i j", i=PACK)
            into = own([P, CHUNK * PACK], BF16, f"signed{c}{rb}")
            nc.scalar.activation(squares[:], rooted[:], ACT.Square)
            for i in range(PACK):
                col = rb * PACK + i
                nc.scalar.activation(rounded[:, i, :], squares[:, i, :], ACT.Copy, scale=sign[:, col : col + 1])
            for lo, hi in HALVES:
                signed[c, rb, lo] = into[:, token_columns(lo, hi)]
                nc.scalar.copy(interleaved(signed[c, rb, lo]), by_output(rounded[:, :, lo:hi]))

        def apply_sign(c, rb, lo, hi, into):
            signed[c, rb, lo] = into
            width = SIGN_TOKENS * PACK
            nc.vector.tensor_tensor(
                into.rearrange("p (g x) -> p g x", x=width),
                unsigned[c, rb][:, token_columns(lo, hi)].rearrange("p (g x) -> p g x", x=width),
                sign_wide[:, rb, :].unsqueeze(1).to_broadcast([P, (hi - lo) // SIGN_TOKENS, width]),
                ALU.mult,
            )

        def quantise(c, rb, lo, hi):
            nc.vector.quantize_mx(
                out=h_codes[c, rb][:, lo:hi].bitcast(FP8X4),
                scales=h_scales[c, rb][:, lo:hi],
                in_=signed[c, rb, lo],
            )

        def gather_residual(t, lo, hi, into):
            nc.vector.tensor_copy(into, r_sb[t][:].indirect(list_slice(lo, hi)))
            for c in range(lo // CHUNK, hi // CHUNK):
                picked_r[c, t] = into[:, c * CHUNK - lo : (c + 1) * CHUNK - lo]

        picked_pair = keep.tile([P, PAIR, J], F32, name="picked_pair")
        for t in range(PAIR):
            gather_residual(t, 0, J, picked_pair[:, t, :])
        second_residual = EARLY_RESIDUAL + ROW_BYTES
        first_block()
        hidden_unsigned(0, 1, own([P, CHUNK * PACK], BF16, "unsigned01"), LOW_BANKS)
        for rb in range(R_BLOCKS):
            h_codes[0, rb] = shared(f"codes0{rb}", [P, CHUNK], U32, f"h_codes0{rb}")
            h_scales[0, rb] = own([P, CHUNK], U8, f"h_scales0{rb}")
        windows.append(shared("first_rooted", [P, T], F32, "window3"))
        nc.gpsimd.memset(windows[3][:], 0.0)
        apply_sign(0, 0, 0, CHUNK, early_tile([P, CHUNK * PACK], BF16, "signed00", second_residual)[:])
        quantise(0, 0, 0, CHUNK)
        gather_residual(2, 0, CHUNK, shared("unsigned00", [P, CHUNK], F32, "picked_r20")[:])
        signed01 = early_tile([P, ROW_BYTES // 2], BF16, "signed01", second_residual)
        for lo, hi in HALVES:
            apply_sign(0, 1, lo, hi, signed01[:, token_columns(lo, hi)])
        for lo, hi in HALVES:
            quantise(0, 1, lo, hi)
        gather_residual(2, CHUNK, J, early_tile([P, CHUNK], F32, "picked_r21", second_residual + J * 4)[:])
        gather_residual(3, 0, J, early_tile([P, J], F32, "picked_r3", second_residual)[:])

        wd_planes = wd_sc[:].rearrange("p b n -> p (b n)").bitcast(U8)
        wd_codes = (
            lambda t: wd8_w[:, t * P : (t + 1) * P].bitcast(FP8X4),
            lambda t: wd4_w[:, t * P // 2 : (t + 1) * P // 2].bitcast(FP4X4),
        )

        def second_layer(c, t, lo, hi, bank, into):
            acc = bank_tile(f"acc_y{c}{t}{lo}", bank)
            order = (1, 0) if c == 1 and hi == CHUNK else (0, 1)
            for rb in order:
                nc.tensor.matmul_mx(
                    out=acc[:, lo:hi],
                    lhsT=wd_codes[rb](t),
                    lhsT_scale=wd_planes[:, rb * N + t * P : rb * N + (t + 1) * P],
                    rhs=h_codes[c, rb][:, lo:hi].bitcast(FP8X4),
                    rhs_scale=h_scales[c, rb][:, lo:hi],
                    start=(rb == order[0]),
                    stop=(rb == order[1]),
                )
            nc.scalar.activation(into, acc[:, lo:hi], ACT.Identity, bias=b_sb[:, t : t + 1])

        def weigh(name, total, residual, weights):
            with_residual = shared("sum", total.shape, F32, name)
            nc.gpsimd.tensor_tensor(with_residual[:], total[:], residual, ALU.add)
            nc.gpsimd.tensor_tensor(total[:], with_residual[:], weights, ALU.mult)

        def finish_pair(c, lo, hi, total, banks):
            for t in range(PAIR):
                second_layer(c, t, lo, hi, banks[t], total[:, t, :])
            tokens = slice(c * CHUNK + lo, c * CHUNK + hi)
            weights = wgo_sb[:, tokens].unsqueeze(1).to_broadcast([P, PAIR, hi - lo])
            weigh(f"pair_sum{c}{lo}", total, picked_pair[:, :, tokens], weights)

        def finish(c, t, total, bank):
            second_layer(c, t, 0, CHUNK, bank, total[:])
            weigh(f"sum{c}{t}", total, picked_r[c, t], wgo_sb[:, c * CHUNK : (c + 1) * CHUNK])

        def scatter(c, t, lo, hi, values):
            window = windows[t][:].indirect(list_slice(c * CHUNK + lo, c * CHUNK + hi))
            nc.vector.tensor_copy(window, values)

        def store(t):
            nc.sync.dma_start(out[t * P : (t + 1) * P, :], windows[t][:])

        pairs = [keep.tile([P, PAIR, HALF], F32, name=f"first_pair{half}") for half in range(2)]
        total02 = shared("total02", [P, CHUNK], F32, "total02")
        total03 = keep.tile([P, CHUNK], F32, name="total03")
        finish_pair(0, 0, HALF, pairs[0], (4, 5))
        finish_pair(0, HALF, CHUNK, pairs[1], (3, 6))
        finish(0, 2, total02, 7)
        finish(0, 3, total03, 2)
        hidden_unsigned(1, 0, shared("codes01", [P, CHUNK * PACK], BF16, "unsigned10"), (0, 1, 4, 5))
        hidden_signed(1, 1, (3, 6, 7, 2))
        for half, (lo, hi) in enumerate(HALVES):
            for t in range(PAIR):
                scatter(0, t, lo, hi, pairs[half][:, t, :])
        scatter(0, 2, 0, CHUNK, total02[:])

        for rb in range(R_BLOCKS):
            h_codes[1, rb] = own([P, CHUNK], U32, f"h_codes1{rb}")
        h_scales[1, 0] = own([P, CHUNK], U8, "h_scales10")
        h_scales[1, 1] = shared("total02", [P, CHUNK], U8, "h_scales11")
        apply_sign(1, 0, 0, HALF, shared("total02", [P, HALF * PACK], BF16, "signed10a", offset=CHUNK)[:])
        quantise(1, 0, 0, HALF)
        quantise(1, 1, 0, HALF)
        late_signed = shared("rounded", [P, HALF * PACK], BF16, "signed10b", offset=2 * CHUNK_BYTES)
        apply_sign(1, 0, HALF, CHUNK, late_signed[:])
        quantise(1, 1, HALF, CHUNK)
        quantise(1, 0, HALF, CHUNK)
        held = shared("rounded", [P, CHUNK], F32, "held")
        nc.scalar.copy(held[:], total03[:])
        scatter(0, 3, 0, CHUNK, held[:])

        pairs = [
            shared("rounded", [P, PAIR, HALF], F32, "second_pair0", offset=CHUNK_BYTES),
            keep.tile([P, PAIR, HALF], F32, name="second_pair1"),
        ]
        totals = {t: keep.tile([P, CHUNK], F32, name=f"total1{t}") for t in range(PAIR, N_TILES)}
        for half, (lo, hi) in enumerate(HALVES):
            finish_pair(1, lo, hi, pairs[half], LOW_BANKS[PAIR * half : PAIR * (half + 1)])
        for t in range(PAIR, N_TILES):
            finish(1, t, totals[t], HIGH_BANKS[t])
        for t in range(PAIR):
            scatter(1, t, 0, HALF, pairs[0][:, t, :])
        for t in range(PAIR):
            scatter(1, t, HALF, CHUNK, pairs[1][:, t, :])
            store(t)
        for t in range(PAIR, N_TILES):
            scatter(1, t, 0, CHUNK, totals[t][:])
            store(t)
